import numpy as np, ml_dtypes
CORES = [3,7,11,15,131,135,139,143]
N = 8
BF = ml_dtypes.bfloat16
def gentries(a):
    return np.ascontiguousarray(a.reshape(8, 16, -1).transpose(0, 2, 1)).reshape(8, -1)
def gtable(e):
    e = np.asarray(e); return np.ascontiguousarray(e.reshape(8, -1, 16).transpose(0, 2, 1)).reshape(128, -1).astype(np.int32)
V, W, U, ND, G, K, B, H = 704, 1024, 4, 5, 64, 3, 2, 1
KV, Q, TOPS, TH, FA, FB = K * V, 8, 2 ** 20 - 1, 7340025, 0.375, 0.625
def pick(t, c):
    return np.take_along_axis(t, c[:, None, :], 2)
def lend(t, sl):
    res = []
    for r in range(N):
        w = [t[r]]
        for e in range(ND):
            q = (r + e + 1) % N; w.append(pick(t[q], sl[q, :, e]))
        res.append(np.concatenate(w, axis=2))
    return np.stack(res)
def home(a, sl, both):
    res = []
    for q in range(N):
        o = a[q][:, :, :V]
        for e in range(ND):
            r = (q - e - 1) % N; b = np.zeros((8, 16, V), a.dtype)
            np.put_along_axis(b, sl[q, :, e][:, None, :], a[r][:, :, V + e * G:V + (e + 1) * G], 2)
            o = both(o, b)
        res.append(o)
    return np.stack(res)
def drop(z, x, both):
    b = np.zeros((8, 16, U * W), x.dtype)
    np.put_along_axis(b, z[:, None, :], x, 2)
    return both.reduce(b.reshape(8, 16, U, W), axis=2)
def coarse(cl, cr, snd, cu):
    c = cu & (W - 1); rule = np.repeat(cr, V, axis=4)
    t = lend(cl, snd[:, :, 0])
    s1 = np.stack([pick(t[r], c[r, :, 0, 0]) + pick(t[r], c[r, :, 0, 1]) + rule[r, :, :, 0] for r in range(N)])
    t = lend(np.maximum.reduce(s1.reshape(N, 8, 16, K, V), axis=3), snd[:, :, 1])
    s2, a = [], []
    for r in range(N):
        x, y = pick(t[r], c[r, :, 1, 0]), pick(t[r], c[r, :, 1, 1]); w = rule[r, :, :, 1]
        s2.append(x + y + w)
        a.append(np.maximum(drop(cu[r, :, 1, 0], y + w, np.maximum), drop(cu[r, :, 1, 1], x + w, np.maximum)))
    o = home(np.stack(a), snd[:, :, 1], np.maximum)
    return s1 + np.tile(o, (1, 1, 1, K)), np.stack(s2)
def parts(rng):
    d = {}
    d["cl"] = rng.integers(0, 2 ** 19, (N, 8, 1, V)) + rng.integers(0, 2 ** 19, (N, 8, 16, V))
    d["cr"] = rng.integers(0, 2 ** 19, (N, 8, 16, 2, K))
    d["cu"] = np.ascontiguousarray(np.argsort(rng.random((N, 8, 2, 2, U * W)), axis=-1)[..., :KV])
    d["fu"] = np.ascontiguousarray(np.argsort(rng.random((N, 8, 2, H, 2, U * W)), axis=-1)[..., :KV])
    d["snd"] = np.ascontiguousarray(np.argsort(rng.random((N, 8, 2, ND, V)), axis=-1)[..., :G])
    d["fl"] = 0.8 + 0.4 * rng.random((N, 8, 16, V))
    d["fw"] = FA + (FB - FA) * rng.random((N, 8, 16, 2, B * H))
    d["top"] = 0.5 + 1.5 * rng.random((N, 8, 16, V))
    return d
def bound(rng, p, lo, hi):
    s = np.sort(p[..., ::16], axis=-1); x = lo + (hi - lo) * rng.random((N, 8, 1, 1)) + 0.04 * rng.random((N, 8, 16, 1))
    return np.take_along_axis(s, (x * s.shape[-1]).astype(np.int64), 3)[..., 0]
def finish(rng, d, lo, hi):
    p = coarse(d["cl"], d["cr"], d["snd"], d["cu"])
    d["th"] = np.stack([bound(rng, p[0], lo, hi), bound(rng, p[1], lo, hi)], axis=-1)
    return d
def pack(d):
    e = {}
    for k in ("cl", "cr", "th"): e[k] = np.ascontiguousarray(d[k].reshape(N, 128, -1)).astype(np.int32)
    for k in ("cu", "fu", "snd"): e[k] = np.stack([gtable(a.reshape(8, -1)) for a in d[k]])
    e["fl"] = d["fl"].reshape(N, 128, V).astype(np.float32).astype(BF)
    e["fw"] = np.clip(d["fw"].reshape(N, 128, 2 * B * H), FA, FB).astype(np.float32)
    e["top"] = d["top"].reshape(N, 128, V).astype(np.float32).astype(BF)
    return e
def setup_inputs(rng):
    return pack(finish(rng, parts(rng), 0.4, 0.56))
def setup_inputs_brink(rng):
    d = parts(rng)
    d["cl"] = rng.integers(2 ** 19, 2 ** 20 - 8, (1, 8, 16, 1)) + rng.integers(0, 4, (N, 8, 16, V))
    d["cr"] = rng.integers(2 ** 19, 2 ** 20 - 8, (1, 8, 16, 1, 1)) + rng.integers(0, 2, (N, 8, 16, 2, K))
    return pack(finish(rng, d, 0.45, 0.56))
def crowd(rng, n):
    x = np.array([0, W - 1, V - 1, V]); o = np.concatenate([x, rng.permutation(np.setdiff1d(np.arange(W), x))])
    z = (o[:, None] + W * np.arange(U)[None, :]).reshape(-1)[:KV + KV // 8]
    return np.stack([rng.permutation(z)[:KV] for i in range(n)])
def setup_inputs_calm(rng):
    d = parts(rng); o = rng.permutation(8); full = o[0]; unit = 2.0 ** -10
    d["snd"] = np.ascontiguousarray(np.argsort(rng.random((N, 8, 2, V)), axis=-1)[..., :ND * G].reshape(N, 8, 2, ND, G))
    d["top"] = unit * (8 + 4 * rng.random((N, 8, 16, V)))
    d["top"][:, full] = unit * np.maximum(1.0, 0.75 + 0.5 * rng.random((N, 16, V)))
    kinds = ((0.25, 0.25, 0, 1), (0.25, 0.25, 1, 1), (0.05, 0.25, 1, 2), (0.02, 0.1, 1, 1))
    for i, (a, b, t1, t2) in enumerate(kinds):
        g = o[i + 1]
        d["cl"][:, g] = rng.random((N, 16, V)) < a
        d["cr"][:, g] = rng.random((N, 16, 2, K)) < b
        if i < 2:
            d["top"][:, g] = 0.5 * d["top"][:, g]
            for q in range(N):
                z = crowd(rng, 1)[0]; d["cu"][q, g, 1, 0] = z; d["cu"][q, g, 1, 1] = rng.permutation(z)
    d["snd"][:, full, :, :, 1:G - 1] = 1 + np.argsort(rng.random((N, 2, ND, V - 2)), axis=-1)[..., :G - 2]
    d["snd"][:, full, :, :, 0] = V - 1; d["snd"][:, full, :, :, G - 1] = 0
    e = V + G * np.arange(ND); most = np.concatenate([np.array([V - 1, 0]), e, e + G - 1])
    must = (most[:, None] + W * np.arange(U)[None, :]).reshape(-1); lack = W * (U - 1); rest = np.setdiff1d(np.arange(U * W), must)
    for q in range(N):
        for m in range(2):
            for h in range(H):
                for s in range(2):
                    first, last = must, must[:0]
                    if h == H - 1 and s == 1: first, last = must[must != lack], must[must == lack]
                    z = rng.permutation(rest); n = B * V - len(first); k = KV - B * V - len(last)
                    d["fu"][q, full, m, h, s] = np.concatenate([rng.permutation(np.concatenate([first, z[:n]])), rng.permutation(np.concatenate([last, z[n:n + k]]))])
    d = finish(rng, d, 0.4, 0.56); d["th"][:, full] = 0
    for i, (a, b, t1, t2) in enumerate(kinds):
        g = o[i + 1]
        for q in range(N):
            for m, t in enumerate((t1, t2)):
                d["th"][q, g, :, m] = t + 1; d["th"][q, g, rng.permutation(16)[:7], m] = t
    return pack(d)
def unused_felt(d, q, g):
    def uses(r):
        u = np.zeros(W, bool); u[d["cu"][r, g, 1] & (W - 1)] = True
        return u
    used = uses(q)[:V]
    for e in range(ND):
        s = d["snd"][q, g, 1, e]; used[s] = used[s] | uses((q - e - 1) % N)[V + e * G:V + (e + 1) * G]
    named = np.zeros(W, bool); named[d["fu"][q, g, 1][:, :, :B * V] & (W - 1)] = True
    return bool(np.any(named[:V] & ~used))
def setup_inputs_corners(rng):
    d = parts(rng); o = rng.permutation(8); few, full, rest = o[:2], o[2:4], o[4:]; lone = o[4]
    rest = rest[1:]
    d["snd"] = np.ascontiguousarray(np.argsort(rng.random((N, 8, 2, V)), axis=-1)[..., :ND * G].reshape(N, 8, 2, ND, G))
    d["top"] = 0.75 + 0.5 * rng.random((N, 8, 16, V)); d["top"][:, full] = d["top"][:, full] * 0.375
    for q in range(N):
        for g in few:
            d["cl"][q, g] = rng.integers(0, 1024, (16, V))
            for m in range(2):
                a = np.zeros(K, bool); i = int(rng.integers(0, 4))
                if i == 0: a[0] = True
                elif i == 1: a[K - 1] = True
                elif i == 2: a[:] = True
                else: a[1:] = True
                d["cr"][q, g, :, m] = np.where(a, TOPS, 0)
        for g in full:
            d["cu"][q, g] = crowd(rng, 4).reshape(2, 2, KV); d["fu"][q, g] = crowd(rng, 4 * H).reshape(2, H, 2, KV)
        g = full[0]; d["cu"][q, g, :, 1] = d["cu"][q, g, :, 0]; d["fu"][q, g, :, :, 1] = d["fu"][q, g, :, :, 0]
        d["cu"][q, lone, 1] = crowd(rng, 2)
    d = finish(rng, d, 0.4, 0.56); d["th"][:, few] = 5 * 2 ** 19
    for q in range(N):
        many, dead = 15 + q % 2, (Q - 1) * (1 - (q // 2) % 2)
        cases = ((many, many), (Q, Q), (Q, dead) if q % 2 == 0 else (dead, 16))
        for i, g in enumerate([lone] + list(rng.permutation(rest)[:2])):
            for m, n in enumerate(cases[i]):
                d["th"][q, g, :, m] = TH; d["th"][q, g, rng.permutation(16)[:n], m] = 0
    assert any(unused_felt(d, q, lone) for q in range(N))
    return pack(d)
def setup_inputs_ends(rng):
    d = parts(rng)
    col = rng.random((N, 8, 1, V)) < 0.85; flip = rng.random((N, 8, 16, V)) < 0.05
    d["cl"] = np.where(col ^ flip, TOPS, 0); d["cl"][..., V - 1] = TOPS; d["cl"][..., V - 2] = 0
    d["cr"] = np.where(rng.random((N, 8, 16, 2, K)) < 0.6, TOPS, 0); d["cr"][:, :, 15, :, K - 1] = TOPS
    th = np.full((N, 8, 16, 2), TH, np.int64)
    for g in range(8):
        i = rng.permutation(15); d["cl"][:, g, i[0]] = 0; d["cr"][:, g, i[0]] = 0
        for q in range(N):
            for m in range(2):
                n = 7 if g == 7 or q == N - 1 else int(rng.choice(np.array([6, 7, 7, 8])))
                th[q, g, i[:n], m] = 0
    d["th"] = th
    d["cr"][N - 1, 7, :, 1, 0] = np.minimum(d["cr"][N - 1, 7, :, 1, 0], TOPS - 1); d["cr"][N - 1, 7, 15, 1, 0] = TOPS - 1
    e = np.concatenate([np.arange(G // 2), np.arange(V - G // 2, V)]); d["snd"] = e[np.argsort(rng.random((N, 8, 2, ND, G)), axis=-1)]
    e = np.concatenate([np.arange(KV // 2), np.arange(U * W - KV // 2, U * W)])
    d["cu"] = e[np.argsort(rng.random((N, 8, 2, 2, KV)), axis=-1)]; d["fu"] = e[np.argsort(rng.random((N, 8, 2, H, 2, KV)), axis=-1)]
    d["fl"] = np.where(rng.random((N, 8, 16, V)) < 0.5, 0.75, 1.25)
    d["fw"] = np.where(rng.random((N, 8, 16, 2, B * H)) < 0.5, FA, FB)
    d["top"] = np.where(rng.random((N, 8, 16, V)) < 0.9, 32.0, 2.0 ** -10)
    return pack(d)
def setup_inputs_spread(rng):
    d = parts(rng)
    d["cl"] = np.minimum((np.exp2(20 * rng.random((N, 8, 1, V))) * (0.25 + 0.75 * rng.random((N, 8, 16, V)))).astype(np.int64), TOPS)
    d["cr"] = np.minimum(np.exp2(20 * rng.random((N, 8, 16, 2, K))).astype(np.int64), TOPS)
    d["fl"] = np.clip(0.75 + 0.5 * rng.random((N, 8, 1, V)) + 0.1 * (rng.random((N, 8, 16, V)) - 0.5), 0.75, 1.25)
    d["top"] = np.exp2(2 * rng.random((N, 8, 1, V)) - 1) * (0.75 + 0.5 * rng.random((N, 8, 16, V)))
    return pack(finish(rng, d, 0.4, 0.56))
def unlist(a, shape):
    return np.stack([gentries(x) for x in a]).astype(np.int64).reshape((N, 8) + shape)
def check_ranges(d):
    bad = []
    for k, lo, hi in (("cl", 0, TOPS), ("cr", 0, TOPS), ("th", 0, TH), ("cu", 0, U * W - 1), ("fu", 0, U * W - 1), ("snd", 0, V - 1)):
        if np.min(d[k]) < lo or np.max(d[k]) > hi: bad.append("range of " + k)
    for k, lo, hi in (("fl", 0.75, 1.25), ("fw", FA, FB), ("top", 2.0 ** -10, 32.0)):
        x = np.asarray(d[k]).astype(np.float64)
        if not np.all((x >= lo) & (x <= hi)): bad.append("range of " + k)
    for k, n in (("cu", KV), ("fu", KV), ("snd", G)):
        s = np.sort(unlist(d[k], (-1, n)), axis=-1)
        if np.any(s[..., 1:] == s[..., :-1]): bad.append("repeated numbers in a block of " + k)
    return bad
def reference(cl, cr, th, cu, fu, snd, fl, fw, top):
    sl = unlist(snd, (2, ND, G)); cz = unlist(cu, (2, 2, KV)); fz = unlist(fu, (2, H, 2, KV)); fc = fz & (W - 1)
    p = coarse(cl.astype(np.int64).reshape(N, 8, 16, V), cr.astype(np.int64).reshape(N, 8, 16, 2, K), sl, cz)
    t = th.astype(np.int64).reshape(N, 8, 16, 2)
    counted, place = [], []
    for m in range(2):
        votes = np.add.reduce((p[m] >= t[:, :, :, m:m + 1]).astype(np.int64), axis=2)
        live = (votes >= Q).astype(np.int64).reshape(N, 8, K, V)
        before = np.add.accumulate(live, axis=2) - live
        counted.append(((live == 1) & (before < B)).reshape(N, 8, KV)); place.append(np.minimum(before, B - 1).reshape(N, 8, KV))
    wts = fw.astype(np.float64).reshape(N, 8, 16, 2, B * H)
    def weight(r, m, h):
        return pick(wts[r, :, :, m], place[m][r] * H + h) * counted[m][r][:, None, :]
    x = fl.astype(np.float64).reshape(N, 8, 16, V); known = []
    for m in range(2):
        known.append(lend(x, sl[:, :, m])); res = []
        for r in range(N):
            y = np.zeros((8, 16, V))
            for h in range(H):
                e = pick(known[m][r], fc[r, :, m, h, 0]) * pick(known[m][r], fc[r, :, m, h, 1]) * weight(r, m, h)
                y = y + np.add.reduce(e.reshape(8, 16, K, V), axis=2)
            res.append(y)
        x = np.stack(res)
    o = top.astype(np.float64).reshape(N, 8, 16, V)
    for m in (1, 0):
        res = []
        for r in range(N):
            a = np.zeros((8, 16, W))
            for h in range(H):
                e = np.tile(o[r], (1, 1, K)) * weight(r, m, h)
                a = a + drop(fz[r, :, m, h, 0], e * pick(known[m][r], fc[r, :, m, h, 1]), np.add) + drop(fz[r, :, m, h, 1], e * pick(known[m][r], fc[r, :, m, h, 0]), np.add)
            res.append(a)
        o = home(np.stack(res), sl[:, :, m], np.add)
    return {"yi": x.reshape(N, 128, V).astype(np.float32), "yo": o.reshape(N, 128, V).astype(np.float32)}

def check_inputs(d):
    bad = list(check_ranges(d))
    if not bad:
        for name, y in reference(**d).items():
            for q in range(N):
                v = np.abs(np.asarray(y[q], np.float64)); s = np.sqrt(np.mean(v * v))
                if v.max() > 15 * s or s < 2.0 ** -10: bad.append('%s of rank %d is uneven or too small' % (name, q))
    return bad

@@ -1,0 +1,476 @@
+from concourse.bass import DstId, RemoteDMATransfer
+from concourse.mybir import AluOpType, ActivationFunctionType
+
+N, V, W, U, ND, G, K = 8, 704, 1024, 4, 5, 64, 3
+KV, GH, C = K * V, ND * G, V // 16
+BIG = float(2 ** 40)
+OFF = 32
+DEAD = float(2 ** 15 + 2 ** 12)
+PE_G, PE_O = 3, 3
+ACT1, ACT2, DVE1 = 3, 2, 2
+EARLY = 2
+YI5 = 1
+SPLIT_F, SPLIT_B = [4, 1], [2, 2, 1]
+
+F, I, H, B16 = "float32", "int32", "uint16", "bfloat16"
+
+
+def _sb(n, dt=F):
+    return ("sbuf", [128] + (n if isinstance(n, list) else [n]), dt)
+
+
+SCRATCH = {
+    "cl_i": _sb(V, I), "snd_i": _sb(40, I), "cu_i": _sb(528, I), "fu_i": _sb([4, 132], I), "cr_i": _sb(8, I), "th_i": _sb(4, I),
+    "fw_f": _sb(4), "top_b": _sb(V, B16), "t0b": _sb(W, B16), "kc": _sb(32),
+    "sndu": _sb(40, H), "cuu": _sb(528, H), "zpu": _sb(264, H), "fcu": _sb([2, 132], H), "invu": _sb(512, H), "idxu": _sb(88, H),
+    "ti": _sb(264, I), "tj": _sb(264, I), "tk": _sb(264, I), "tf": _sb(264), "tg": _sb(264), "t3": _sb([2, 132], I), "base": _sb([4, 132]),
+    "w0": _sb(U * W), "w1": _sb(U * W), "w2": _sb(U * W), "w3": _sb(U * W), "fill": _sb(256), "invf": _sb(512),
+    "nt0": _sb(W), "bb": _sb(KV), "nr": _sb(KV), "nm": _sb(V), "t1c": _sb(W), "xl": _sb(KV + 8), "xr": _sb(KV + 8), "pp": _sb(KV + 8),
+    "ga": _sb(GH), "gb": _sb(GH), "oa": _sb(V), "ob": _sb(V), "oc": _sb(V), "o1": _sb(V), "o0": _sb(V), "ht": _sb(GH), "a0": _sb(V),
+    "sb1": _sb(GH), "sbf": _sb(GH, B16), "sb2": _sb(GH), "sb3": _sb(GH), "sb4": _sb(GH), "sb5": _sb(GH), "sb6": _sb(GH),
+    "rb3": _sb(GH), "rb5": _sb(GH), "rb6": _sb(GH),
+    "vt1": _sb(KV, B16), "vt2": _sb(KV, B16), "sel": _sb(144, B16), "ones": _sb(128), "ident": _sb(128), "idents": _sb(128),
+    "dg0": _sb(128), "dg1": _sb(128), "s8a": _sb(8), "s8b": _sb(8), "pi": _sb(4, I), "pj": _sb(4, I), "vali": _sb(132), "val": _sb(132),
+    "uu": _sb(132), "mn": _sb(C), "mx": _sb(C), "tt": _sb(C), "idxf": _sb(88),
+    "key": _sb([2, 132]), "kmn": _sb([2, C]), "kmx": _sb([2, C]), "kt": _sb([2, C]), "ksel": _sb([2, 88], I), "ks": _sb([2, 88], I), "kg": _sb([2, 88], I),
+    "su1": _sb([2, 88], H), "gu1": _sb([2, 88], H), "su2": _sb([2, 88], H), "gu2": _sb([2, 88], H),
+    "t1": _sb(W + 8), "t0w0": _sb(W + 8), "t0w1": _sb(W + 8), "tw": _sb(2 * V), "yib": _sb(V),
+    "p0": ("psum", [128, 1024], F), "p1": ("psum", [128, 1024], F), "p2": ("psum", [128, 1024], F), "pa": ("psum", [128, 512], F), "pb": ("psum", [128, 512], F),
+}
+FWD, BACK = ["e1", "ef", "e2", "e4"], ["e3", "e5", "e6"]
+SEMAPHORES = (["cv", "ca", "cp", "cg"] + ["d%d" % i for i in range(32)] + ["s" + e for e in FWD + BACK] + FWD
+              + ["%s_%d" % (e, d) for e in BACK for d in range(1, ND + 1)])
+
+
+def calls_of(topo, cores, r, sign):
+    src = cores[r]; here = topo.cores_of(src)
+    off = [d for d in range(1, ND + 1) if cores[(r + sign * d) % N] not in here]
+    on = [d for d in range(1, ND + 1) if d not in off]
+    out = topo.engines(src, cores[(r + sign * off[0]) % N])
+    calls = []
+    for m in (SPLIT_F if sign < 0 else SPLIT_B):
+        part, off = off[:m], off[m:]
+        if part:
+            n = len(out) // len(part)
+            calls.append([(d, out[i * n:(i + 1) * n]) for i, d in enumerate(part)])
+    for d in on:
+        calls[0].append((d, [e for e in topo.engines(src, cores[(r + sign * d) % N]) if e not in out]))
+    return calls
+
+
+def rank_program(g, core, T, topo):
+    rank = T.rank_of(core)
+    if rank is None:
+        return
+    A, AF = AluOpType, ActivationFunctionType
+    cores = list(T.cores)
+    Q = {"v": g.vector, "a": g.scalar, "p": g.tensor, "g": g, "s": g.sync}
+    cnt, clock = {}, {q: {} for q in Q}
+    writer, readers, holder, nd = {}, {}, {}, [0]
+
+    def need(q, ev):
+        s, n, ck = ev[1], ev[2], ev[3]
+        if clock[q].get(s, 0) >= n:
+            return
+        Q[q].wait_ge(T.sem[s], n)
+        clock[q][s] = n
+        for k2, v2 in ck.items():
+            if clock[q].get(k2, 0) < v2:
+                clock[q][k2] = v2
+
+    def banks(x):
+        return [b for t in x for b in (["p1a", "p1b"] if t == "p1" else [t])]
+
+    def order(q, r, w, x, dma):
+        evs = []
+        for t in r:
+            evs += writer[t]
+        for t in w:
+            evs += [ev for ev in writer.get(t, []) + readers.get(t, [])]
+        evs += [holder[t] for t in banks(x) if t in holder and holder[t][0] != q]
+        for ev in sorted(evs, key=lambda ev: -ev[2]):
+            need(q, ev)
+
+    def note(ev, r, w, x):
+        for t in r:
+            readers.setdefault(t, []).append(ev)
+        for t in w:
+            writer[t] = [ev]; readers[t] = []
+        for t in banks(x):
+            holder[t] = ev
+
+    def op(q, fn, r=(), w=(), x=()):
+        order(q, r, w, x, False)
+        s = "c" + q
+        cnt[s] = cnt.get(s, 0) + 1
+        fn().then_inc(T.sem[s], 1)
+        note((q, s, cnt[s], dict(clock[q])), r, w, x)
+
+    def dma(q, out, in_, r=(), w=()):
+        order(q, r, w, (), True)
+        s = "d%d" % nd[0]; nd[0] += 1
+        cnt[s] = 16
+        Q[q].dma_start(out, in_).then_inc(T.sem[s], 16)
+        note(("dma", s, 16, dict(clock[q])), r, w, ())
+
+    def exchange(e, src, dst, at, r):
+        sign = -1 if e in FWD else 1
+        order("g", r, (), (), True)
+        total = 0
+        for call in calls_of(topo, cores, rank, sign):
+            trs = []
+            for d, eng in call:
+                rid, pid = topo.addr(cores[(rank + sign * d) % N], core)
+                trs.append(RemoteDMATransfer(dst_ids=[DstId(rid=rid, pnc=pid)], dma_engine_mask=sum(1 << k for k in eng),
+                                             remote_sem=T.sem[e if e in FWD else "%s_%d" % (e, d)],
+                                             src=src[:, (d - 1) * G:d * G], dst=dst[:, at + (d - 1) * G:at + d * G]))
+                total += len(eng)
+            g.remote_dma_fused(trs, local_sem=T.sem["s" + e])
+        cnt["s" + e] = total
+        note(("dma", "s" + e, total, dict(clock["g"])), r, ["sent" + e], ())
+        late = {}
+        for d in range(1, ND + 1):
+            for j, call in enumerate(calls_of(topo, cores, (rank - sign * d) % N, sign)):
+                for d2, eng in call:
+                    if d2 == d:
+                        s = e if e in FWD else "%s_%d" % (e, d)
+                        cnt[s] = cnt.get(s, 0) + len(eng)
+                        late[d] = (j, cores[(rank - sign * d) % N] not in topo.cores_of(core), d)
+        for s in ([e] if e in FWD else ["%s_%d" % (e, d) for d in range(1, ND + 1)]):
+            writer[s] = [("dma", s, cnt[s], {})]
+        return sorted(late, key=lambda d: late[d])
+
+    v, a, pe = g.vector, g.scalar, g.tensor
+    tt = lambda o, i0, i1, f, r, w, x=(): op("v", lambda: v.tensor_tensor(o, i0, i1, f), r, w, x)
+    ts = lambda o, i0, s1, f, r, w, x=(): op("v", lambda: v.tensor_scalar(o, i0, s1, None, f), r, w, x)
+    ts2 = lambda o, i0, s1, f, s2, f2, r, w, x=(): op("v", lambda: v.tensor_scalar(o, i0, s1, s2, f, f2), r, w, x)
+    cp = lambda o, i0, r, w, x=(): op("v", lambda: v.tensor_copy(o, i0), r, w, x)
+    ms = lambda o, c, w: op("v", lambda: v.memset(o, c), (), w)
+
+    def act(o, i0, r, w, x=(), f=None, **kw):
+        op("a", lambda: a.activation(o, i0, AF.Identity if f is None else f, **kw), r, w, x)
+
+    def mm(items, r, w, x):
+        def fn():
+            for j, (o, l, rr) in enumerate(items):
+                ins = pe.matmul(o, l, rr, j == 0, j == len(items) - 1)
+            return ins
+        op("p", fn, r, w, x)
+
+    kc = lambda j: T.kc[:, j:j + 1]
+    fw = lambda j: T.fw_f[:, j:j + 1]
+    ks = lambda k: slice(k * V, (k + 1) * V)
+    wins = [T.w0, T.w1, T.w2, T.w3]
+    rows8 = slice(0, 128, 18)
+    P2 = ["p2a", "p2b"]
+
+    dma("s", T.cl_i[:], T.cl[:], w=["cl"])
+    dma("a", T.snd_i[:], T.snd[:], w=["snd_i"])
+    dma("a", T.cu_i[:, 264:528], T.cu[:, 264:528], w=["cu2"])
+    op("g", lambda: g.iota(T.pp[:, 0:V], [[1, V]], OFF, 0, allow_small_or_imprecise_dtypes=True), w=["pp0"])
+    ms(T.fill[:], float(KV + OFF), ["fill"])
+    dma("s", T.t0b[:, 0:V], T.fl[:], w=["t0b"])
+    dma("s", T.w0[rows8, :], T.fill[:], r=["fill"], w=["w0"])
+    dma("s", T.w1[rows8, :], T.fill[:], r=["fill"], w=["w1"])
+    dma("s", T.cu_i[:, 0:264], T.cu[:, 0:264], w=["cu1"])
+    dma("s", T.cr_i[:, 0:6], T.cr[:], w=["cr"])
+    dma("s", T.th_i[:, 0:2], T.th[:], w=["th"])
+    dma("s", T.fw_f[:], T.fw[:], w=["fw"])
+    dma("s", T.fu_i[:], T.fu[:], w=["fu"])
+    dma("s", T.top_b[:], T.top[:], w=["top"])
+    for name in ("xl", "xr", "pp"):
+        ms(T[name][:, KV:KV + 8], 0.0, [name + "z"])
+    for name in ("t1", "t0w0", "t0w1"):
+        ms(T[name][:, W:W + 8], 0.0, [name + "z"])
+    ms(T.sel[:], 0.0, ["sel0"])
+    ms(T.w2[:, 0:512], 0.0, ["zero0"])
+    act(T.pp[:, ks(1)], T.pp[:, ks(0)], ["pp0"], ["pp1"], f=AF.Silu, bias=float(V))
+    ts(T.pp[:, ks(2)], T.pp[:, ks(0)], float(2 * V), A.add, ["pp0"], ["pp2"])
+
+    cp(T.sndu[:], T.snd_i[:], ["snd_i"], ["sndu"])
+    ts(T.sb1[:], T.cl_i[:, 0:V].indirect(T.sndu[:, 0:20]), -1.0, A.mult, ["cl", "sndu"], ["sb1"])
+    exchange("e1", T.sb1, T.nt0, V, ["sb1"])
+    act(T.sbf[:], T.t0b[:, 0:V].indirect(T.sndu[:, 0:20]), ["t0b", "sndu"], ["sbf"])
+    ts(T.ti[:], T.cu_i[:, 264:528], 4, A.arith_shift_right, ["cu2"], ["ti"])
+    ts(T.tf[:], T.ti[:], -4095.0 / 256.0, A.mult, ["ti"], ["tf"])
+    tt(T.tg[:], T.cu_i[:, 264:528], T.tf[:], A.add, ["cu2", "tf"], ["tg"])
+    ts(T.zpu[:], T.tg[:], 256.0, A.mult, ["tg"], ["zpu"])
+    ts(T.tj[:], T.cu_i[:, 0:264], W - 1, A.bitwise_and, ["cu1"], ["tj"])
+    exchange("ef", T.sbf, T.t0b, V, ["sbf"])
+    op("g", lambda: g.iota(T.w2[:, 512:2048], [[0, 1536]], 0, 0, allow_small_or_imprecise_dtypes=True), ["zero0"], ["zero"])
+    op("g", lambda: g.iota(T.ones[:], [[0, 128]], 1, 0, allow_small_or_imprecise_dtypes=True), w=["ones"])
+    op("g", lambda: g.iota(T.pi[:, 0:1], [[0, 1]], 0, 1), w=["pi"])
+    op("g", lambda: g.affine_select(T.ident[:], T.ones[:], [[-1, 128]], A.is_equal, 0.0, 0, 1), ["ones"], ["ident"])
+    op("g", lambda: g.affine_select(T.s8a[:], T.ones[:, 0:8], [[-16, 8]], A.is_ge, 0.0, 0, 1), ["ones"], ["s8a"])
+    op("g", lambda: g.iota(T.vali[:], [[16, 132]], 0, 1, allow_small_or_imprecise_dtypes=True), w=["vali"])
+    op("g", lambda: g.affine_select(T.s8b[:], T.s8a[:], [[16, 8]], A.is_ge, 0.0, 15, -1), ["s8a"], ["s8b"])
+
+    todo = {0: list(range(6)), 1: list(range(6))}
+
+    def invert(q, s, n):
+        m = min(n, len(todo[s]))
+        if m:
+            j = todo[s][0]
+            del todo[s][:m]
+            out = wins[s][:].indirect(T.zpu[:, s * 132 + j * 22:s * 132 + (j + m) * 22])
+            src = T.pp[:, j * 352:(j + m) * 352]
+            r, w = ["zpu"] + ["pp%d" % k for k in range(j // 2, (j + m + 1) // 2)], ["w%d" % s]
+            if q == "a":
+                act(out, src, r, w, f=AF.Silu)
+            else:
+                cp(out, src, r, w)
+
+    invert("a", 0, ACT1)
+    ts(T.nt0[:, 0:V], T.cl_i[:], -1.0, A.mult, ["cl"], ["nt0"])
+    cp(T.cuu[:, 0:264], T.tj[:], ["tj"], ["cuu1"])
+    cp(T.kc[:, 0:6], T.cr_i[:, 0:6], ["cr"], ["kcr"])
+    cp(T.kc[:, 6:8], T.th_i[:, 0:2], ["th"], ["kth"])
+    ts(T.t3[:], T.fu_i[:, 0:2, :], W - 1, A.bitwise_and, ["fu"], ["t3"])
+    ts2(T.kc[:, 8:11], T.kc[:, 0:3], -1.0, A.mult, kc(6), A.add, ["kcr", "kth"], ["kb1"])
+    cp(T.fcu[:], T.t3[:], ["t3"], ["fcu"])
+    ts(T.tk[:], T.cu_i[:, 264:528], W - 1, A.bitwise_and, ["cu2"], ["tk"])
+    ts2(T.kc[:, 20:23], T.kc[:, 3:6], kc(7), A.add, -1.0, A.mult, ["kcr", "kth"], ["kb2a"])
+    cp(T.cuu[:, 264:528], T.tk[:], ["tk"], ["cuu2"])
+    invert("v", 1, DVE1)
+    dma("s", T.w2[:, 2048:4096], T.w2[:, 0:2048], ["zero", "sentef"], ["w2b"])
+    dma("s", T.w3[:, 0:2048], T.w2[:, 0:2048], ["zero"], ["w3a"])
+
+    cu = lambda blk, c0, c1: T.cuu[:, blk * 132 + c0:blk * 132 + c1]
+    for c0, c1 in ((0, 12), (12, C), (C, 2 * C), (2 * C, 3 * C)):
+        k, e = c0 // C, slice(16 * c0, 16 * c1)
+        tok = ["bb%d" % k] if c0 != 0 else ["bbx"]
+        act(T.bb[:, e], T.nt0[:].indirect(cu(0, c0, c1)), ["nt0", "e1", "cuu1", "kb1"], tok, bias=kc(8 + k))
+        tt(T.nr[:, e], T.nt0[:].indirect(cu(1, c0, c1)), T.bb[:, e], A.add, ["nt0", "e1", "cuu1"] + tok, ["nr%d" % k] if c0 != 0 else ["nrx"])
+    act(T.p0[:, 0:V], T.nr[:, ks(0)], ["nr0", "nrx"], ["pn0"], ["p0"])
+    tt(T.p1[:, 0:V], T.nr[:, ks(1)], T.p0[:, 0:V], A.min, ["nr1", "pn0"], ["m01"], ["p0", "p1"])
+    invert("a", 1, ACT2)
+    tt(T.nm[:], T.nr[:, ks(2)], T.p1[:, 0:V], A.min, ["nr2", "m01"], ["nm"], ["p1"])
+    ts2(T.sb2[:], T.nm[:].indirect(T.sndu[:, 20:40]), -1.0, A.mult, kc(6), A.add, ["nm", "sndu", "kth"], ["sb2"])
+    exchange("e2", T.sb2, T.t1c, V, ["sb2"])
+
+    def product_left(k):
+        act(T.bb[:, ks(k)], T.t0b[:].indirect(T.fcu[:, 0, k * C:(k + 1) * C]), ["t0b", "ef", "fcu", "fw"], ["bb%d" % k, "bbx"], scale=fw(1))
+
+    def product(k):
+        tt(T.pp[:, ks(k)], T.t0b[:].indirect(T.fcu[:, 1, k * C:(k + 1) * C]), T.bb[:, ks(k)], A.mult, ["t0b", "ef", "fcu", "bb%d" % k], ["pp%d" % k])
+
+    invert("v", 0, 6)
+    invert("a", 1, 6)
+    act(T.t1c[:, 0:V], T.nm[:], ["nm", "kth"], ["t1c"], scale=-1.0, bias=kc(6))
+    dma("s", T.invf[:, 0:256], T.w0[rows8, :], ["w0"], ["invf0"])
+    dma("s", T.invf[:, 256:512], T.w1[rows8, :], ["w1"], ["invf1"])
+    dma("s", T.w3[:, 2048:4096], T.w2[:, 0:2048], ["zero"], ["w3b"])
+    op("v", lambda: v.reciprocal(T.kc[:, 14:15], fw(1)), ["fw"], ["krec"])
+    ts(T.kc[:, 11:14], T.kc[:, 20:23], 0.5, A.add, ["kb2a"], ["kb2"])
+    ts(T.kc[:, 16:20], T.fw_f[:], BIG, A.mult, ["fw"], ["kw"])
+    ts(T.kc[:, 15:16], T.kc[:, 14:15], fw(0), A.mult, ["krec", "fw"], ["krat"])
+    ts(T.pj[:, 0:1], T.pi[:, 0:1], 112, A.bitwise_and, ["pi"], ["pj"])
+    cp(T.kc[:, 24:25], T.pj[:, 0:1], ["pj"], ["kp"])
+    cp(T.sel[:, 15:143:16], T.s8b[:], ["s8b", "sel0"], ["sel"])
+    ts(T.val[:], T.vali[:], kc(24), A.subtract, ["vali", "kp"], ["val"])
+    for k in range(EARLY):
+        product_left(k)
+        product(k)
+
+    for k in range(K):
+        ts(T.xl[:, ks(k)], T.t1c[:].indirect(cu(3, k * C, (k + 1) * C)), kc(3 + k), A.add, ["t1c", "e2", "cuu2", "kcr"], ["xl%d" % k])
+        act(T.xr[:, ks(k)], T.t1c[:].indirect(cu(2, k * C, (k + 1) * C)), ["t1c", "e2", "cuu2", "kcr"], ["xr%d" % k], bias=kc(3 + k))
+        if k < 2:
+            ts(T.invu[:, k * 256:(k + 1) * 256], T.invf[:, k * 256:(k + 1) * 256], 0.25 - OFF, A.add, ["invf%d" % k], ["invu%d" % k])
+    XL, XR = ["xl0", "xl1", "xl2", "xlz", "invu0"], ["xr0", "xr1", "xr2", "xrz", "invu1"]
+
+    def offer(s, u, own):
+        c0 = s * 256 + u * 64
+        return (T.xr if s else T.xl)[:].indirect(T.invu[:, c0:c0 + C] if own else T.invu[:, c0 + C:c0 + 64])
+
+    act(T.sb4[:], offer(1, 0, False), XR, ["sb4"])
+    act(T.sb5[:], offer(1, 1, False), XR, ["sb5"])
+    act(T.sb6[:], offer(1, 2, False), XR, ["sb6"])
+    act(T.pa[:, 0:GH], T.sb5[:], ["sb5"], ["qa"], ["pa"])
+    cp(T.ga[:], offer(0, 0, False), XL, ["ga"])
+    tt(T.gb[:], offer(1, 3, False), T.sb4[:], A.max, XR + ["sb4"], ["gb"])
+    tt(T.ga[:], offer(0, 1, False), T.ga[:], A.max, XL + ["ga"], ["ga"])
+    tt(T.gb[:], offer(0, 2, False), T.gb[:], A.max, XL + ["gb"], ["gb"])
+    tt(T.ga[:], offer(0, 3, False), T.ga[:], A.max, XL + ["ga"], ["ga"])
+    tt(T.pa[:, 0:GH], T.sb6[:], T.pa[:, 0:GH], A.max, ["sb6", "qa"], ["qa"], ["pa"])
+    tt(T.pa[:, 0:GH], T.gb[:], T.pa[:, 0:GH], A.max, ["gb", "qa"], ["qa"], ["pa"])
+    tt(T.sb3[:], T.ga[:], T.pa[:, 0:GH], A.max, ["ga", "qa"], ["sb3"], ["pa"])
+    seq3 = exchange("e3", T.sb3, T.rb3, 0, ["sb3"])
+    for j in range(4):
+        dma("s", wins[j // 2][:, (j % 2) * 2048:(j % 2 + 1) * 2048], T.w2[:, 0:2048], ["zero", "sente3"], ["w%d" % (j // 2)] * (1 - j % 2) + ["wz%d" % j])
+
+    vb = [("p1a", T.p1[:, 0:352], "q1a"), ("p1b", T.p1[:, 512:864], "q1b"), ("pb", T.pb[:, 0:352], "qb"), ("pa", T.pa[:, 0:352], "qa")]
+
+    def sum2(j):
+        k, c0 = j // 2, j * 352
+        bank, ps, tok = vb[j % 4]
+        mm([(ps, T.ident[:], T.xl[:, c0:c0 + 352]), (ps, T.ident[:], T.xr[:, c0:c0 + 352])], ["ident", "xl%d" % k, "xr%d" % k], [tok, "m01"], [bank])
+
+    def sign2(j):
+        bank, ps, tok = vb[j % 4]
+        act(T.vt2[:, j * 352:(j + 1) * 352], ps, [tok, "kb2"], ["vt2_%d" % j], [bank], f=AF.Sign, bias=kc(11 + j // 2))
+
+    for j in range(4):
+        sum2(j)
+
+    def count(out, votes, c0, c1, r, w, x):
+        mm([(out, T.sel[:, 15 - i:143 - i], votes[:, c0 + i:c1:16]) for i in range(16)], ["sel"] + r, w, x)
+
+    act(T.oa[:], offer(0, 3, True), XL, ["oa"])
+    act(T.nm[:], offer(1, 0, True), XR, ["nm"])
+    act(T.p2[:, 0:V], T.nm[:], ["nm"], ["q2"], P2)
+    for u, name in ((1, "ob"), (2, "o0"), (3, "o1")):
+        act(T[name][:], offer(1, u, True), XR, [name])
+        if u == 1:
+            for j in range(2):
+                sign2(j)
+                sum2(4 + j)
+    for k in range(EARLY, K):
+        product_left(k)
+    for j in range(2, 6):
+        sign2(j)
+    for u in range(3):
+        tt(T.oa[:], offer(0, u, True), T.oa[:], A.max, XL + ["oa"], ["oa"])
+    for name in ("ob", "o0", "o1"):
+        tt(T.p2[:, 0:V], T[name][:], T.p2[:, 0:V], A.max, [name, "q2"], ["q2"], P2)
+    tt(T.oc[:], T.oa[:], T.p2[:, 0:V], A.max, ["oa", "q2"], ["oc"], P2)
+    act(T.p1[:, 0:V], T.nr[:, ks(1)], ["nr1"], ["pn1", "q1a", "q1b"], ["p1"])
+    act(T.p2[:, 0:V], T.nr[:, ks(2)], ["nr2"], ["pn2", "q2"], P2)
+    for k in range(EARLY, K):
+        product(k)
+    count(T.pb[:, 380:512], T.vt2, 0, KV, ["vt2_%d" % j for j in range(6)], ["cnt2"], ["pb"])
+
+    def home(e, seq, acc, name, rb, n, f):
+        for d in seq:
+            off = T.sndu[:, n * 20 + (d - 1) * 4:n * 20 + d * 4]
+            blk = slice((d - 1) * G, d * G)
+            tt(T.ht[:, blk], acc[:].indirect(off), rb[:, blk], f, [name, "sndu", "%s_%d" % (e, d)], ["ht%d" % d])
+            cp(acc[:].indirect(off), T.ht[:, blk], ["ht%d" % d, "sndu"], [name])
+
+    home("e3", seq3, T.oc, "oc", T.rb3, 1, A.max)
+
+    tt(T.vt1[:, ks(0)], T.oc[:], T.p0[:, 0:V], A.is_ge, ["oc", "pn0"], ["vt1_0"], ["p0"])
+    tt(T.vt1[:, ks(1)], T.oc[:], T.p1[:, 0:V], A.is_ge, ["oc", "pn1"], ["vt1_1"], ["p1"])
+    count(T.pa[:, 0:88], T.vt1, 0, 2 * V, ["vt1_0", "vt1_1"], ["cntA", "qa"], ["pa"])
+    tt(T.vt1[:, ks(2)], T.oc[:], T.p2[:, 0:V], A.is_ge, ["oc", "pn2"], ["vt1_2"], P2)
+    count(T.pb[:, 0:C], T.vt1, 2 * V, KV, ["vt1_2"], ["cntB", "qb"], ["pb"])
+    ts2(T.pa[:, 0:88], T.pa[:, 0:88], 7.5, A.is_lt, DEAD, A.mult, ["cntA"], ["cntA"], ["pa"])
+    tt(T.uu[:, 0:88], T.val[:, 0:88], T.pa[:, 0:88], A.add, ["val", "cntA"], ["uA"], ["pa"])
+    ts2(T.pb[:, 0:C], T.pb[:, 0:C], 7.5, A.is_lt, DEAD, A.mult, ["cntB"], ["cntB"], ["pb"])
+    tt(T.mn[:], T.uu[:, 0:C], T.uu[:, C:88], A.min, ["uA"], ["mn"])
+    tt(T.uu[:, 88:132], T.val[:, 88:132], T.pb[:, 0:C], A.add, ["val", "cntB"], ["uB"], ["pb"])
+    tt(T.mx[:], T.uu[:, 0:C], T.uu[:, C:88], A.max, ["uA"], ["mx"])
+    tt(T.idxf[:, 0:C], T.mn[:], T.uu[:, 88:132], A.min, ["mn", "uB"], ["i0"])
+    tt(T.tt[:], T.mx[:], T.uu[:, 88:132], A.min, ["mx", "uB"], ["tt"])
+    ts(T.idxu[:, 0:C], T.idxf[:, 0:C], float(KV), A.min, ["i0"], ["idx0"])
+    tt(T.idxf[:, C:88], T.mn[:], T.tt[:], A.max, ["mn", "tt"], ["i1"])
+    PP = ["pp0", "pp1", "pp2", "ppz"]
+    for h in range(2):
+        act(T.a0[:, h * 352:(h + 1) * 352], T.pp[:].indirect(T.idxu[:, h * 22:(h + 1) * 22]), PP + ["idx0", "krat"], ["a0%d" % h], scale=kc(15))
+    ts(T.idxu[:, C:88], T.idxf[:, C:88], float(KV), A.min, ["i1"], ["idx1"])
+    for h in range(2):
+        tt(T.t1[:, h * 352:(h + 1) * 352], T.pp[:].indirect(T.idxu[:, C + h * 22:C + (h + 1) * 22]), T.a0[:, h * 352:(h + 1) * 352], A.add,
+           PP + ["idx1", "a0%d" % h], ["t1%d" % h])
+    cp(T.sb4[:], T.t1[:, 0:V].indirect(T.sndu[:, 20:40]), ["t10", "t11", "sndu"], ["sb4"])
+    exchange("e4", T.sb4, T.t1, V, ["sb4"])
+    for b in range(2):
+        act(T.tw[:, ks(b)], T.top_b[:], ["top", "kw"], ["tw%d" % b], scale=kc(18 + b))
+    act(T.idents[:], T.ident[:], ["ident"], ["idents"], scale=1.0 / BIG)
+    act(T.dg0[:], T.ident[:], ["ident", "kw"], ["dg0"], scale=kc(18))
+    act(T.dg1[:], T.ident[:], ["ident", "kw"], ["dg1"], scale=kc(19))
+    for b in range(2):
+        act(T["t0w%d" % b][:, 0:W], T.t0b[:], ["t0b", "ef", "kw"], ["t0w%d" % b], scale=kc(16 + b))
+
+    def choose(m, dead, su, gu, name):
+        BASE = ["base0", "base1", "base2"]
+        for s in range(2):
+            for c0, c1, ap, tok, bank in dead:
+                tt(T.key[:, s, c0:c1], T.base[:, 2 * m + s, c0:c1], ap, A.add, BASE + [tok], ["key%d%d" % (s, c0)], [bank])
+        KEY = ["key%d%d" % (s, d[0]) for s in range(2) for d in dead]
+        k0, k1, k2 = [T.key[:, :, k * C:(k + 1) * C] for k in range(K)]
+        tt(T.kmx[:], k0, k1, A.max, KEY, ["kmx"])
+        tt(T.kmn[:], k0, k1, A.min, KEY, ["kmn"])
+        tt(T.kt[:], T.kmx[:], k2, A.min, KEY + ["kmx"], ["kt"])
+        tt(T.ksel[:, :, 0:C], T.kmn[:], k2, A.min, KEY + ["kmn"], ["ksa"])
+        tt(T.ksel[:, :, C:88], T.kmn[:], T.kt[:], A.max, ["kmn", "kt"], ["ksb"])
+        ts(T.kg[:], T.ksel[:], 4096 + W - 1, A.bitwise_and, ["ksa", "ksb"], ["kg"])
+        ts(T.ks[:], T.ksel[:], 4095, A.bitwise_and, ["ksa", "ksb"], ["ks"])
+        ts(gu[:], T.kg[:], float(W), A.min, ["kg"], ["gu" + name])
+        cp(su[:], T.ks[:], ["ks"], ["su" + name])
+
+    for k in range(K):
+        ts(T.base[:, :, k * C:(k + 1) * C], T.fu_i[:, :, k * C:(k + 1) * C], float(k * 8192), A.add, ["fu"], ["base%d" % k])
+    ts2(T.pb[:, 380:512], T.pb[:, 380:512], -1.0, A.is_lt, DEAD, A.mult, ["cnt2"], ["cnt2"], ["pb"])
+    choose(1, [(0, 132, T.pb[:, 380:512], "cnt2", "pb")], T.su2, T.gu2, "2")
+    choose(0, [(0, 88, T.pa[:, 0:88], "cntA", "pa"), (88, 132, T.pb[:, 0:C], "cntB", "pb")], T.su1, T.gu1, "1")
+
+    def fold(wl, wr, tl, tr, c0, n, npe, pv, bv, pt, bt, tmp, tn, out, on, between=None):
+        sl = lambda w, u: w[:, u * W + c0:u * W + c0 + n]
+        qv, qt, acc = "q" + bv, "q" + bt, pv[:, 0:n]
+        done = []
+        for b0 in range(0, n if npe else 0, 512):
+            m = min(512, n - b0)
+            mm([(pt[:, b0:b0 + m], T.idents[:], wr[:, u * W + c0 + b0:u * W + c0 + b0 + m]) for u in range(npe)], ["idents", tr], [qt + str(b0)], [bt])
+            done.append(qt + str(b0))
+        rest, left = list(range(npe, U)), list(range(U))
+        if len(rest) == 0:
+            tt(acc, sl(wl, 0), sl(wl, 1), A.add, [tl], [qv], [bv]); left = left[2:]
+        elif len(rest) == 1 and c0 == 0:
+            act(acc, sl(wr, rest[0]), [tr], [qv], [bv], scale=1.0 / BIG)
+        elif len(rest) == 1:
+            ts(acc, sl(wr, rest[0]), 1.0 / BIG, A.mult, [tr], [qv], [bv])
+        else:
+            tt(acc, sl(wr, rest[0]), sl(wr, rest[1]), A.add, [tr], [qv], [bv])
+            for u in rest[2:]:
+                tt(acc, sl(wr, u), acc, A.add, [tr, qv], [qv], [bv])
+            ts(acc, acc, 1.0 / BIG, A.mult, [qv], [qv], [bv])
+        for u in left[:-1]:
+            tt(acc, sl(wl, u), acc, A.add, [tl, qv], [qv], [bv])
+        if npe:
+            tt(tmp[:], sl(wl, left[-1]), acc, A.add, [tl, qv], [tn], [bv])
+            if between:
+                between()
+            tt(out[:], tmp[:], pt[:, 0:n], A.add, [tn] + done, [on], [bt])
+        else:
+            tt(out[:], sl(wl, left[-1]), acc, A.add, [tl, qv], [on], [bv])
+            if between:
+                between()
+
+    T1 = ["t10", "t11", "t1z", "e4", "gu2"]
+
+    def inside2(b):
+        tt(T.bb[:, ks(b)], T.t1[:].indirect(T.gu2[:, 0, b * C:(b + 1) * C]), T.xl[:, ks(b)], A.mult, T1 + ["xl%d" % b], ["bb%d" % b])
+        for b0, m, bank in ((0, 512, "p2a"), (512, V - 512, "p2b")):
+            op("p", lambda: pe.matmul(T.p2[:, b0:b0 + m], T["dg%d" % b][:], T.bb[:, b * V + b0:b * V + b0 + m], b == 0, b == 1),
+               ["dg%d" % b, "bb%d" % b], ["y" + bank], [bank])
+
+    for b in range(2):
+        tt(T.xr[:, ks(b)], T.t1[:].indirect(T.gu2[:, 0, b * C:(b + 1) * C]), T.tw[:, ks(b)], A.mult, T1 + ["tw%d" % b], ["xr%d" % b])
+    act(T.xl[:, 0:2 * V], T.t1[:].indirect(T.gu2[:, 1, :]), T1, ["xl0", "xl1"], scale=1.0 / BIG)
+    tt(T.w2[:].indirect(T.su2[:, 0, :]), T.xl[:, 0:2 * V], T.tw[:], A.mult, ["xl0", "xl1", "tw0", "tw1", "su2", "w2b"], ["zero", "w2"])
+    act(T.w3[:].indirect(T.su2[:, 1, :]), T.xr[:, 0:2 * V], ["xr0", "xr1", "su2", "w3a", "w3b"], ["w3"], f=AF.Silu)
+    fold(T.w2, T.w3, "w2", "w3", V, GH, PE_G, T.pa, "pa", T.pb, "pb", T.ga, "ga", T.sb5, "sb5")
+    seq5 = exchange("e5", T.sb5, T.rb5, 0, ["sb5"])
+    fold(T.w2, T.w3, "w2", "w3", 0, V, PE_O, T.p0, "p0", T.p1, "p1", T.oa, "oa", T.o1, "o1",
+         lambda: [inside2(b) for b in range(YI5)])
+    for b in range(2):
+        act(T.nr[:, ks(b)], T["t0w%d" % b][:].indirect(T.gu1[:, 1, b * C:(b + 1) * C]), ["t0w%d" % b, "t0w%dz" % b, "gu1"], ["nr%d" % b], scale=1.0 / BIG)
+    home("e5", seq5, T.o1, "o1", T.rb5, 1, A.add)
+
+    for b in range(2):
+        tt(T.xr[:, ks(b)], T["t0w%d" % b][:].indirect(T.gu1[:, 0, b * C:(b + 1) * C]), T.o1[:], A.mult,
+           ["t0w%d" % b, "t0w%dz" % b, "gu1", "o1"], ["xr%d" % b])
+        act(T.w1[:].indirect(T.su1[:, 1, b * C:(b + 1) * C]), T.xr[:, ks(b)], ["xr%d" % b, "su1", "wz2", "wz3"], ["w1"], f=AF.Silu)
+    for b in range(2):
+        tt(T.w0[:].indirect(T.su1[:, 0, b * C:(b + 1) * C]), T.nr[:, ks(b)], T.o1[:], A.mult, ["nr%d" % b, "o1", "su1", "wz0", "wz1"], ["w0"])
+    fold(T.w0, T.w1, "w0", "w1", V, GH, PE_G, T.pa, "pa", T.pb, "pb", T.ga, "ga", T.sb6, "sb6")
+    seq6 = exchange("e6", T.sb6, T.rb6, 0, ["sb6"])
+    fold(T.w0, T.w1, "w0", "w1", 0, V, PE_O, T.p0, "p0", T.p1, "p1", T.oa, "oa", T.o0, "o0",
+         lambda: [inside2(b) for b in range(YI5, 2)])
+    act(T.yib[:], T.p2[:, 0:V], ["yp2a", "yp2b"], ["yib"], P2)
+    dma("s", T.yi[:], T.yib[:], ["yib"], ["yi"])
+    home("e6", seq6, T.o0, "o0", T.rb6, 0, A.add)
+    dma("s", T.yo[:], T.o0[:], ["o0"], ["yo"])
+
+    for s in sorted(cnt):
+        need("g", ("end", s, cnt[s], {}))

@@ -2,15 +2,16 @@ from concourse.bass import DstId, RemoteDMATransfer
 from concourse.mybir import AluOpType, ActivationFunctionType
 
 N, V, W, U, ND, G, K = 8, 704, 1024, 4, 5, 64, 3
-KV, GH, C = K * V, ND * G, V // 16
+KV, GH, C, HV = K * V, ND * G, V // 16, V // 2
 BIG = float(2 ** 40)
 OFF = 32
 DEAD = float(2 ** 15 + 2 ** 12)
 PE_G, PE_O = 3, 3
-ACT1, ACT2, DVE1 = 3, 2, 2
-EARLY = 2
-YI5 = 1
+ACT1, DVE1, ACT2 = 4, 3, 3
+B_CUT = (0, 12, 44, 88, 110, 132)
 SPLIT_F, SPLIT_B = [4, 1], [2, 2, 1]
+OWN, OWNV = "0acp1bde2n3", "lblblrbrr"
+HALVES = 2
 
 F, I, H, B16 = "float32", "int32", "uint16", "bfloat16"
 
@@ -21,20 +22,21 @@ def _sb(n, dt=F):
 
 SCRATCH = {
     "cl_i": _sb(V, I), "snd_i": _sb(40, I), "cu_i": _sb(528, I), "fu_i": _sb([4, 132], I), "cr_i": _sb(8, I), "th_i": _sb(4, I),
-    "fw_f": _sb(4), "top_b": _sb(V, B16), "t0b": _sb(W, B16), "kc": _sb(32),
-    "sndu": _sb(40, H), "cuu": _sb(528, H), "zpu": _sb(264, H), "fcu": _sb([2, 132], H), "invu": _sb(512, H), "idxu": _sb(88, H),
-    "ti": _sb(264, I), "tj": _sb(264, I), "tk": _sb(264, I), "tf": _sb(264), "tg": _sb(264), "t3": _sb([2, 132], I), "base": _sb([4, 132]),
+    "fw_f": _sb(4), "top_b": _sb(V, B16), "t0b": _sb(W + 16, B16), "kc": _sb(32),
+    "sndu": _sb(40, H), "cuu": _sb(528, H), "zpu": _sb(264, H), "invu": _sb(512, H), "lk0": _sb(64, H), "lk1": _sb(64, H),
+    "ti": _sb(264, I), "tj": _sb(264, I), "tk": _sb(264, I), "tg": _sb(264), "base": _sb([4, 132]),
     "w0": _sb(U * W), "w1": _sb(U * W), "w2": _sb(U * W), "w3": _sb(U * W), "fill": _sb(256), "invf": _sb(512),
-    "nt0": _sb(W), "bb": _sb(KV), "nr": _sb(KV), "nm": _sb(V), "t1c": _sb(W), "xl": _sb(KV + 8), "xr": _sb(KV + 8), "pp": _sb(KV + 8),
-    "ga": _sb(GH), "gb": _sb(GH), "oa": _sb(V), "ob": _sb(V), "oc": _sb(V), "o1": _sb(V), "o0": _sb(V), "ht": _sb(GH), "a0": _sb(V),
+    "t0c": _sb(W), "bb": _sb(KV), "ss": _sb(KV), "t1c": _sb(W), "xl": _sb(KV + 8), "xr": _sb(KV + 8), "pp": _sb(KV),
+    "zp0": _sb(W), "zp1": _sb(W), "xc": _sb(W), "x1": _sb(W), "x0": _sb(W), "wl": _sb(2 * V), "wr": _sb(2 * V), "pr": _sb(2 * V),
+    "ga": _sb(GH), "gb": _sb(GH), "oa": _sb(V), "ob": _sb(V), "oc": _sb(V), "od": _sb(V), "o1": _sb(V), "o0": _sb(V), "n0": _sb(V),
     "sb1": _sb(GH), "sbf": _sb(GH, B16), "sb2": _sb(GH), "sb3": _sb(GH), "sb4": _sb(GH), "sb5": _sb(GH), "sb6": _sb(GH),
     "rb3": _sb(GH), "rb5": _sb(GH), "rb6": _sb(GH),
-    "vt1": _sb(KV, B16), "vt2": _sb(KV, B16), "sel": _sb(144, B16), "ones": _sb(128), "ident": _sb(128), "idents": _sb(128),
-    "dg0": _sb(128), "dg1": _sb(128), "s8a": _sb(8), "s8b": _sb(8), "pi": _sb(4, I), "pj": _sb(4, I), "vali": _sb(132), "val": _sb(132),
-    "uu": _sb(132), "mn": _sb(C), "mx": _sb(C), "tt": _sb(C), "idxf": _sb(88),
-    "key": _sb([2, 132]), "kmn": _sb([2, C]), "kmx": _sb([2, C]), "kt": _sb([2, C]), "ksel": _sb([2, 88], I), "ks": _sb([2, 88], I), "kg": _sb([2, 88], I),
+    "vt1": _sb(KV, B16), "vt2": _sb(KV, B16), "sel": _sb(144, B16), "self": _sb(144), "ones": _sb(128), "ident": _sb(128),
+    "s8a": _sb(8), "s8b": _sb(8),
+    "key": _sb([2, 132]), "kmn": _sb([2, C]), "kmx": _sb([2, C]), "kt": _sb([2, C]), "kg": _sb([2, 88], I),
+    "ksel1": _sb([2, 88], I), "ksel2": _sb([2, 88], I), "ks1": _sb([2, 88], I), "ks2": _sb([2, 88], I),
     "su1": _sb([2, 88], H), "gu1": _sb([2, 88], H), "su2": _sb([2, 88], H), "gu2": _sb([2, 88], H),
-    "t1": _sb(W + 8), "t0w0": _sb(W + 8), "t0w1": _sb(W + 8), "tw": _sb(2 * V), "yib": _sb(V),
+    "t1": _sb(W + 8), "tw": _sb(2 * V), "yib": _sb(V),
     "p0": ("psum", [128, 1024], F), "p1": ("psum", [128, 1024], F), "p2": ("psum", [128, 1024], F), "pa": ("psum", [128, 512], F), "pb": ("psum", [128, 512], F),
 }
 FWD, BACK = ["e1", "ef", "e2", "e4"], ["e3", "e5", "e6"]
@@ -58,6 +60,15 @@ def calls_of(topo, cores, r, sign):
     return calls
 
 
+def arrivals(topo, cores, r, sign):
+    late = []
+    for d in range(1, ND + 1):
+        q = (r - sign * d) % N
+        for j, call in enumerate(calls_of(topo, cores, q, sign)):
+            late += [(j, cores[q] not in topo.cores_of(cores[r]), d, len(eng)) for d2, eng in call if d2 == d]
+    return [(d, n) for j, far, d, n in sorted(late)]
+
+
 def rank_program(g, core, T, topo):
     rank = T.rank_of(core)
     if rank is None:
@@ -78,16 +89,13 @@ def rank_program(g, core, T, topo):
             if clock[q].get(k2, 0) < v2:
                 clock[q][k2] = v2
 
-    def banks(x):
-        return [b for t in x for b in (["p1a", "p1b"] if t == "p1" else [t])]
-
-    def order(q, r, w, x, dma):
+    def order(q, r, w, x):
         evs = []
         for t in r:
             evs += writer[t]
         for t in w:
-            evs += [ev for ev in writer.get(t, []) + readers.get(t, [])]
-        evs += [holder[t] for t in banks(x) if t in holder and holder[t][0] != q]
+            evs += writer.get(t, []) + readers.get(t, [])
+        evs += [holder[t] for t in x if t in holder and holder[t][0] != q]
         for ev in sorted(evs, key=lambda ev: -ev[2]):
             need(q, ev)
 
@@ -96,26 +104,28 @@ def rank_program(g, core, T, topo):
             readers.setdefault(t, []).append(ev)
         for t in w:
             writer[t] = [ev]; readers[t] = []
-        for t in banks(x):
+        for t in x:
             holder[t] = ev
 
     def op(q, fn, r=(), w=(), x=()):
-        order(q, r, w, x, False)
+        order(q, r, w, x)
         s = "c" + q
         cnt[s] = cnt.get(s, 0) + 1
         fn().then_inc(T.sem[s], 1)
         note((q, s, cnt[s], dict(clock[q])), r, w, x)
 
     def dma(q, out, in_, r=(), w=()):
-        order(q, r, w, (), True)
+        order(q, r, w, ())
         s = "d%d" % nd[0]; nd[0] += 1
         cnt[s] = 16
         Q[q].dma_start(out, in_).then_inc(T.sem[s], 16)
         note(("dma", s, 16, dict(clock[q])), r, w, ())
 
-    def exchange(e, src, dst, at, r):
+    seq = [d for d, n in arrivals(topo, cores, rank, 1)]
+
+    def exchange(e, src, dst, at, r, after=()):
         sign = -1 if e in FWD else 1
-        order("g", r, (), (), True)
+        order("g", list(r) + list(after), (), ())
         total = 0
         for call in calls_of(topo, cores, rank, sign):
             trs = []
@@ -128,17 +138,10 @@ def rank_program(g, core, T, topo):
             g.remote_dma_fused(trs, local_sem=T.sem["s" + e])
         cnt["s" + e] = total
         note(("dma", "s" + e, total, dict(clock["g"])), r, ["sent" + e], ())
-        late = {}
-        for d in range(1, ND + 1):
-            for j, call in enumerate(calls_of(topo, cores, (rank - sign * d) % N, sign)):
-                for d2, eng in call:
-                    if d2 == d:
-                        s = e if e in FWD else "%s_%d" % (e, d)
-                        cnt[s] = cnt.get(s, 0) + len(eng)
-                        late[d] = (j, cores[(rank - sign * d) % N] not in topo.cores_of(core), d)
-        for s in ([e] if e in FWD else ["%s_%d" % (e, d) for d in range(1, ND + 1)]):
+        for d, n in arrivals(topo, cores, rank, sign):
+            s = e if e in FWD else "%s_%d" % (e, d)
+            cnt[s] = cnt.get(s, 0) + n
             writer[s] = [("dma", s, cnt[s], {})]
-        return sorted(late, key=lambda d: late[d])
 
     v, a, pe = g.vector, g.scalar, g.tensor
     tt = lambda o, i0, i1, f, r, w, x=(): op("v", lambda: v.tensor_tensor(o, i0, i1, f), r, w, x)
@@ -146,63 +149,85 @@ def rank_program(g, core, T, topo):
     ts2 = lambda o, i0, s1, f, s2, f2, r, w, x=(): op("v", lambda: v.tensor_scalar(o, i0, s1, s2, f, f2), r, w, x)
     cp = lambda o, i0, r, w, x=(): op("v", lambda: v.tensor_copy(o, i0), r, w, x)
     ms = lambda o, c, w: op("v", lambda: v.memset(o, c), (), w)
+    later = lambda f, *args: lambda: f(*args)
+
+    def run(calls, n=None):
+        for j in range(len(calls) if n is None else min(n, len(calls))):
+            calls.pop(0)()
+
+    def weave(*chains):
+        while any(chains):
+            for c in chains:
+                run(c, 1)
 
     def act(o, i0, r, w, x=(), f=None, **kw):
         op("a", lambda: a.activation(o, i0, AF.Identity if f is None else f, **kw), r, w, x)
 
-    def mm(items, r, w, x):
+    def mm(groups, r, w, x):
         def fn():
-            for j, (o, l, rr) in enumerate(items):
-                ins = pe.matmul(o, l, rr, j == 0, j == len(items) - 1)
+            for items in groups:
+                for j, (o, l, rr) in enumerate(items):
+                    ins = pe.matmul(o, l, rr, j == 0, j == len(items) - 1)
             return ins
         op("p", fn, r, w, x)
+
+    def pe_sum(ps, srcs, n, r, w, x):
+        mm([[(ps[:, b0:min(n, b0 + 512)], T.ident[:], t[:, c + b0:c + min(n, b0 + 512)]) for t, c in srcs] for b0 in range(0, n, 512)],
+           ["ident"] + r, w, x)
+
+    def iota(o, pattern, base, w, r=()):
+        op("g", lambda: g.iota(o, pattern, base, 0, allow_small_or_imprecise_dtypes=True), r, w)
+
+    def tolist(out, sel, x, c0, c1, r, w, bank):
+        mm([[(out, T[sel][:, 15 - i:143 - i], x[:, c0 + i:c1:16]) for i in range(16)]], [sel] + r, w, bank)
 
     kc = lambda j: T.kc[:, j:j + 1]
     fw = lambda j: T.fw_f[:, j:j + 1]
     ks = lambda k: slice(k * V, (k + 1) * V)
     wins = [T.w0, T.w1, T.w2, T.w3]
     rows8 = slice(0, 128, 18)
-    P2 = ["p2a", "p2b"]
+    P0, P1, P2, PA, PB = ["p0"], ["p1"], ["p2"], ["pa"], ["pb"]
+    snd = lambda n, d: T.sndu[:, n * 20 + (d - 1) * 4:n * 20 + d * 4]
 
     dma("s", T.cl_i[:], T.cl[:], w=["cl"])
     dma("a", T.snd_i[:], T.snd[:], w=["snd_i"])
     dma("a", T.cu_i[:, 264:528], T.cu[:, 264:528], w=["cu2"])
-    op("g", lambda: g.iota(T.pp[:, 0:V], [[1, V]], OFF, 0, allow_small_or_imprecise_dtypes=True), w=["pp0"])
+    iota(T.pp[:, 0:V], [[1, V]], OFF, ["pp0"])
     ms(T.fill[:], float(KV + OFF), ["fill"])
-    dma("s", T.t0b[:, 0:V], T.fl[:], w=["t0b"])
     dma("s", T.w0[rows8, :], T.fill[:], r=["fill"], w=["w0"])
     dma("s", T.w1[rows8, :], T.fill[:], r=["fill"], w=["w1"])
     dma("s", T.cu_i[:, 0:264], T.cu[:, 0:264], w=["cu1"])
     dma("s", T.cr_i[:, 0:6], T.cr[:], w=["cr"])
+    dma("s", T.t0b[:, 0:V], T.fl[:], w=["t0b"])
     dma("s", T.th_i[:, 0:2], T.th[:], w=["th"])
     dma("s", T.fw_f[:], T.fw[:], w=["fw"])
     dma("s", T.fu_i[:], T.fu[:], w=["fu"])
     dma("s", T.top_b[:], T.top[:], w=["top"])
-    for name in ("xl", "xr", "pp"):
+    for name in ("xl", "xr"):
         ms(T[name][:, KV:KV + 8], 0.0, [name + "z"])
-    for name in ("t1", "t0w0", "t0w1"):
-        ms(T[name][:, W:W + 8], 0.0, [name + "z"])
-    ms(T.sel[:], 0.0, ["sel0"])
-    ms(T.w2[:, 0:512], 0.0, ["zero0"])
+    ms(T.t1[:, W:W + 8], 0.0, ["t1z"])
+    ms(T.t0b[:, W:W + 16], 0.0, ["t0z"])
+    ms(T.self[:], 0.0, ["sel0"])
+    ms(T.w2[:, 0:1024], 0.0, ["zero0"])
     act(T.pp[:, ks(1)], T.pp[:, ks(0)], ["pp0"], ["pp1"], f=AF.Silu, bias=float(V))
     ts(T.pp[:, ks(2)], T.pp[:, ks(0)], float(2 * V), A.add, ["pp0"], ["pp2"])
 
     cp(T.sndu[:], T.snd_i[:], ["snd_i"], ["sndu"])
-    ts(T.sb1[:], T.cl_i[:, 0:V].indirect(T.sndu[:, 0:20]), -1.0, A.mult, ["cl", "sndu"], ["sb1"])
-    exchange("e1", T.sb1, T.nt0, V, ["sb1"])
-    act(T.sbf[:], T.t0b[:, 0:V].indirect(T.sndu[:, 0:20]), ["t0b", "sndu"], ["sbf"])
-    ts(T.ti[:], T.cu_i[:, 264:528], 4, A.arith_shift_right, ["cu2"], ["ti"])
-    ts(T.tf[:], T.ti[:], -4095.0 / 256.0, A.mult, ["ti"], ["tf"])
-    tt(T.tg[:], T.cu_i[:, 264:528], T.tf[:], A.add, ["cu2", "tf"], ["tg"])
-    ts(T.zpu[:], T.tg[:], 256.0, A.mult, ["tg"], ["zpu"])
-    ts(T.tj[:], T.cu_i[:, 0:264], W - 1, A.bitwise_and, ["cu1"], ["tj"])
-    exchange("ef", T.sbf, T.t0b, V, ["sbf"])
-    op("g", lambda: g.iota(T.w2[:, 512:2048], [[0, 1536]], 0, 0, allow_small_or_imprecise_dtypes=True), ["zero0"], ["zero"])
-    op("g", lambda: g.iota(T.ones[:], [[0, 128]], 1, 0, allow_small_or_imprecise_dtypes=True), w=["ones"])
-    op("g", lambda: g.iota(T.pi[:, 0:1], [[0, 1]], 0, 1), w=["pi"])
-    op("g", lambda: g.affine_select(T.ident[:], T.ones[:], [[-1, 128]], A.is_equal, 0.0, 0, 1), ["ones"], ["ident"])
+    cp(T.sb1[:], T.cl_i[:, 0:V].indirect(T.sndu[:, 0:20]), ["cl", "sndu"], ["sb1"])
+    exchange("e1", T.sb1, T.t0c, V, ["sb1"])
+
+    def window_columns(s):
+        c = slice(s * 132, (s + 1) * 132); z = T.cu_i[:, 264 + s * 132:396 + s * 132]
+        return [later(ts, T.ti[:, c], z, 4, A.arith_shift_right, ["cu2"], ["ti%d" % s]),
+                later(ts, T.pa[:, c], T.ti[:, c], -4095.0 / 256.0, A.mult, ["ti%d" % s], ["tf%d" % s], PA),
+                later(tt, T.tg[:, c], z, T.pa[:, c], A.add, ["cu2", "tf%d" % s], ["tg%d" % s], PA),
+                later(ts, T.zpu[:, c], T.tg[:, c], 256.0, A.mult, ["tg%d" % s], ["zpu%d" % s])]
+
+    weave(window_columns(0), window_columns(1))
+    iota(T.ones[:], [[0, 128]], 1, ["ones"])
+    iota(T.w2[:, 1024:2048], [[0, 1024]], 0, ["zero"], ["zero0"])
     op("g", lambda: g.affine_select(T.s8a[:], T.ones[:, 0:8], [[-16, 8]], A.is_ge, 0.0, 0, 1), ["ones"], ["s8a"])
-    op("g", lambda: g.iota(T.vali[:], [[16, 132]], 0, 1, allow_small_or_imprecise_dtypes=True), w=["vali"])
+    op("g", lambda: g.affine_select(T.ident[:], T.ones[:], [[-1, 128]], A.is_equal, 0.0, 0, 1), ["ones"], ["ident"])
     op("g", lambda: g.affine_select(T.s8b[:], T.s8a[:], [[16, 8]], A.is_ge, 0.0, 15, -1), ["s8a"], ["s8b"])
 
     todo = {0: list(range(6)), 1: list(range(6))}
@@ -214,263 +239,304 @@ def rank_program(g, core, T, topo):
             del todo[s][:m]
             out = wins[s][:].indirect(T.zpu[:, s * 132 + j * 22:s * 132 + (j + m) * 22])
             src = T.pp[:, j * 352:(j + m) * 352]
-            r, w = ["zpu"] + ["pp%d" % k for k in range(j // 2, (j + m + 1) // 2)], ["w%d" % s]
+            r, w = ["zpu%d" % s] + ["pp%d" % k for k in range(j // 2, (j + m + 1) // 2)], ["w%d" % s]
             if q == "a":
                 act(out, src, r, w, f=AF.Silu)
             else:
                 cp(out, src, r, w)
 
+    def links(q, n):
+        zp, name, calls = T["zp%d" % n], "zp%d" % n, []
+        for p, d in enumerate(seq):
+            c, nodes = slice(V + p * G, V + (p + 1) * G), zp[:, 0:V].indirect(snd(n, d))
+            if p:
+                calls.append(later(act if q == "a" else cp, zp[:, c], nodes, [name, "sndu"], [name + str(p)]))
+            if q == "a":
+                calls.append(later(act, nodes, T.pp[:, c], ["sndu", "pp1"], [name], (), AF.Silu))
+            else:
+                calls.append(later(cp, nodes, T.pp[:, c], ["sndu", "pp1"], [name]))
+        return calls
+
+    def links_list(n, ps, bank):
+        tolist(ps, "self", T["zp%d" % n], 0, W, ["zp%d" % n] + ["zp%d%d" % (n, p) for p in range(1, ND)], ["lkp"], bank)
+
+    def links_done(n, ps, bank):
+        ts2(T["lk%d" % n][:], ps, 1.0 / 16, A.mult, 0.25 - OFF, A.add, ["lkp"], ["lk%d" % n], bank)
+
     invert("a", 0, ACT1)
-    ts(T.nt0[:, 0:V], T.cl_i[:], -1.0, A.mult, ["cl"], ["nt0"])
+    act(T.sbf[:], T.t0b[:, 0:V].indirect(T.sndu[:, 0:20]), ["t0b", "sndu"], ["sbf"])
+    exchange("ef", T.sbf, T.t0b, V, ["sbf"], ["sente1"])
+    iota(T.zp1[:, 0:V + G], [[1, V + G]], OFF, ["zp1"])
+    iota(T.zp0[:, 0:V + G], [[1, V + G]], OFF, ["zp0"])
+    ts(T.tj[:], T.cu_i[:, 0:264], W - 1, A.bitwise_and, ["cu1"], ["tj"])
+    cp(T.t0c[:, 0:V], T.cl_i[:], ["cl"], ["t0c"])
     cp(T.cuu[:, 0:264], T.tj[:], ["tj"], ["cuu1"])
     cp(T.kc[:, 0:6], T.cr_i[:, 0:6], ["cr"], ["kcr"])
-    cp(T.kc[:, 6:8], T.th_i[:, 0:2], ["th"], ["kth"])
-    ts(T.t3[:], T.fu_i[:, 0:2, :], W - 1, A.bitwise_and, ["fu"], ["t3"])
-    ts2(T.kc[:, 8:11], T.kc[:, 0:3], -1.0, A.mult, kc(6), A.add, ["kcr", "kth"], ["kb1"])
-    cp(T.fcu[:], T.t3[:], ["t3"], ["fcu"])
-    ts(T.tk[:], T.cu_i[:, 264:528], W - 1, A.bitwise_and, ["cu2"], ["tk"])
-    ts2(T.kc[:, 20:23], T.kc[:, 3:6], kc(7), A.add, -1.0, A.mult, ["kcr", "kth"], ["kb2a"])
-    cp(T.cuu[:, 264:528], T.tk[:], ["tk"], ["cuu2"])
     invert("v", 1, DVE1)
-    dma("s", T.w2[:, 2048:4096], T.w2[:, 0:2048], ["zero", "sentef"], ["w2b"])
-    dma("s", T.w3[:, 0:2048], T.w2[:, 0:2048], ["zero"], ["w3a"])
+
+    odd = [later(cp, T.kc[:, 6:8], T.th_i[:, 0:2], ["th"], ["kth"]),
+           later(ts, T.tk[:], T.cu_i[:, 264:528], W - 1, A.bitwise_and, ["cu2"], ["tk"]),
+           later(ts2, T.kc[:, 20:23], T.kc[:, 3:6], kc(7), A.add, -1.0, A.mult, ["kcr", "kth"], ["kb2a"]),
+           later(cp, T.cuu[:, 264:528], T.tk[:], ["tk"], ["cuu2"]),
+           later(ts, T.kc[:, 11:14], T.kc[:, 20:23], 0.5, A.add, ["kb2a"], ["kb2"]),
+           later(cp, T.self[:, 15:143:16], T.s8b[:], ["s8b", "sel0"], ["self"]),
+           later(ts, T.kc[:, 18:20], T.fw_f[:, 2:4], BIG, A.mult, ["fw"], ["kw"]),
+           later(cp, T.sel[:], T.self[:], ["self"], ["sel"])]
+    bases = [later(ts, T.base[:, :, k * C:(k + 1) * C], T.fu_i[:, :, k * C:(k + 1) * C], float(k * 8192), A.add, ["fu"], ["base%d" % k])
+             for k in range(K)]
 
     cu = lambda blk, c0, c1: T.cuu[:, blk * 132 + c0:blk * 132 + c1]
-    for c0, c1 in ((0, 12), (12, C), (C, 2 * C), (2 * C, 3 * C)):
+    for c0, c1 in zip(B_CUT, B_CUT[1:]):
         k, e = c0 // C, slice(16 * c0, 16 * c1)
-        tok = ["bb%d" % k] if c0 != 0 else ["bbx"]
-        act(T.bb[:, e], T.nt0[:].indirect(cu(0, c0, c1)), ["nt0", "e1", "cuu1", "kb1"], tok, bias=kc(8 + k))
-        tt(T.nr[:, e], T.nt0[:].indirect(cu(1, c0, c1)), T.bb[:, e], A.add, ["nt0", "e1", "cuu1"] + tok, ["nr%d" % k] if c0 != 0 else ["nrx"])
-    act(T.p0[:, 0:V], T.nr[:, ks(0)], ["nr0", "nrx"], ["pn0"], ["p0"])
-    tt(T.p1[:, 0:V], T.nr[:, ks(1)], T.p0[:, 0:V], A.min, ["nr1", "pn0"], ["m01"], ["p0", "p1"])
+        act(T.bb[:, e], T.t0c[:].indirect(cu(0, c0, c1)), ["t0c", "e1", "cuu1", "kcr"], ["bb_%d" % c0], bias=kc(k))
+        tt(T.ss[:, e], T.t0c[:].indirect(cu(1, c0, c1)), T.bb[:, e], A.add, ["t0c", "e1", "cuu1", "bb_%d" % c0], ["ss_%d" % c0])
+        if c1 <= C:
+            run(odd, 3 if c0 == 0 else 2)
+    SS = [["ss_%d" % c0 for c0 in B_CUT[:-1] if c0 // C == k] for k in range(K)]
+    act(T.p1[:, 0:V], T.ss[:, ks(1)], SS[1], ["ps1"], P1)
+    tt(T.p0[:, 0:V], T.ss[:, ks(0)], T.p1[:, 0:V], A.max, SS[0] + ["ps1"], ["m01"], P0 + P1)
     invert("a", 1, ACT2)
-    tt(T.nm[:], T.nr[:, ks(2)], T.p1[:, 0:V], A.min, ["nr2", "m01"], ["nm"], ["p1"])
-    ts2(T.sb2[:], T.nm[:].indirect(T.sndu[:, 20:40]), -1.0, A.mult, kc(6), A.add, ["nm", "sndu", "kth"], ["sb2"])
+    run(odd, 2)
+    tt(T.t1c[:, 0:V], T.ss[:, ks(2)], T.p0[:, 0:V], A.max, SS[2] + ["m01"], ["t1c"], P0)
+    run(odd)
+    cp(T.sb2[:], T.t1c[:, 0:V].indirect(T.sndu[:, 20:40]), ["t1c", "sndu"], ["sb2"])
     exchange("e2", T.sb2, T.t1c, V, ["sb2"])
+    pe_sum(T.p2, [(T.ss, 2 * V)], V, SS[2], ["ps2"], P2)
 
-    def product_left(k):
-        act(T.bb[:, ks(k)], T.t0b[:].indirect(T.fcu[:, 0, k * C:(k + 1) * C]), ["t0b", "ef", "fcu", "fw"], ["bb%d" % k, "bbx"], scale=fw(1))
-
-    def product(k):
-        tt(T.pp[:, ks(k)], T.t0b[:].indirect(T.fcu[:, 1, k * C:(k + 1) * C]), T.bb[:, ks(k)], A.mult, ["t0b", "ef", "fcu", "bb%d" % k], ["pp%d" % k])
-
-    invert("v", 0, 6)
-    invert("a", 1, 6)
-    act(T.t1c[:, 0:V], T.nm[:], ["nm", "kth"], ["t1c"], scale=-1.0, bias=kc(6))
-    dma("s", T.invf[:, 0:256], T.w0[rows8, :], ["w0"], ["invf0"])
+    invert("v", 1, 6)
+    invert("a", 0, 6)
     dma("s", T.invf[:, 256:512], T.w1[rows8, :], ["w1"], ["invf1"])
+    dma("s", T.invf[:, 0:256], T.w0[rows8, :], ["w0"], ["invf0"])
+    dma("s", T.w2[:, 2048:4096], T.w2[:, 0:2048], ["zero", "sente2"], ["w2b"])
+    dma("s", T.w3[:, 0:2048], T.w2[:, 0:2048], ["zero"], ["w3a"])
     dma("s", T.w3[:, 2048:4096], T.w2[:, 0:2048], ["zero"], ["w3b"])
-    op("v", lambda: v.reciprocal(T.kc[:, 14:15], fw(1)), ["fw"], ["krec"])
-    ts(T.kc[:, 11:14], T.kc[:, 20:23], 0.5, A.add, ["kb2a"], ["kb2"])
-    ts(T.kc[:, 16:20], T.fw_f[:], BIG, A.mult, ["fw"], ["kw"])
-    ts(T.kc[:, 15:16], T.kc[:, 14:15], fw(0), A.mult, ["krec", "fw"], ["krat"])
-    ts(T.pj[:, 0:1], T.pi[:, 0:1], 112, A.bitwise_and, ["pi"], ["pj"])
-    cp(T.kc[:, 24:25], T.pj[:, 0:1], ["pj"], ["kp"])
-    cp(T.sel[:, 15:143:16], T.s8b[:], ["s8b", "sel0"], ["sel"])
-    ts(T.val[:], T.vali[:], kc(24), A.subtract, ["vali", "kp"], ["val"])
-    for k in range(EARLY):
-        product_left(k)
-        product(k)
+    weave(links("v", 1), links("v", 0))
+    links_list(1, T.pa[:, 0:64], PA)
 
     for k in range(K):
         ts(T.xl[:, ks(k)], T.t1c[:].indirect(cu(3, k * C, (k + 1) * C)), kc(3 + k), A.add, ["t1c", "e2", "cuu2", "kcr"], ["xl%d" % k])
         act(T.xr[:, ks(k)], T.t1c[:].indirect(cu(2, k * C, (k + 1) * C)), ["t1c", "e2", "cuu2", "kcr"], ["xr%d" % k], bias=kc(3 + k))
-        if k < 2:
-            ts(T.invu[:, k * 256:(k + 1) * 256], T.invf[:, k * 256:(k + 1) * 256], 0.25 - OFF, A.add, ["invf%d" % k], ["invu%d" % k])
+        if k:
+            s = 2 - k
+            ts(T.invu[:, s * 256:(s + 1) * 256], T.invf[:, s * 256:(s + 1) * 256], 0.25 - OFF, A.add, ["invf%d" % s], ["invu%d" % s])
     XL, XR = ["xl0", "xl1", "xl2", "xlz", "invu0"], ["xr0", "xr1", "xr2", "xrz", "invu1"]
 
-    def offer(s, u, own):
-        c0 = s * 256 + u * 64
-        return (T.xr if s else T.xl)[:].indirect(T.invu[:, c0:c0 + C] if own else T.invu[:, c0 + C:c0 + 64])
+    def offer(s, u, c0=0, c1=C):
+        at = s * 256 + u * 64
+        return (T.xr if s else T.xl)[:].indirect(T.invu[:, at + c0:at + c1])
 
-    act(T.sb4[:], offer(1, 0, False), XR, ["sb4"])
-    act(T.sb5[:], offer(1, 1, False), XR, ["sb5"])
-    act(T.sb6[:], offer(1, 2, False), XR, ["sb6"])
-    act(T.pa[:, 0:GH], T.sb5[:], ["sb5"], ["qa"], ["pa"])
-    cp(T.ga[:], offer(0, 0, False), XL, ["ga"])
-    tt(T.gb[:], offer(1, 3, False), T.sb4[:], A.max, XR + ["sb4"], ["gb"])
-    tt(T.ga[:], offer(0, 1, False), T.ga[:], A.max, XL + ["ga"], ["ga"])
-    tt(T.gb[:], offer(0, 2, False), T.gb[:], A.max, XL + ["gb"], ["gb"])
-    tt(T.ga[:], offer(0, 3, False), T.ga[:], A.max, XL + ["ga"], ["ga"])
-    tt(T.pa[:, 0:GH], T.sb6[:], T.pa[:, 0:GH], A.max, ["sb6", "qa"], ["qa"], ["pa"])
-    tt(T.pa[:, 0:GH], T.gb[:], T.pa[:, 0:GH], A.max, ["gb", "qa"], ["qa"], ["pa"])
-    tt(T.sb3[:], T.ga[:], T.pa[:, 0:GH], A.max, ["ga", "qa"], ["sb3"], ["pa"])
-    seq3 = exchange("e3", T.sb3, T.rb3, 0, ["sb3"])
-    for j in range(4):
-        dma("s", wins[j // 2][:, (j % 2) * 2048:(j % 2 + 1) * 2048], T.w2[:, 0:2048], ["zero", "sente3"], ["w%d" % (j // 2)] * (1 - j % 2) + ["wz%d" % j])
-
-    vb = [("p1a", T.p1[:, 0:352], "q1a"), ("p1b", T.p1[:, 512:864], "q1b"), ("pb", T.pb[:, 0:352], "qb"), ("pa", T.pa[:, 0:352], "qa")]
+    vb = [(PB, T.pb, "qb"), (PA, T.pa, "qa")]
 
     def sum2(j):
-        k, c0 = j // 2, j * 352
-        bank, ps, tok = vb[j % 4]
-        mm([(ps, T.ident[:], T.xl[:, c0:c0 + 352]), (ps, T.ident[:], T.xr[:, c0:c0 + 352])], ["ident", "xl%d" % k, "xr%d" % k], [tok, "m01"], [bank])
+        bank, ps, tok = vb[j % 2]
+        pe_sum(ps, [(T.xl, j * HV), (T.xr, j * HV)], HV, ["xl%d" % (j // 2), "xr%d" % (j // 2)], [tok], bank)
 
     def sign2(j):
-        bank, ps, tok = vb[j % 4]
-        act(T.vt2[:, j * 352:(j + 1) * 352], ps, [tok, "kb2"], ["vt2_%d" % j], [bank], f=AF.Sign, bias=kc(11 + j // 2))
+        bank, ps, tok = vb[j % 2]
+        act(T.vt2[:, j * HV:(j + 1) * HV], ps[:, 0:HV], [tok, "kb2"], ["vt2_%d" % j], bank, f=AF.Sign, bias=kc(11 + j // 2))
+        if j < 4:
+            sum2(j + 2)
 
-    for j in range(4):
-        sum2(j)
+    sum2(0)
+    of, ps = lambda s, u: offer(s, u, C, 64), T.p0[:, 0:GH]
+    act(T.sb4[:], of(1, 0), XR, ["sb4"])
+    act(T.sb5[:], of(1, 1), XR, ["sb5"])
+    act(T.sb6[:], of(1, 2), XR, ["sb6"])
+    act(ps, T.sb5[:], ["sb5"], ["q0"], P0)
+    cp(T.ga[:], of(0, 0), XL, ["ga"])
+    tt(T.gb[:], of(1, 3), T.sb4[:], A.max, XR + ["sb4"], ["gb"])
+    tt(T.ga[:], of(0, 1), T.ga[:], A.max, XL + ["ga"], ["ga"])
+    tt(T.gb[:], of(0, 2), T.gb[:], A.max, XL + ["gb"], ["gb"])
+    tt(ps, T.sb6[:], ps, A.max, ["sb6", "q0"], ["q0"], P0)
+    tt(T.ga[:], of(0, 3), T.ga[:], A.max, XL + ["ga"], ["ga"])
+    tt(ps, T.gb[:], ps, A.max, ["gb", "q0"], ["q0"], P0)
+    links_done(1, T.pa[:, 0:64], PA)
+    tt(T.sb3[:], T.ga[:], ps, A.max, ["ga", "q0"], ["sb3"], P0)
+    exchange("e3", T.sb3, T.rb3, 0, ["sb3"])
+    sum2(1)
+    for j in range(2):
+        dma("s", T.w0[:, j * 2048:(j + 1) * 2048], T.w2[:, 0:2048], ["zero", "sente3"], ["w0"] * (1 - j) + ["wz%d" % j])
 
-    def count(out, votes, c0, c1, r, w, x):
-        mm([(out, T.sel[:, 15 - i:143 - i], votes[:, c0 + i:c1:16]) for i in range(16)], ["sel"] + r, w, x)
+    own = {"a": later(act, T.oa[:], offer(0, 3), XL, ["oa"]), "c": later(act, T.oc[:], offer(1, 0), XR, ["oc"]),
+           "p": later(act, T.p0[:, 0:V], T.oc[:], ["oc"], ["q0"], P0), "b": later(act, T.ob[:], offer(1, 1), XR, ["ob"]),
+           "d": later(act, T.od[:], offer(1, 2), XR, ["od"]), "e": later(act, T.o1[:], offer(1, 3), XR, ["o1"]),
+           "n": lambda: act(T.n0[:], T.ss[:, ks(0)], SS[0] + ["kth"], ["n0"], scale=-1.0, bias=kc(6))}
+    for ch in OWN:
+        (own[ch] if ch in own else later(sign2, int(ch)))()
+    left = [later(tt, T.oa[:], offer(0, u), T.oa[:], A.max, XL + ["oa"], ["oa"]) for u in range(3)]
+    right = [later(tt, T.p0[:, 0:V], T[name][:], T.p0[:, 0:V], A.max, [name, "q0"], ["q0"], P0) for name in ("ob", "od", "o1")]
+    for ch in OWNV:
+        run({"l": left, "r": right, "b": bases}[ch], 1)
+    tt(T.xc[:, 0:V], T.oa[:], T.p0[:, 0:V], A.max, ["oa", "q0"], ["xc"], P0)
 
-    act(T.oa[:], offer(0, 3, True), XL, ["oa"])
-    act(T.nm[:], offer(1, 0, True), XR, ["nm"])
-    act(T.p2[:, 0:V], T.nm[:], ["nm"], ["q2"], P2)
-    for u, name in ((1, "ob"), (2, "o0"), (3, "o1")):
-        act(T[name][:], offer(1, u, True), XR, [name])
-        if u == 1:
-            for j in range(2):
-                sign2(j)
-                sum2(4 + j)
-    for k in range(EARLY, K):
-        product_left(k)
-    for j in range(2, 6):
-        sign2(j)
-    for u in range(3):
-        tt(T.oa[:], offer(0, u, True), T.oa[:], A.max, XL + ["oa"], ["oa"])
-    for name in ("ob", "o0", "o1"):
-        tt(T.p2[:, 0:V], T[name][:], T.p2[:, 0:V], A.max, [name, "q2"], ["q2"], P2)
-    tt(T.oc[:], T.oa[:], T.p2[:, 0:V], A.max, ["oa", "q2"], ["oc"], P2)
-    act(T.p1[:, 0:V], T.nr[:, ks(1)], ["nr1"], ["pn1", "q1a", "q1b"], ["p1"])
-    act(T.p2[:, 0:V], T.nr[:, ks(2)], ["nr2"], ["pn2", "q2"], P2)
-    for k in range(EARLY, K):
-        product(k)
-    count(T.pb[:, 380:512], T.vt2, 0, KV, ["vt2_%d" % j for j in range(6)], ["cnt2"], ["pb"])
+    def home(e, x, name, rb, n, f):
+        calls = []
+        for p, d in enumerate(seq):
+            at = V + p * G
+            off = snd(n, d) if p == 0 else T["lk%d" % n][:, C + 4 * p:C + 4 * p + 4]
+            calls.append(later(tt, x[:, at:at + G], x[:, 0:at].indirect(off), rb[:, (d - 1) * G:d * G], f,
+                               [name, "sndu", "lk%d" % n, "%s_%d" % (e, d)], [name]))
+        return calls
 
-    def home(e, seq, acc, name, rb, n, f):
-        for d in seq:
-            off = T.sndu[:, n * 20 + (d - 1) * 4:n * 20 + d * 4]
-            blk = slice((d - 1) * G, d * G)
-            tt(T.ht[:, blk], acc[:].indirect(off), rb[:, blk], f, [name, "sndu", "%s_%d" % (e, d)], ["ht%d" % d])
-            cp(acc[:].indirect(off), T.ht[:, blk], ["ht%d" % d, "sndu"], [name])
+    latest = lambda x, n, c0=0, c1=C: x[:].indirect(T["lk%d" % n][:, c0:c1])
+    weave(bases, home("e3", T.xc, "xc", T.rb3, 1, A.max))
 
-    home("e3", seq3, T.oc, "oc", T.rb3, 1, A.max)
-
-    tt(T.vt1[:, ks(0)], T.oc[:], T.p0[:, 0:V], A.is_ge, ["oc", "pn0"], ["vt1_0"], ["p0"])
-    tt(T.vt1[:, ks(1)], T.oc[:], T.p1[:, 0:V], A.is_ge, ["oc", "pn1"], ["vt1_1"], ["p1"])
-    count(T.pa[:, 0:88], T.vt1, 0, 2 * V, ["vt1_0", "vt1_1"], ["cntA", "qa"], ["pa"])
-    tt(T.vt1[:, ks(2)], T.oc[:], T.p2[:, 0:V], A.is_ge, ["oc", "pn2"], ["vt1_2"], P2)
-    count(T.pb[:, 0:C], T.vt1, 2 * V, KV, ["vt1_2"], ["cntB", "qb"], ["pb"])
-    ts2(T.pa[:, 0:88], T.pa[:, 0:88], 7.5, A.is_lt, DEAD, A.mult, ["cntA"], ["cntA"], ["pa"])
-    tt(T.uu[:, 0:88], T.val[:, 0:88], T.pa[:, 0:88], A.add, ["val", "cntA"], ["uA"], ["pa"])
-    ts2(T.pb[:, 0:C], T.pb[:, 0:C], 7.5, A.is_lt, DEAD, A.mult, ["cntB"], ["cntB"], ["pb"])
-    tt(T.mn[:], T.uu[:, 0:C], T.uu[:, C:88], A.min, ["uA"], ["mn"])
-    tt(T.uu[:, 88:132], T.val[:, 88:132], T.pb[:, 0:C], A.add, ["val", "cntB"], ["uB"], ["pb"])
-    tt(T.mx[:], T.uu[:, 0:C], T.uu[:, C:88], A.max, ["uA"], ["mx"])
-    tt(T.idxf[:, 0:C], T.mn[:], T.uu[:, 88:132], A.min, ["mn", "uB"], ["i0"])
-    tt(T.tt[:], T.mx[:], T.uu[:, 88:132], A.min, ["mx", "uB"], ["tt"])
-    ts(T.idxu[:, 0:C], T.idxf[:, 0:C], float(KV), A.min, ["i0"], ["idx0"])
-    tt(T.idxf[:, C:88], T.mn[:], T.tt[:], A.max, ["mn", "tt"], ["i1"])
-    PP = ["pp0", "pp1", "pp2", "ppz"]
-    for h in range(2):
-        act(T.a0[:, h * 352:(h + 1) * 352], T.pp[:].indirect(T.idxu[:, h * 22:(h + 1) * 22]), PP + ["idx0", "krat"], ["a0%d" % h], scale=kc(15))
-    ts(T.idxu[:, C:88], T.idxf[:, C:88], float(KV), A.min, ["i1"], ["idx1"])
-    for h in range(2):
-        tt(T.t1[:, h * 352:(h + 1) * 352], T.pp[:].indirect(T.idxu[:, C + h * 22:C + (h + 1) * 22]), T.a0[:, h * 352:(h + 1) * 352], A.add,
-           PP + ["idx1", "a0%d" % h], ["t1%d" % h])
-    cp(T.sb4[:], T.t1[:, 0:V].indirect(T.sndu[:, 20:40]), ["t10", "t11", "sndu"], ["sb4"])
-    exchange("e4", T.sb4, T.t1, V, ["sb4"])
+    tt(T.vt1[:, ks(0)], latest(T.xc, 1), T.n0[:], A.is_ge, ["xc", "n0"], ["vt1_0"])
+    act(T.oc[:], latest(T.xc, 1), ["xc", "kth"], ["oc"], scale=-1.0, bias=kc(6))
+    tt(T.vt1[:, ks(1)], T.oc[:], T.p1[:, 0:V], A.is_le, ["oc", "ps1"], ["vt1_1"], P1)
+    tolist(T.p0[:, 0:88], "sel", T.vt1, 0, 2 * V, ["vt1_0", "vt1_1"], ["q0"], P0)
+    tt(T.vt1[:, ks(2)], T.oc[:], T.p2[:, 0:V], A.is_le, ["oc", "ps2"], ["vt1_2"], P2)
+    tolist(T.p1[:, 0:C], "sel", T.vt1, 2 * V, KV, ["vt1_2"], ["ps1"], P1)
+    for j in range(6):
+        if str(j) not in OWN:
+            sign2(j)
+    tolist(T.pa[:, 0:132], "sel", T.vt2, 0, KV, ["vt2_%d" % j for j in range(6)], ["qa"], PA)
     for b in range(2):
         act(T.tw[:, ks(b)], T.top_b[:], ["top", "kw"], ["tw%d" % b], scale=kc(18 + b))
-    act(T.idents[:], T.ident[:], ["ident"], ["idents"], scale=1.0 / BIG)
-    act(T.dg0[:], T.ident[:], ["ident", "kw"], ["dg0"], scale=kc(18))
-    act(T.dg1[:], T.ident[:], ["ident", "kw"], ["dg1"], scale=kc(19))
-    for b in range(2):
-        act(T["t0w%d" % b][:, 0:W], T.t0b[:], ["t0b", "ef", "kw"], ["t0w%d" % b], scale=kc(16 + b))
+    links_list(0, T.p2[:, 0:64], P2)
 
-    def choose(m, dead, su, gu, name):
-        BASE = ["base0", "base1", "base2"]
+    k0, k1, k2 = [T.key[:, :, k * C:(k + 1) * C] for k in range(K)]
+    KA, KB = ["ka0", "ka1"], ["kb0", "kb1"]
+    dead = lambda ps, least, tok, bank: ts2(ps, ps, least, A.is_lt, DEAD, A.mult, [tok], [tok], bank)
+
+    def keys(m, c0, c1, ps, tok, bank, w):
         for s in range(2):
-            for c0, c1, ap, tok, bank in dead:
-                tt(T.key[:, s, c0:c1], T.base[:, 2 * m + s, c0:c1], ap, A.add, BASE + [tok], ["key%d%d" % (s, c0)], [bank])
-        KEY = ["key%d%d" % (s, d[0]) for s in range(2) for d in dead]
-        k0, k1, k2 = [T.key[:, :, k * C:(k + 1) * C] for k in range(K)]
-        tt(T.kmx[:], k0, k1, A.max, KEY, ["kmx"])
-        tt(T.kmn[:], k0, k1, A.min, KEY, ["kmn"])
-        tt(T.kt[:], T.kmx[:], k2, A.min, KEY + ["kmx"], ["kt"])
-        tt(T.ksel[:, :, 0:C], T.kmn[:], k2, A.min, KEY + ["kmn"], ["ksa"])
-        tt(T.ksel[:, :, C:88], T.kmn[:], T.kt[:], A.max, ["kmn", "kt"], ["ksb"])
-        ts(T.kg[:], T.ksel[:], 4096 + W - 1, A.bitwise_and, ["ksa", "ksb"], ["kg"])
-        ts(T.ks[:], T.ksel[:], 4095, A.bitwise_and, ["ksa", "ksb"], ["ks"])
-        ts(gu[:], T.kg[:], float(W), A.min, ["kg"], ["gu" + name])
-        cp(su[:], T.ks[:], ["ks"], ["su" + name])
+            tt(T.key[:, s, c0:c1], T.base[:, 2 * m + s, c0:c1], ps, A.add, ["base0", "base1", "base2", tok], [t + str(s) for t in w], bank)
 
-    for k in range(K):
-        ts(T.base[:, :, k * C:(k + 1) * C], T.fu_i[:, :, k * C:(k + 1) * C], float(k * 8192), A.add, ["fu"], ["base%d" % k])
-    ts2(T.pb[:, 380:512], T.pb[:, 380:512], -1.0, A.is_lt, DEAD, A.mult, ["cnt2"], ["cnt2"], ["pb"])
-    choose(1, [(0, 132, T.pb[:, 380:512], "cnt2", "pb")], T.su2, T.gu2, "2")
-    choose(0, [(0, 88, T.pa[:, 0:88], "cntA", "pa"), (88, 132, T.pb[:, 0:C], "cntB", "pb")], T.su1, T.gu1, "1")
+    least = lambda: tt(T.kmn[:], k0, k1, A.min, KA, ["kmn"])
+    most = lambda: tt(T.kmx[:], k0, k1, A.max, KA, ["kmx"])
+    first = lambda m: tt(T["ksel%d" % m][:, :, 0:C], T.kmn[:], k2, A.min, KB + ["kmn"], ["ksel%d0" % m])
+    third = lambda: tt(T.kt[:], T.kmx[:], k2, A.min, KB + ["kmx"], ["kt"])
+    second = lambda m: tt(T["ksel%d" % m][:, :, C:2 * C], T.kmn[:], T.kt[:], A.max, ["kmn", "kt"], ["ksel%d1" % m])
 
-    def fold(wl, wr, tl, tr, c0, n, npe, pv, bv, pt, bt, tmp, tn, out, on, between=None):
-        sl = lambda w, u: w[:, u * W + c0:u * W + c0 + n]
-        qv, qt, acc = "q" + bv, "q" + bt, pv[:, 0:n]
-        done = []
-        for b0 in range(0, n if npe else 0, 512):
-            m = min(512, n - b0)
-            mm([(pt[:, b0:b0 + m], T.idents[:], wr[:, u * W + c0 + b0:u * W + c0 + b0 + m]) for u in range(npe)], ["idents", tr], [qt + str(b0)], [bt])
-            done.append(qt + str(b0))
-        rest, left = list(range(npe, U)), list(range(U))
-        if len(rest) == 0:
-            tt(acc, sl(wl, 0), sl(wl, 1), A.add, [tl], [qv], [bv]); left = left[2:]
-        elif len(rest) == 1 and c0 == 0:
-            act(acc, sl(wr, rest[0]), [tr], [qv], [bv], scale=1.0 / BIG)
-        elif len(rest) == 1:
-            ts(acc, sl(wr, rest[0]), 1.0 / BIG, A.mult, [tr], [qv], [bv])
+    def children(m, b0, b1):
+        c, tok = slice(b0 * C, b1 * C), lambda s: [s + str(b) for b in range(b0, b1)]
+        return [later(ts, T.kg[:, :, c], T["ksel%d" % m][:, :, c], 4096 + W - 1, A.bitwise_and, tok("ksel%d" % m), tok("kg")),
+                later(ts, T["gu%d" % m][:, :, c], T.kg[:, :, c], float(W), A.min, tok("kg"), tok("gu%d" % m))]
+
+    def places(m):
+        return [later(ts, T["ks%d" % m][:], T["ksel%d" % m][:], 4095, A.bitwise_and, ["ksel%d0" % m, "ksel%d1" % m], ["ks%d" % m]),
+                later(cp, T["su%d" % m][:], T["ks%d" % m][:], ["ks%d" % m], ["su%d" % m])]
+
+    dead(T.p0[:, 0:88], 7.5, "q0", P0)
+    keys(0, 0, 88, T.p0[:, 0:88], "q0", P0, ["ka"])
+    dead(T.p1[:, 0:C], 7.5, "ps1", P1)
+    least()
+    keys(0, 88, 132, T.p1[:, 0:C], "ps1", P1, ["kb"])
+    most()
+    first(1)
+    third()
+    weave(children(1, 0, 1), [later(second, 1)])
+
+    T0 = ["t0b", "t0z", "ef", "fw"]
+    leaf = lambda s, c0, c1: T.t0b[:].indirect(T.gu1[:, s, c0:c1])
+    for h in range(4):
+        b, e = h // 2, slice(h * HV, (h + 1) * HV)
+        if h == 0:
+            late = children(1, 1, 2)
+            run(late, 1)
+            ts(T.wl[:, e], leaf(0, 0, 22), fw(0), A.mult, T0 + ["gu10"], ["wl0"])
+            run(late)
         else:
-            tt(acc, sl(wr, rest[0]), sl(wr, rest[1]), A.add, [tr], [qv], [bv])
-            for u in rest[2:]:
-                tt(acc, sl(wr, u), acc, A.add, [tr, qv], [qv], [bv])
-            ts(acc, acc, 1.0 / BIG, A.mult, [qv], [qv], [bv])
-        for u in left[:-1]:
-            tt(acc, sl(wl, u), acc, A.add, [tl, qv], [qv], [bv])
-        if npe:
-            tt(tmp[:], sl(wl, left[-1]), acc, A.add, [tl, qv], [tn], [bv])
-            if between:
-                between()
-            tt(out[:], tmp[:], pt[:, 0:n], A.add, [tn] + done, [on], [bt])
-        else:
-            tt(out[:], sl(wl, left[-1]), acc, A.add, [tl, qv], [on], [bv])
-            if between:
-                between()
+            act(T.wl[:, e], leaf(0, h * 22, (h + 1) * 22), T0 + ["gu1%d" % b], ["wl%d" % h], scale=fw(b))
+        tt(T.pr[:, e], leaf(1, h * 22, (h + 1) * 22), T.wl[:, e], A.mult, T0 + ["gu1%d" % b, "wl%d" % h], ["pr%d" % h])
+    act(T.ga[:], T.pr[:, ks(0)].indirect(T.sndu[:, 20:40]), ["pr0", "pr1", "sndu"], ["ga"])
+    pe_sum(T.p1, [(T.pr, 0)], V, ["pr0", "pr1"], ["ps1"], P1)
+    tt(T.sb4[:], T.pr[:, ks(1)].indirect(T.sndu[:, 20:40]), T.ga[:], A.add, ["pr2", "pr3", "ga"], ["sb4"])
+    exchange("e4", T.sb4, T.t1, V, ["sb4"])
+    for j in range(2):
+        dma("s", T.w1[:, j * 2048:(j + 1) * 2048], T.w0[:, 0:2048], ["wz0", "sente4"], ["w1"] * (1 - j) + ["wz%d" % (2 + j)])
+    right_leaves = [later(lambda b: act(T.wr[:, ks(b)], leaf(1, b * C, (b + 1) * C), T0 + ["gu1%d" % b], ["wr%d" % b], scale=fw(b)), b) for b in range(2)]
+    run(right_leaves)
+    dead(T.pa[:, 0:132], -1.0, "qa", PA)
+    tt(T.t1[:, 0:V], T.pr[:, ks(1)], T.p1[:, 0:V], A.add, ["pr2", "pr3", "ps1"], ["t1"], P1)
+    keys(1, 0, 132, T.pa[:, 0:132], "qa", PA, ["ka", "kb"])
+    links_done(0, T.p2[:, 0:64], P2)
+    least()
+    most()
+    first(2)
+    third()
+    su1 = places(1)
+    run(su1, 1)
+    second(2)
+    run(su1)
+    weave(children(2, 0, 2), places(2))
 
-    T1 = ["t10", "t11", "t1z", "e4", "gu2"]
+    def fold(wl, wr, tl, tr, c0, n, npe, pv, bv, pt, bt, tmp, tn, out, on, beside=None):
+        qv, qt, runs = "q" + bv[0][1], "q" + bt[0][1], 1 if beside else HALVES
+        pe_sum(pt, [(wr, u * W + c0) for u in range(npe)], n, [tr], [qt], bt)
+        slots = [(wl, u, tl) for u in range(U)] + [(wr, u, tr) for u in range(npe, U)]
+        if c0 == 0:
+            w, u, t = slots.pop()
+            act(pv[:, 0:n], w[:, u * W:u * W + n], [t], [qv + str(h) for h in range(runs)] + [qv], bv)
+        chains = []
+        for h in range(runs):
+            e0, e1 = h * n // runs, (h + 1) * n // runs
+            sl = lambda w, u: w[:, u * W + c0 + e0:u * W + c0 + e1]
+            acc, q, rest, chain = pv[:, e0:e1], qv + str(h), slots, []
+            if c0:
+                chain.append(later(tt, acc, sl(wl, 0), sl(wl, 1), A.add, [tl], [q] + [qv] * (1 - h), bv))
+                rest = slots[2:]
+            for w, u, t in rest[:-1]:
+                chain.append(later(tt, acc, sl(w, u), acc, A.add, [t, q], [q], bv))
+            w, u, t = rest[-1]
+            chain.append(later(tt, T[tmp][:, e0:e1], sl(w, u), acc, A.add, [t, q], [tn + str(h)] + [tn] * (1 - h), bv))
+            chains.append(chain)
+        weave(*(chains + ([beside] if beside else [])))
+        tt(out, T[tmp][:, 0:n], pt[:, 0:n], A.add, [tn + str(h) for h in range(runs)] + [qt], [on], bt)
 
-    def inside2(b):
-        tt(T.bb[:, ks(b)], T.t1[:].indirect(T.gu2[:, 0, b * C:(b + 1) * C]), T.xl[:, ks(b)], A.mult, T1 + ["xl%d" % b], ["bb%d" % b])
-        for b0, m, bank in ((0, 512, "p2a"), (512, V - 512, "p2b")):
-            op("p", lambda: pe.matmul(T.p2[:, b0:b0 + m], T["dg%d" % b][:], T.bb[:, b * V + b0:b * V + b0 + m], b == 0, b == 1),
-               ["dg%d" % b, "bb%d" % b], ["y" + bank], [bank])
+    T1 = ["t1", "t1z", "e4", "gu20", "gu21"]
+    halves = ((T.pa, PA, "qa"), (T.pb, PB, "qb"))
+
+    def staged(out, x, xc, y, yc, rx, ry, w):
+        lay, mult = [], []
+        for h, (ps, bank, tok) in enumerate(halves):
+            e = lambda c: slice(c + h * HV, c + (h + 1) * HV)
+            lay.append(later(act, ps[:, 0:HV], x[:, e(xc)], rx, [tok], bank))
+            mult.append(later(tt, out[:, e(xc)], y[:, e(yc)], ps[:, 0:HV], A.mult, ry + [tok], [w] * (1 - h) + [w + str(h)], bank))
+        return lay, mult
 
     for b in range(2):
         tt(T.xr[:, ks(b)], T.t1[:].indirect(T.gu2[:, 0, b * C:(b + 1) * C]), T.tw[:, ks(b)], A.mult, T1 + ["tw%d" % b], ["xr%d" % b])
-    act(T.xl[:, 0:2 * V], T.t1[:].indirect(T.gu2[:, 1, :]), T1, ["xl0", "xl1"], scale=1.0 / BIG)
+    act(T.xl[:, 0:2 * V], T.t1[:].indirect(T.gu2[:, 1, :]), T1, ["xl0", "xl1"])
     tt(T.w2[:].indirect(T.su2[:, 0, :]), T.xl[:, 0:2 * V], T.tw[:], A.mult, ["xl0", "xl1", "tw0", "tw1", "su2", "w2b"], ["zero", "w2"])
     act(T.w3[:].indirect(T.su2[:, 1, :]), T.xr[:, 0:2 * V], ["xr0", "xr1", "su2", "w3a", "w3b"], ["w3"], f=AF.Silu)
-    fold(T.w2, T.w3, "w2", "w3", V, GH, PE_G, T.pa, "pa", T.pb, "pb", T.ga, "ga", T.sb5, "sb5")
-    seq5 = exchange("e5", T.sb5, T.rb5, 0, ["sb5"])
-    fold(T.w2, T.w3, "w2", "w3", 0, V, PE_O, T.p0, "p0", T.p1, "p1", T.oa, "oa", T.o1, "o1",
-         lambda: [inside2(b) for b in range(YI5)])
-    for b in range(2):
-        act(T.nr[:, ks(b)], T["t0w%d" % b][:].indirect(T.gu1[:, 1, b * C:(b + 1) * C]), ["t0w%d" % b, "t0w%dz" % b, "gu1"], ["nr%d" % b], scale=1.0 / BIG)
-    home("e5", seq5, T.o1, "o1", T.rb5, 1, A.add)
+    fold(T.w2, T.w3, "w2", "w3", V, GH, PE_G, T.pa, PA, T.pb, PB, "ga", "ga", T.sb5[:], "sb5")
+    exchange("e5", T.sb5, T.rb5, 0, ["sb5"])
 
+    def inside2(b):
+        lay, mult = staged(T.bb, T.xl, b * V, T.ss, b * V, ["xl%d" % b], ["yl%d" % b], "bb%d" % b)
+
+        def begin():
+            act(T.ss[:, ks(b)], T.t1[:].indirect(T.gu2[:, 0, b * C:(b + 1) * C]), T1 + ["fw"], ["yl%d" % b, "n0"], scale=fw(2 + b))
+            run(lay)
+            run(mult, 1)
+        return [begin, later(run, mult)]
+
+    fold(T.w2, T.w3, "w2", "w3", 0, V, PE_O, T.p0, P0, T.p1, P1, "oa", "oa", T.x1[:, 0:V], "x1", inside2(0) + inside2(1))
+    pe_sum(T.p2, [(T.bb, 0), (T.bb, V)], V, ["bb00", "bb01", "bb10", "bb11"], ["yp"], P2)
+    run(right_leaves)
+    lay, mult = staged(T.xr, T.wl, V, T.o1, 0, ["wl2", "wl3"], ["o1"], "xr1")
+    run(lay)
+    run(home("e5", T.x1, "x1", T.rb5, 1, A.add))
+
+    tt(T.xr[:, ks(0)], latest(T.x1, 1), T.wl[:, ks(0)], A.mult, ["x1", "wl0", "wl1"], ["xr0"])
+    act(T.o1[:], latest(T.x1, 1), ["x1"], ["o1"])
+    act(T.w1[:].indirect(T.su1[:, 1, 0:C]), T.xr[:, ks(0)], ["xr0", "su1", "wz2", "wz3"], ["w1"], f=AF.Silu)
+    run(mult)
+    act(T.w1[:].indirect(T.su1[:, 1, C:2 * C]), T.xr[:, ks(1)], ["xr10", "xr11", "su1"], ["w1"], f=AF.Silu)
     for b in range(2):
-        tt(T.xr[:, ks(b)], T["t0w%d" % b][:].indirect(T.gu1[:, 0, b * C:(b + 1) * C]), T.o1[:], A.mult,
-           ["t0w%d" % b, "t0w%dz" % b, "gu1", "o1"], ["xr%d" % b])
-        act(T.w1[:].indirect(T.su1[:, 1, b * C:(b + 1) * C]), T.xr[:, ks(b)], ["xr%d" % b, "su1", "wz2", "wz3"], ["w1"], f=AF.Silu)
-    for b in range(2):
-        tt(T.w0[:].indirect(T.su1[:, 0, b * C:(b + 1) * C]), T.nr[:, ks(b)], T.o1[:], A.mult, ["nr%d" % b, "o1", "su1", "wz0", "wz1"], ["w0"])
-    fold(T.w0, T.w1, "w0", "w1", V, GH, PE_G, T.pa, "pa", T.pb, "pb", T.ga, "ga", T.sb6, "sb6")
-    seq6 = exchange("e6", T.sb6, T.rb6, 0, ["sb6"])
-    fold(T.w0, T.w1, "w0", "w1", 0, V, PE_O, T.p0, "p0", T.p1, "p1", T.oa, "oa", T.o0, "o0",
-         lambda: [inside2(b) for b in range(YI5, 2)])
-    act(T.yib[:], T.p2[:, 0:V], ["yp2a", "yp2b"], ["yib"], P2)
-    dma("s", T.yi[:], T.yib[:], ["yib"], ["yi"])
-    home("e6", seq6, T.o0, "o0", T.rb6, 0, A.add)
-    dma("s", T.yo[:], T.o0[:], ["o0"], ["yo"])
+        tt(T.w0[:].indirect(T.su1[:, 0, b * C:(b + 1) * C]), T.wr[:, ks(b)], T.o1[:], A.mult, ["wr%d" % b, "o1", "su1", "wz1"], ["w0", "wz0"])
+    fold(T.w0, T.w1, "w0", "w1", V, GH, PE_G, T.pa, PA, T.pb, PB, "ga", "ga", T.sb6[:], "sb6")
+    exchange("e6", T.sb6, T.rb6, 0, ["sb6"])
+    fold(T.w0, T.w1, "w0", "w1", 0, V, PE_O, T.p0, P0, T.p1, P1, "oa", "oa", T.x0[:, 0:V], "x0")
+    act(T.yib[:], T.p2[:, 0:V], ["yp"], ["yib"], P2)
+    dma("s", T.yi[:], T.yib[:], ["yib", "sente6"], ["yi"])
+    run(home("e6", T.x0, "x0", T.rb6, 0, A.add))
+    ts(T.o0[:, 0:HV], latest(T.x0, 0, 0, 22), 1.0 / BIG, A.mult, ["x0"], ["o0a"])
+    act(T.o0[:, HV:V], latest(T.x0, 0, 22, C), ["x0"], ["o0b"], scale=1.0 / BIG)
+    dma("s", T.yo[:, 0:HV], T.o0[:, 0:HV], ["o0a"], ["yoa"])
+    dma("a", T.yo[:, HV:V], T.o0[:, HV:V], ["o0b"], ["yob"])
 
     for s in sorted(cnt):
         need("g", ("end", s, cnt[s], {}))

@@ -5,13 +5,14 @@ N, V, W, U, ND, G, K = 8, 704, 1024, 4, 5, 64, 3
 KV, GH, C, HV = K * V, ND * G, V // 16, V // 2
 BIG = float(2 ** 40)
 OFF = 32
-DEAD = float(2 ** 15 + 2 ** 12)
-PE_G, PE_O = 3, 3
-ACT1, DVE1, ACT2 = 4, 3, 3
-B_CUT = (0, 12, 44, 88, 110, 132)
+NO = 2 ** 15
+DEAD = {1: 7 * NO + 16 * NO, 2: 30 * NO}
+SPARE = 1536
+ACT1, DVE1, ACT2 = 4, 4, 1
 SPLIT_F, SPLIT_B = [4, 1], [2, 2, 1]
-OWN, OWNV = "0acp1bde2n3", "lblblrbrr"
-HALVES = 2
+PE_G, PE_1, PE_0 = (3, 2), (3, 2), (3, 3)
+OWN = "a0cpb1d2n3"
+LATE = 4
 
 F, I, H, B16 = "float32", "int32", "uint16", "bfloat16"
 
@@ -23,20 +24,21 @@ def _sb(n, dt=F):
 SCRATCH = {
     "cl_i": _sb(V, I), "snd_i": _sb(40, I), "cu_i": _sb(528, I), "fu_i": _sb([4, 132], I), "cr_i": _sb(8, I), "th_i": _sb(4, I),
     "fw_f": _sb(4), "top_b": _sb(V, B16), "t0b": _sb(W + 16, B16), "kc": _sb(32),
-    "sndu": _sb(40, H), "cuu": _sb(528, H), "zpu": _sb(264, H), "invu": _sb(512, H), "lk0": _sb(64, H), "lk1": _sb(64, H),
-    "ti": _sb(264, I), "tj": _sb(264, I), "tk": _sb(264, I), "tg": _sb(264), "base": _sb([4, 132]),
-    "w0": _sb(U * W), "w1": _sb(U * W), "w2": _sb(U * W), "w3": _sb(U * W), "fill": _sb(256), "invf": _sb(512),
+    "sndu": _sb(40, H), "cuu": _sb(528, H), "zpu": _sb(264, H), "invu": _sb([8, 64], H), "lk": _sb(128, H),
+    "ti": _sb(264, I), "tj": _sb(264, I), "tg": _sb(264), "base": _sb([4, 132]), "spare": _sb([2, 88]),
+    "w0": _sb(U * W + SPARE), "w1": _sb(U * W + SPARE), "w2": _sb(U * W + SPARE), "w3": _sb(U * W + SPARE), "fill": _sb(256), "invf": _sb([8, 64]),
     "t0c": _sb(W), "bb": _sb(KV), "ss": _sb(KV), "t1c": _sb(W), "xl": _sb(KV + 8), "xr": _sb(KV + 8), "pp": _sb(KV),
-    "zp0": _sb(W), "zp1": _sb(W), "xc": _sb(W), "x1": _sb(W), "x0": _sb(W), "wl": _sb(2 * V), "wr": _sb(2 * V), "pr": _sb(2 * V),
-    "ga": _sb(GH), "gb": _sb(GH), "oa": _sb(V), "ob": _sb(V), "oc": _sb(V), "od": _sb(V), "o1": _sb(V), "o0": _sb(V), "n0": _sb(V),
+    "zp": _sb(2 * W), "xc": _sb(W), "wl": _sb(2 * V),
+    "ga": _sb(GH), "gb": _sb(GH), "gc": _sb(GH), "gd": _sb(GH),
+    "oa": _sb(V), "ob": _sb(V), "oc": _sb(V), "od": _sb(V), "n0": _sb(V),
     "sb1": _sb(GH), "sbf": _sb(GH, B16), "sb2": _sb(GH), "sb3": _sb(GH), "sb4": _sb(GH), "sb5": _sb(GH), "sb6": _sb(GH),
     "rb3": _sb(GH), "rb5": _sb(GH), "rb6": _sb(GH),
     "vt1": _sb(KV, B16), "vt2": _sb(KV, B16), "sel": _sb(144, B16), "self": _sb(144), "ones": _sb(128), "ident": _sb(128),
-    "s8a": _sb(8), "s8b": _sb(8),
-    "key": _sb([2, 132]), "kmn": _sb([2, C]), "kmx": _sb([2, C]), "kt": _sb([2, C]), "kg": _sb([2, 88], I),
+    "idents": _sb(128), "s8a": _sb(8), "s8b": _sb(8),
+    "key": _sb([2, 132]), "kq1": _sb([2, 88], I), "kq2": _sb([2, 88], I), "kt": _sb([2, C]), "kg": _sb([2, 88], I),
     "ksel1": _sb([2, 88], I), "ksel2": _sb([2, 88], I), "ks1": _sb([2, 88], I), "ks2": _sb([2, 88], I),
     "su1": _sb([2, 88], H), "gu1": _sb([2, 88], H), "su2": _sb([2, 88], H), "gu2": _sb([2, 88], H),
-    "t1": _sb(W + 8), "tw": _sb(2 * V), "yib": _sb(V),
+    "t1": _sb(W + 8), "tw": _sb(2 * V),
     "p0": ("psum", [128, 1024], F), "p1": ("psum", [128, 1024], F), "p2": ("psum", [128, 1024], F), "pa": ("psum", [128, 512], F), "pb": ("psum", [128, 512], F),
 }
 FWD, BACK = ["e1", "ef", "e2", "e4"], ["e3", "e5", "e6"]
@@ -121,13 +123,22 @@ def rank_program(g, core, T, topo):
         Q[q].dma_start(out, in_).then_inc(T.sem[s], 16)
         note(("dma", s, 16, dict(clock[q])), r, w, ())
 
+    def reuse(name, old, new):
+        for t in new:
+            readers[t] = [ev for t0 in old for ev in writer[t0] + readers.get(t0, [])]
+        return T[name]
+
     seq = [d for d, n in arrivals(topo, cores, rank, 1)]
+    cut = max(d for d, eng in calls_of(topo, cores, rank, 1)[0])
+    parts = [(0, cut), (cut, ND)]
+    two = lambda name: [name + "0", name + "1"]
 
     def exchange(e, src, dst, at, r, after=()):
         sign = -1 if e in FWD else 1
-        order("g", list(r) + list(after), (), ())
+        order("g", after, (), ())
         total = 0
-        for call in calls_of(topo, cores, rank, sign):
+        for j, call in enumerate(calls_of(topo, cores, rank, sign)):
+            order("g", r if e in FWD else [r[min(j, 1)]], (), ())
             trs = []
             for d, eng in call:
                 rid, pid = topo.addr(cores[(rank + sign * d) % N], core)
@@ -171,9 +182,9 @@ def rank_program(g, core, T, topo):
             return ins
         op("p", fn, r, w, x)
 
-    def pe_sum(ps, srcs, n, r, w, x):
-        mm([[(ps[:, b0:min(n, b0 + 512)], T.ident[:], t[:, c + b0:c + min(n, b0 + 512)]) for t, c in srcs] for b0 in range(0, n, 512)],
-           ["ident"] + r, w, x)
+    def pe_sum(ps, srcs, n, r, w, x, by="ident"):
+        mm([[(ps[:, b0:min(n, b0 + 512)], T[by][:], t[:, c + b0:c + min(n, b0 + 512)]) for t, c in srcs] for b0 in range(0, n, 512)],
+           [by] + r, w, x)
 
     def iota(o, pattern, base, w, r=()):
         op("g", lambda: g.iota(o, pattern, base, 0, allow_small_or_imprecise_dtypes=True), r, w)
@@ -184,9 +195,10 @@ def rank_program(g, core, T, topo):
     kc = lambda j: T.kc[:, j:j + 1]
     fw = lambda j: T.fw_f[:, j:j + 1]
     ks = lambda k: slice(k * V, (k + 1) * V)
+    half = lambda h, at=0: slice(at + h * HV, at + (h + 1) * HV)
     wins = [T.w0, T.w1, T.w2, T.w3]
     rows8 = slice(0, 128, 18)
-    P0, P1, P2, PA, PB = ["p0"], ["p1"], ["p2"], ["pa"], ["pb"]
+    P0, P1, P2, PA, PB = ["p0a", "p0b"], ["p1"], ["p2"], ["pa"], ["pb"]
     snd = lambda n, d: T.sndu[:, n * 20 + (d - 1) * 4:n * 20 + d * 4]
 
     dma("s", T.cl_i[:], T.cl[:], w=["cl"])
@@ -194,8 +206,8 @@ def rank_program(g, core, T, topo):
     dma("a", T.cu_i[:, 264:528], T.cu[:, 264:528], w=["cu2"])
     iota(T.pp[:, 0:V], [[1, V]], OFF, ["pp0"])
     ms(T.fill[:], float(KV + OFF), ["fill"])
-    dma("s", T.w0[rows8, :], T.fill[:], r=["fill"], w=["w0"])
-    dma("s", T.w1[rows8, :], T.fill[:], r=["fill"], w=["w1"])
+    dma("s", T.w0[rows8, 0:U * W], T.fill[:], r=["fill"], w=["w0"])
+    dma("s", T.w1[rows8, 0:U * W], T.fill[:], r=["fill"], w=["w1"])
     dma("s", T.cu_i[:, 0:264], T.cu[:, 0:264], w=["cu1"])
     dma("s", T.cr_i[:, 0:6], T.cr[:], w=["cr"])
     dma("s", T.t0b[:, 0:V], T.fl[:], w=["t0b"])
@@ -237,7 +249,7 @@ def rank_program(g, core, T, topo):
         if m:
             j = todo[s][0]
             del todo[s][:m]
-            out = wins[s][:].indirect(T.zpu[:, s * 132 + j * 22:s * 132 + (j + m) * 22])
+            out = wins[s][:, 0:U * W].indirect(T.zpu[:, s * 132 + j * 22:s * 132 + (j + m) * 22])
             src = T.pp[:, j * 352:(j + m) * 352]
             r, w = ["zpu%d" % s] + ["pp%d" % k for k in range(j // 2, (j + m + 1) // 2)], ["w%d" % s]
             if q == "a":
@@ -245,29 +257,21 @@ def rank_program(g, core, T, topo):
             else:
                 cp(out, src, r, w)
 
-    def links(q, n):
-        zp, name, calls = T["zp%d" % n], "zp%d" % n, []
+    def links(n):
+        name, calls = "zp%d" % n, []
         for p, d in enumerate(seq):
-            c, nodes = slice(V + p * G, V + (p + 1) * G), zp[:, 0:V].indirect(snd(n, d))
+            c, nodes = V + p * G, T.zp[:, n * W:n * W + V].indirect(snd(n, d))
             if p:
-                calls.append(later(act if q == "a" else cp, zp[:, c], nodes, [name, "sndu"], [name + str(p)]))
-            if q == "a":
-                calls.append(later(act, nodes, T.pp[:, c], ["sndu", "pp1"], [name], (), AF.Silu))
-            else:
-                calls.append(later(cp, nodes, T.pp[:, c], ["sndu", "pp1"], [name]))
+                calls.append(later(act, T.zp[:, n * W + c:n * W + c + G], nodes, [name, "sndu"], [name + str(p)]))
+            calls.append(later(act, nodes, T.pp[:, c:c + G], ["sndu", "pp1"], [name], (), AF.Silu))
         return calls
-
-    def links_list(n, ps, bank):
-        tolist(ps, "self", T["zp%d" % n], 0, W, ["zp%d" % n] + ["zp%d%d" % (n, p) for p in range(1, ND)], ["lkp"], bank)
-
-    def links_done(n, ps, bank):
-        ts2(T["lk%d" % n][:], ps, 1.0 / 16, A.mult, 0.25 - OFF, A.add, ["lkp"], ["lk%d" % n], bank)
 
     invert("a", 0, ACT1)
     act(T.sbf[:], T.t0b[:, 0:V].indirect(T.sndu[:, 0:20]), ["t0b", "sndu"], ["sbf"])
     exchange("ef", T.sbf, T.t0b, V, ["sbf"], ["sente1"])
-    iota(T.zp1[:, 0:V + G], [[1, V + G]], OFF, ["zp1"])
-    iota(T.zp0[:, 0:V + G], [[1, V + G]], OFF, ["zp0"])
+    for n in range(2):
+        iota(T.zp[:, n * W:n * W + V + G], [[1, V + G]], OFF, ["zp%d" % n])
+    op("g", lambda: g.iota(T.spare[:], [[0, 2], [16, 88]], U * W, 1, allow_small_or_imprecise_dtypes=True), w=["spare"])
     ts(T.tj[:], T.cu_i[:, 0:264], W - 1, A.bitwise_and, ["cu1"], ["tj"])
     cp(T.t0c[:, 0:V], T.cl_i[:], ["cl"], ["t0c"])
     cp(T.cuu[:, 0:264], T.tj[:], ["tj"], ["cuu1"])
@@ -275,55 +279,64 @@ def rank_program(g, core, T, topo):
     invert("v", 1, DVE1)
 
     odd = [later(cp, T.kc[:, 6:8], T.th_i[:, 0:2], ["th"], ["kth"]),
-           later(ts, T.tk[:], T.cu_i[:, 264:528], W - 1, A.bitwise_and, ["cu2"], ["tk"]),
-           later(ts2, T.kc[:, 20:23], T.kc[:, 3:6], kc(7), A.add, -1.0, A.mult, ["kcr", "kth"], ["kb2a"]),
-           later(cp, T.cuu[:, 264:528], T.tk[:], ["tk"], ["cuu2"]),
-           later(ts, T.kc[:, 11:14], T.kc[:, 20:23], 0.5, A.add, ["kb2a"], ["kb2"]),
            later(cp, T.self[:, 15:143:16], T.s8b[:], ["s8b", "sel0"], ["self"]),
-           later(ts, T.kc[:, 18:20], T.fw_f[:, 2:4], BIG, A.mult, ["fw"], ["kw"]),
-           later(cp, T.sel[:], T.self[:], ["self"], ["sel"])]
-    bases = [later(ts, T.base[:, :, k * C:(k + 1) * C], T.fu_i[:, :, k * C:(k + 1) * C], float(k * 8192), A.add, ["fu"], ["base%d" % k])
-             for k in range(K)]
+           later(ts2, T.kc[:, 20:23], T.kc[:, 3:6], kc(7), A.add, -1.0, A.mult, ["kcr", "kth"], ["kb2a"]),
+           later(ts, T.kc[:, 16:18], T.fw_f[:, 0:2], 1.0 / BIG, A.mult, ["fw"], ["kw1"]),
+           later(ts2, T.kc[:, 11:14], T.kc[:, 20:23], -1.0, A.mult, -0.5, A.add, ["kb2a"], ["kb2"]),
+           later(ts, T.kc[:, 18:20], T.fw_f[:, 2:4], BIG, A.mult, ["fw"], ["kw"])]
+    bases = [later(ts, T.base[:, 2 * m:2 * m + 2, k * C:(k + 1) * C], T.fu_i[:, 2 * m:2 * m + 2, k * C:(k + 1) * C], float(k * 8192 + (1 - m) * 8 * NO), A.add,
+                   ["fu"], ["base%d%d" % (m, k)]) for m in range(2) for k in range(K)]
 
     cu = lambda blk, c0, c1: T.cuu[:, blk * 132 + c0:blk * 132 + c1]
-    for c0, c1 in zip(B_CUT, B_CUT[1:]):
-        k, e = c0 // C, slice(16 * c0, 16 * c1)
-        act(T.bb[:, e], T.t0c[:].indirect(cu(0, c0, c1)), ["t0c", "e1", "cuu1", "kcr"], ["bb_%d" % c0], bias=kc(k))
-        tt(T.ss[:, e], T.t0c[:].indirect(cu(1, c0, c1)), T.bb[:, e], A.add, ["t0c", "e1", "cuu1", "bb_%d" % c0], ["ss_%d" % c0])
-        if c1 <= C:
-            run(odd, 3 if c0 == 0 else 2)
-    SS = [["ss_%d" % c0 for c0 in B_CUT[:-1] if c0 // C == k] for k in range(K)]
-    act(T.p1[:, 0:V], T.ss[:, ks(1)], SS[1], ["ps1"], P1)
-    tt(T.p0[:, 0:V], T.ss[:, ks(0)], T.p1[:, 0:V], A.max, SS[0] + ["ps1"], ["m01"], P0 + P1)
+    T0C = ["t0c", "e1", "cuu1"]
+    for j in range(2 * K):
+        k, c0, c1 = j // 2, j * 22, (j + 1) * 22
+        if j == 0:
+            ts(T.bb[:, half(j)], T.t0c[:].indirect(cu(0, c0, c1)), kc(k), A.add, T0C + ["kcr"], ["bb_%d" % j])
+            run(odd, 2)
+        else:
+            act(T.bb[:, half(j)], T.t0c[:].indirect(cu(0, c0, c1)), T0C + ["kcr"], ["bb_%d" % j], bias=kc(k))
+        tt(T.ss[:, half(j)], T.t0c[:].indirect(cu(1, c0, c1)), T.bb[:, half(j)], A.add, T0C + ["bb_%d" % j], ["ss%d%d" % (k, j % 2)])
+    sent = lambda k: T.ss[:, ks(k)].indirect(T.sndu[:, 20:40])
+    act(T.ga[:], sent(0), two("ss0") + ["sndu"], two("ga"))
+    act(T.p1[:, 0:V], T.ss[:, ks(1)], two("ss1"), ["ps1"], P1)
     invert("a", 1, ACT2)
+    tt(T.gb[:], sent(1), T.ga[:], A.max, two("ss1") + two("ga"), two("gb"))
     run(odd, 2)
-    tt(T.t1c[:, 0:V], T.ss[:, ks(2)], T.p0[:, 0:V], A.max, SS[2] + ["m01"], ["t1c"], P0)
-    run(odd)
-    cp(T.sb2[:], T.t1c[:, 0:V].indirect(T.sndu[:, 20:40]), ["t1c", "sndu"], ["sb2"])
+    tt(T.sb2[:], sent(2), T.gb[:], A.max, two("ss2") + two("gb"), ["sb2"])
     exchange("e2", T.sb2, T.t1c, V, ["sb2"])
-    pe_sum(T.p2, [(T.ss, 2 * V)], V, SS[2], ["ps2"], P2)
+    for h in range(2):
+        tt(T.p0[:, half(h)], T.ss[:, half(h)], T.p1[:, half(h)], A.max, ["ss0%d" % h, "ps1"], ["m01%d" % h], P0 + P1)
+    for h in range(2):
+        tt(T.t1c[:, half(h)], T.ss[:, half(h, 2 * V)], T.p0[:, half(h)], A.max, ["ss2%d" % h, "m01%d" % h], ["t1c%d" % h], P0)
+    pe_sum(T.p2, [(T.ss, 2 * V)], V, two("ss2"), ["ps2"], P2)
 
+    ts(T.tj[:], T.cu_i[:, 264:528], W - 1, A.bitwise_and, ["cu2"], ["tj"])
+    run(odd)
+    cp(T.cuu[:, 264:528], T.tj[:], ["tj"], ["cuu2"])
     invert("v", 1, 6)
-    invert("a", 0, 6)
-    dma("s", T.invf[:, 256:512], T.w1[rows8, :], ["w1"], ["invf1"])
-    dma("s", T.invf[:, 0:256], T.w0[rows8, :], ["w0"], ["invf0"])
-    dma("s", T.w2[:, 2048:4096], T.w2[:, 0:2048], ["zero", "sente2"], ["w2b"])
+    invert("v", 0, 6)
+    for s in (1, 0):
+        dma("s", T.invf[:, 4 * s:4 * s + 4, :], wins[s][rows8, 0:U * W], ["w%d" % s, "sente2"], ["invf%d" % s])
+    dma("s", T.w2[:, 2048:4096], T.w2[:, 0:2048], ["zero"], ["w2b"])
     dma("s", T.w3[:, 0:2048], T.w2[:, 0:2048], ["zero"], ["w3a"])
     dma("s", T.w3[:, 2048:4096], T.w2[:, 0:2048], ["zero"], ["w3b"])
-    weave(links("v", 1), links("v", 0))
-    links_list(1, T.pa[:, 0:64], PA)
+    weave(links(1), links(0))
+    tolist(T.pa[:, 0:128], "self", T.zp, 0, 2 * W, ["zp%d%s" % (n, p or "") for n in range(2) for p in range(ND)], ["lkp"], PA)
 
+    T1C = two("t1c") + ["e2", "cuu2", "kcr"]
     for k in range(K):
-        ts(T.xl[:, ks(k)], T.t1c[:].indirect(cu(3, k * C, (k + 1) * C)), kc(3 + k), A.add, ["t1c", "e2", "cuu2", "kcr"], ["xl%d" % k])
-        act(T.xr[:, ks(k)], T.t1c[:].indirect(cu(2, k * C, (k + 1) * C)), ["t1c", "e2", "cuu2", "kcr"], ["xr%d" % k], bias=kc(3 + k))
-        if k:
-            s = 2 - k
-            ts(T.invu[:, s * 256:(s + 1) * 256], T.invf[:, s * 256:(s + 1) * 256], 0.25 - OFF, A.add, ["invf%d" % s], ["invu%d" % s])
-    XL, XR = ["xl0", "xl1", "xl2", "xlz", "invu0"], ["xr0", "xr1", "xr2", "xrz", "invu1"]
+        ts(T.xl[:, ks(k)], T.t1c[:].indirect(cu(3, k * C, (k + 1) * C)), kc(3 + k), A.add, T1C, ["xl%d" % k])
+        act(T.xr[:, ks(k)], T.t1c[:].indirect(cu(2, k * C, (k + 1) * C)), T1C, ["xr%d" % k], bias=kc(3 + k))
+        if k == 1:
+            ts(T.invu[:, :, C:64], T.invf[:, :, C:64], 0.25 - OFF, A.add, two("invf"), ["invg"])
+    act(T.idents[:], T.ident[:], ["ident"], ["idents"], scale=1.0 / BIG)
+    XL, XR = ["xl0", "xl1", "xl2", "xlz", "invg"], ["xr0", "xr1", "xr2", "xrz", "invg"]
+    lists = [later(ts, T.invu[:, 4 * s:4 * s + 4, 0:C], T.invf[:, 4 * s:4 * s + 4, 0:C], 0.25 - OFF, A.add, two("invf"), ["invu%d" % s]) for s in range(2)]
+    run(lists, 1)
 
     def offer(s, u, c0=0, c1=C):
-        at = s * 256 + u * 64
-        return (T.xr if s else T.xl)[:].indirect(T.invu[:, at + c0:at + c1])
+        return (T.xr if s else T.xl)[:].indirect(T.invu[:, 4 * s + u, c0:c1])
 
     vb = [(PB, T.pb, "qb"), (PA, T.pa, "qa")]
 
@@ -333,59 +346,69 @@ def rank_program(g, core, T, topo):
 
     def sign2(j):
         bank, ps, tok = vb[j % 2]
-        act(T.vt2[:, j * HV:(j + 1) * HV], ps[:, 0:HV], [tok, "kb2"], ["vt2_%d" % j], bank, f=AF.Sign, bias=kc(11 + j // 2))
+        act(T.vt2[:, half(j)], ps[:, 0:HV], [tok, "kb2"], ["vt2_%d" % j], bank, f=AF.Sign, scale=-1.0, bias=kc(11 + j // 2))
         if j < 4:
             sum2(j + 2)
 
     sum2(0)
-    of, ps = lambda s, u: offer(s, u, C, 64), T.p0[:, 0:GH]
-    act(T.sb4[:], of(1, 0), XR, ["sb4"])
-    act(T.sb5[:], of(1, 1), XR, ["sb5"])
-    act(T.sb6[:], of(1, 2), XR, ["sb6"])
-    act(ps, T.sb5[:], ["sb5"], ["q0"], P0)
-    cp(T.ga[:], of(0, 0), XL, ["ga"])
-    tt(T.gb[:], of(1, 3), T.sb4[:], A.max, XR + ["sb4"], ["gb"])
-    tt(T.ga[:], of(0, 1), T.ga[:], A.max, XL + ["ga"], ["ga"])
-    tt(T.gb[:], of(0, 2), T.gb[:], A.max, XL + ["gb"], ["gb"])
-    tt(ps, T.sb6[:], ps, A.max, ["sb6", "q0"], ["q0"], P0)
-    tt(T.ga[:], of(0, 3), T.ga[:], A.max, XL + ["ga"], ["ga"])
-    tt(ps, T.gb[:], ps, A.max, ["gb", "q0"], ["q0"], P0)
-    links_done(1, T.pa[:, 0:64], PA)
-    tt(T.sb3[:], T.ga[:], ps, A.max, ["ga", "q0"], ["sb3"], P0)
-    exchange("e3", T.sb3, T.rb3, 0, ["sb3"])
+    tail = []
+    for j, (d0, d1) in enumerate(parts):
+        e, n, bank = slice(d0 * G, d1 * G), str(j), [P0[j]]
+        of = lambda s, u: offer(s, u, C + 4 * d0, C + 4 * d1)
+        ps, q = T.p0[:, j * 512:j * 512 + (d1 - d0) * G], "qg" + n
+        for u, name in enumerate(("ga", "gb", "gc", "gd")):
+            act(T[name][:, e], of(1, u), XR, [name + n])
+        act(ps, T["gc"][:, e], ["gc" + n], [q], bank)
+        for u in range(U):
+            name = ("ga", "gb")[u % 2]
+            tt(T[name][:, e], of(0, u), T[name][:, e], A.max, XL + [name + n], [name + n])
+            run(tail)
+            if u == 2:
+                run(lists)
+                tt(ps, T.gd[:, e], ps, A.max, ["gd" + n, q], [q], bank)
+        tt(ps, T.ga[:, e], ps, A.max, ["ga" + n, q], [q], bank)
+        tail = [later(tt, T.sb3[:, e], T.gb[:, e], ps, A.max, ["gb" + n, q], ["sb3" + n], bank)]
+    ts2(T.lk[:], T.pa[:, 0:128], 1.0 / 16, A.mult, 0.25 - OFF, A.add, ["lkp"], ["lk"], PA)
+    run(tail)
     sum2(1)
+    exchange("e3", T.sb3, T.rb3, 0, two("sb3"))
     for j in range(2):
         dma("s", T.w0[:, j * 2048:(j + 1) * 2048], T.w2[:, 0:2048], ["zero", "sente3"], ["w0"] * (1 - j) + ["wz%d" % j])
 
-    own = {"a": later(act, T.oa[:], offer(0, 3), XL, ["oa"]), "c": later(act, T.oc[:], offer(1, 0), XR, ["oc"]),
-           "p": later(act, T.p0[:, 0:V], T.oc[:], ["oc"], ["q0"], P0), "b": later(act, T.ob[:], offer(1, 1), XR, ["ob"]),
-           "d": later(act, T.od[:], offer(1, 2), XR, ["od"]), "e": later(act, T.o1[:], offer(1, 3), XR, ["o1"]),
-           "n": lambda: act(T.n0[:], T.ss[:, ks(0)], SS[0] + ["kth"], ["n0"], scale=-1.0, bias=kc(6))}
+    XL, XR = XL + ["invu0"], XR + ["invu1"]
+    own = {"a": later(act, T.oa[:], offer(0, 3), XL, two("oa")), "c": later(act, T.oc[:], offer(1, 0), XR, ["oc"]),
+           "p": later(act, T.p0[:, 0:V], T.oc[:], ["oc"], two("q0"), P0), "b": later(act, T.ob[:], offer(1, 1), XR, ["ob"]),
+           "d": later(act, T.od[:], offer(1, 2), XR, ["od"]),
+           "n": lambda: act(T.n0[:], T.ss[:, ks(0)], two("ss0") + ["kth"], ["n0"], scale=-1.0, bias=kc(6))}
     for ch in OWN:
         (own[ch] if ch in own else later(sign2, int(ch)))()
-    left = [later(tt, T.oa[:], offer(0, u), T.oa[:], A.max, XL + ["oa"], ["oa"]) for u in range(3)]
-    right = [later(tt, T.p0[:, 0:V], T[name][:], T.p0[:, 0:V], A.max, [name, "q0"], ["q0"], P0) for name in ("ob", "od", "o1")]
-    for ch in OWNV:
-        run({"l": left, "r": right, "b": bases}[ch], 1)
-    tt(T.xc[:, 0:V], T.oa[:], T.p0[:, 0:V], A.max, ["oa", "q0"], ["xc"], P0)
+    for s, u in ((0, 0), (0, 1), (0, 2), (1, 3)):
+        for h in range(2):
+            tt(T.oa[:, half(h)], offer(s, u, h * 22, (h + 1) * 22), T.oa[:, half(h)], A.max, XL + XR + ["oa%d" % h], ["oa%d" % h])
+    for name in ("ob", "od"):
+        for h in range(2):
+            tt(T.p0[:, half(h)], T[name][:, half(h)], T.p0[:, half(h)], A.max, [name, "q0%d" % h], ["q0%d" % h], P0)
+    for h in range(2):
+        tt(T.xc[:, half(h)], T.oa[:, half(h)], T.p0[:, half(h)], A.max, ["oa%d" % h, "q0%d" % h], ["xc%d" % h], P0)
 
-    def home(e, x, name, rb, n, f):
+    def home(e, x, own, name, rb, n, f):
         calls = []
         for p, d in enumerate(seq):
             at = V + p * G
-            off = snd(n, d) if p == 0 else T["lk%d" % n][:, C + 4 * p:C + 4 * p + 4]
+            off = snd(n, d) if p == 0 else T.lk[:, n * 64 + C + 4 * p:n * 64 + C + 4 * p + 4]
             calls.append(later(tt, x[:, at:at + G], x[:, 0:at].indirect(off), rb[:, (d - 1) * G:d * G], f,
-                               [name, "sndu", "lk%d" % n, "%s_%d" % (e, d)], [name]))
+                               own + [name] * (p > 0) + ["sndu", "lk", "%s_%d" % (e, d)], [name]))
         return calls
 
-    latest = lambda x, n, c0=0, c1=C: x[:].indirect(T["lk%d" % n][:, c0:c1])
-    weave(bases, home("e3", T.xc, "xc", T.rb3, 1, A.max))
+    latest = lambda x, n, c0=0, c1=C: x[:, 0:W].indirect(T.lk[:, n * 64 + c0:n * 64 + c1])
+    weave(bases[:5] + [later(ts, T.sel[:], T.self[:], float(NO), A.mult, ["self"], ["sel"])], home("e3", T.xc, two("xc"), "xc", T.rb3, 1, A.max))
 
-    tt(T.vt1[:, ks(0)], latest(T.xc, 1), T.n0[:], A.is_ge, ["xc", "n0"], ["vt1_0"])
-    act(T.oc[:], latest(T.xc, 1), ["xc", "kth"], ["oc"], scale=-1.0, bias=kc(6))
-    tt(T.vt1[:, ks(1)], T.oc[:], T.p1[:, 0:V], A.is_le, ["oc", "ps1"], ["vt1_1"], P1)
-    tolist(T.p0[:, 0:88], "sel", T.vt1, 0, 2 * V, ["vt1_0", "vt1_1"], ["q0"], P0)
-    tt(T.vt1[:, ks(2)], T.oc[:], T.p2[:, 0:V], A.is_le, ["oc", "ps2"], ["vt1_2"], P2)
+    tt(T.vt1[:, ks(0)], latest(T.xc, 1), T.n0[:], A.is_lt, ["xc", "n0"], ["vt1_0"])
+    for h in range(2):
+        act(T.oc[:, half(h)], latest(T.xc, 1, h * 22, (h + 1) * 22), ["xc", "kth"], ["oc%d" % h] + ["oc"] * (1 - h), scale=-1.0, bias=kc(6))
+        tt(T.vt1[:, half(h, V)], T.oc[:, half(h)], T.p1[:, half(h)], A.is_gt, ["oc%d" % h, "ps1"], ["vt1_1%d" % h], P1)
+    tolist(T.p0[:, 0:88], "sel", T.vt1, 0, 2 * V, ["vt1_0"] + two("vt1_1"), ["q0"], P0)
+    tt(T.vt1[:, ks(2)], T.oc[:], T.p2[:, 0:V], A.is_gt, two("oc") + ["ps2"], ["vt1_2"], P2)
     tolist(T.p1[:, 0:C], "sel", T.vt1, 2 * V, KV, ["vt1_2"], ["ps1"], P1)
     for j in range(6):
         if str(j) not in OWN:
@@ -393,34 +416,33 @@ def rank_program(g, core, T, topo):
     tolist(T.pa[:, 0:132], "sel", T.vt2, 0, KV, ["vt2_%d" % j for j in range(6)], ["qa"], PA)
     for b in range(2):
         act(T.tw[:, ks(b)], T.top_b[:], ["top", "kw"], ["tw%d" % b], scale=kc(18 + b))
-    links_list(0, T.p2[:, 0:64], P2)
 
     k0, k1, k2 = [T.key[:, :, k * C:(k + 1) * C] for k in range(K)]
-    KA, KB = ["ka0", "ka1"], ["kb0", "kb1"]
-    dead = lambda ps, least, tok, bank: ts2(ps, ps, least, A.is_lt, DEAD, A.mult, [tok], [tok], bank)
+    KA, KB = two("ka"), two("kb")
+    kmn, kmx = T.p0[:, 512:600], T.p0[:, 600:688]
 
-    def keys(m, c0, c1, ps, tok, bank, w):
-        for s in range(2):
-            tt(T.key[:, s, c0:c1], T.base[:, 2 * m + s, c0:c1], ps, A.add, ["base0", "base1", "base2", tok], [t + str(s) for t in w], bank)
+    def keys(m, c0, c1, ps, tok, bank, w, sides=(0, 1)):
+        for s in sides:
+            tt(T.key[:, s, c0:c1], T.base[:, 2 * m + s, c0:c1], ps, A.max, ["base%d%d" % (m, k) for k in range(K)] + [tok], [t + str(s) for t in w], bank)
 
-    least = lambda: tt(T.kmn[:], k0, k1, A.min, KA, ["kmn"])
-    most = lambda: tt(T.kmx[:], k0, k1, A.max, KA, ["kmx"])
-    first = lambda m: tt(T["ksel%d" % m][:, :, 0:C], T.kmn[:], k2, A.min, KB + ["kmn"], ["ksel%d0" % m])
-    third = lambda: tt(T.kt[:], T.kmx[:], k2, A.min, KB + ["kmx"], ["kt"])
-    second = lambda m: tt(T["ksel%d" % m][:, :, C:2 * C], T.kmn[:], T.kt[:], A.max, ["kmn", "kt"], ["ksel%d1" % m])
+    least = lambda: tt(kmn, k0, k1, A.min, KA, ["kmn"], P0)
+    most = lambda: tt(kmx, k0, k1, A.max, KA, ["kmx"], P0)
+    first = lambda m: tt(T["ksel%d" % m][:, :, 0:C], k2, kmn, A.min, KB + ["kmn"], ["ksel%d0" % m], P0)
+    third = lambda: tt(T.kt[:], k2, kmx, A.min, KB + ["kmx"], ["kt"], P0)
+    second = lambda m: tt(T["ksel%d" % m][:, :, C:2 * C], T.kt[:], kmn, A.max, ["kmn", "kt"], ["ksel%d1" % m], P0)
 
     def children(m, b0, b1):
         c, tok = slice(b0 * C, b1 * C), lambda s: [s + str(b) for b in range(b0, b1)]
-        return [later(ts, T.kg[:, :, c], T["ksel%d" % m][:, :, c], 4096 + W - 1, A.bitwise_and, tok("ksel%d" % m), tok("kg")),
+        return [later(ts, T.kg[:, :, c], T["ksel%d" % m][:, :, c], DEAD[m] + W - 1, A.bitwise_and, tok("ksel%d" % m), tok("kg")),
                 later(ts, T["gu%d" % m][:, :, c], T.kg[:, :, c], float(W), A.min, tok("kg"), tok("gu%d" % m))]
 
     def places(m):
-        return [later(ts, T["ks%d" % m][:], T["ksel%d" % m][:], 4095, A.bitwise_and, ["ksel%d0" % m, "ksel%d1" % m], ["ks%d" % m]),
-                later(cp, T["su%d" % m][:], T["ks%d" % m][:], ["ks%d" % m], ["su%d" % m])]
+        return [later(ts, T["ks%d" % m][:], T["ksel%d" % m][:], DEAD[m] + U * W - 1, A.bitwise_and, two("ksel%d" % m), ["ks%d" % m]),
+                later(tt, T["kq%d" % m][:], T["ks%d" % m][:], T.spare[:], A.min, ["ks%d" % m, "spare"], ["kq%d" % m]),
+                later(cp, T["su%d" % m][:], T["kq%d" % m][:], ["kq%d" % m], ["su%d" % m])]
 
-    dead(T.p0[:, 0:88], 7.5, "q0", P0)
     keys(0, 0, 88, T.p0[:, 0:88], "q0", P0, ["ka"])
-    dead(T.p1[:, 0:C], 7.5, "ps1", P1)
+    bases[5]()
     least()
     keys(0, 88, 132, T.p1[:, 0:C], "ps1", P1, ["kb"])
     most()
@@ -431,27 +453,27 @@ def rank_program(g, core, T, topo):
     T0 = ["t0b", "t0z", "ef", "fw"]
     leaf = lambda s, c0, c1: T.t0b[:].indirect(T.gu1[:, s, c0:c1])
     for h in range(4):
-        b, e = h // 2, slice(h * HV, (h + 1) * HV)
+        b = h // 2
         if h == 0:
             late = children(1, 1, 2)
             run(late, 1)
-            ts(T.wl[:, e], leaf(0, 0, 22), fw(0), A.mult, T0 + ["gu10"], ["wl0"])
+            ts(T.wl[:, half(h)], leaf(0, 0, 22), fw(0), A.mult, T0 + ["gu10"], ["wl0"])
             run(late)
         else:
-            act(T.wl[:, e], leaf(0, h * 22, (h + 1) * 22), T0 + ["gu1%d" % b], ["wl%d" % h], scale=fw(b))
-        tt(T.pr[:, e], leaf(1, h * 22, (h + 1) * 22), T.wl[:, e], A.mult, T0 + ["gu1%d" % b, "wl%d" % h], ["pr%d" % h])
-    act(T.ga[:], T.pr[:, ks(0)].indirect(T.sndu[:, 20:40]), ["pr0", "pr1", "sndu"], ["ga"])
-    pe_sum(T.p1, [(T.pr, 0)], V, ["pr0", "pr1"], ["ps1"], P1)
-    tt(T.sb4[:], T.pr[:, ks(1)].indirect(T.sndu[:, 20:40]), T.ga[:], A.add, ["pr2", "pr3", "ga"], ["sb4"])
+            act(T.wl[:, half(h)], leaf(0, h * 22, (h + 1) * 22), T0 + ["gu1%d" % b], ["wl%d" % h], scale=fw(b))
+        tt(T.bb[:, half(h)], leaf(1, h * 22, (h + 1) * 22), T.wl[:, half(h)], A.mult, T0 + ["gu1%d" % b, "wl%d" % h], ["bb_%d" % h])
+    act(T.ga[:], T.bb[:, ks(0)].indirect(T.sndu[:, 20:40]), ["bb_0", "bb_1", "sndu"], two("ga"))
+    pe_sum(T.p1, [(T.bb, 0)], V, ["bb_0", "bb_1"], ["ps1"], P1)
+    keys(1, 0, 132, T.pa[:, 0:132], "qa", PA, ["ka", "kb"], [0])
+    tt(T.sb4[:], T.bb[:, ks(1)].indirect(T.sndu[:, 20:40]), T.ga[:], A.add, ["bb_2", "bb_3"] + two("ga"), ["sb4"])
     exchange("e4", T.sb4, T.t1, V, ["sb4"])
     for j in range(2):
         dma("s", T.w1[:, j * 2048:(j + 1) * 2048], T.w0[:, 0:2048], ["wz0", "sente4"], ["w1"] * (1 - j) + ["wz%d" % (2 + j)])
-    right_leaves = [later(lambda b: act(T.wr[:, ks(b)], leaf(1, b * C, (b + 1) * C), T0 + ["gu1%d" % b], ["wr%d" % b], scale=fw(b)), b) for b in range(2)]
-    run(right_leaves)
-    dead(T.pa[:, 0:132], -1.0, "qa", PA)
-    tt(T.t1[:, 0:V], T.pr[:, ks(1)], T.p1[:, 0:V], A.add, ["pr2", "pr3", "ps1"], ["t1"], P1)
-    keys(1, 0, 132, T.pa[:, 0:132], "qa", PA, ["ka", "kb"])
-    links_done(0, T.p2[:, 0:64], P2)
+    wr1 = reuse("pp", two("pp"), two("wr"))
+    for b in range(2):
+        act(wr1[:, ks(b)], leaf(1, b * C, (b + 1) * C), T0 + ["gu1%d" % b, "kw1"], ["wr%d" % b], scale=kc(16 + b))
+    keys(1, 0, 132, T.pa[:, 0:132], "qa", PA, ["ka", "kb"], [1])
+    tt(T.t1[:, 0:V], T.bb[:, ks(1)], T.p1[:, 0:V], A.add, ["bb_2", "bb_3", "ps1"], ["t1"], P1)
     least()
     most()
     first(2)
@@ -459,84 +481,99 @@ def rank_program(g, core, T, topo):
     su1 = places(1)
     run(su1, 1)
     second(2)
-    run(su1)
-    weave(children(2, 0, 2), places(2))
+    run(su1, 1)
+    weave(places(2), children(2, 0, 2))
 
-    def fold(wl, wr, tl, tr, c0, n, npe, pv, bv, pt, bt, tmp, tn, out, on, beside=None):
-        qv, qt, runs = "q" + bv[0][1], "q" + bt[0][1], 1 if beside else HALVES
-        pe_sum(pt, [(wr, u * W + c0) for u in range(npe)], n, [tr], [qt], bt)
-        slots = [(wl, u, tl) for u in range(U)] + [(wr, u, tr) for u in range(npe, U)]
-        if c0 == 0:
+    def fold(wl, wr, tl, tr, c0, cuts, npe, skip, start, pv, bv, tmp, tn, also=()):
+        slots = [(wl, u, [tl] + list(also) * (u == 0)) for u in range(skip, U)] + [(wr, U - 1, [tr])]
+        if start:
             w, u, t = slots.pop()
-            act(pv[:, 0:n], w[:, u * W:u * W + n], [t], [qv + str(h) for h in range(runs)] + [qv], bv)
+            act(pv[:, 0:cuts[-1]], w[:, u * W + c0:u * W + c0 + cuts[-1]], t, two(tn + "q"), bv, scale=start)
         chains = []
-        for h in range(runs):
-            e0, e1 = h * n // runs, (h + 1) * n // runs
+        for h, (e0, e1) in enumerate(zip(cuts, cuts[1:])):
             sl = lambda w, u: w[:, u * W + c0 + e0:u * W + c0 + e1]
-            acc, q, rest, chain = pv[:, e0:e1], qv + str(h), slots, []
-            if c0:
-                chain.append(later(tt, acc, sl(wl, 0), sl(wl, 1), A.add, [tl], [q] + [qv] * (1 - h), bv))
-                rest = slots[2:]
+            acc, q, rest, chain = pv[:, e0:e1], tn + "q%d" % h, slots + [(wr, u, [tr]) for u in range(npe[h], U - 1)], []
+            if not start:
+                chain.append(later(tt, acc, sl(wl, 0), sl(wl, 1), A.add, slots[0][2], [q], bv))
+                rest = rest[2:]
             for w, u, t in rest[:-1]:
-                chain.append(later(tt, acc, sl(w, u), acc, A.add, [t, q], [q], bv))
+                chain.append(later(tt, acc, sl(w, u), acc, A.add, t + [q], [q], bv))
             w, u, t = rest[-1]
-            chain.append(later(tt, T[tmp][:, e0:e1], sl(w, u), acc, A.add, [t, q], [tn + str(h)] + [tn] * (1 - h), bv))
+            chain.append(later(tt, tmp[:, e0:e1], sl(w, u), acc, A.add, t + [q], [tn + str(h)], bv))
             chains.append(chain)
-        weave(*(chains + ([beside] if beside else [])))
-        tt(out, T[tmp][:, 0:n], pt[:, 0:n], A.add, [tn + str(h) for h in range(runs)] + [qt], [on], bt)
+        return chains
+
+    def fold_ghosts(wl, wr, tl, tr, npe, start, by, on, banks):
+        chains = fold(wl, wr, tl, tr, V, [0, cut * G, GH], npe, 0, start, T.pa, PA, T.ga, "ga", [tl + "g"])
+        for j, (d0, d1) in enumerate(parts):
+            n, e, (pt, bt) = (d1 - d0) * G, slice(d0 * G, d1 * G), banks[j]
+            pe_sum(pt, [(wr, u * W + V + d0 * G) for u in range(npe[j])], n, [tr], ["qt%d" % j], bt, by)
+            chains[j].append(later(tt, T[on][:, e], T.ga[:, e], pt[:, 0:n], A.add, ["ga%d" % j, "qt%d" % j], [on + str(j)], bt))
+        weave(*chains)
+
+    def fold_own(wl, wr, tl, tr, npe, skip, start, by, pv, bv, out, on):
+        mm([[(T.p1[:, h * 512:h * 512 + HV], T[by][:], wr[:, half(h, u * W)]) for u in range(npe[h])] for h in range(2)], [by, tr], ["ps1"], P1)
+        c0, c1 = fold(wl, wr, tl, tr, 0, [0, HV, V], npe, skip, start, pv, bv, T.oa, "oa")
+        calls = []
+        while c0 or c1:
+            calls += c1[:1] + c0[:1]
+            del c0[:1], c1[:1]
+        return calls + [later(tt, out[:, half(h)], T.oa[:, half(h)], T.p1[:, h * 512:h * 512 + HV], A.add, ["oa%d" % h, "ps1"],
+                              [on + str(h)] + [on] * (1 - h), P1) for h in range(2)]
 
     T1 = ["t1", "t1z", "e4", "gu20", "gu21"]
-    halves = ((T.pa, PA, "qa"), (T.pb, PB, "qb"))
-
-    def staged(out, x, xc, y, yc, rx, ry, w):
-        lay, mult = [], []
-        for h, (ps, bank, tok) in enumerate(halves):
-            e = lambda c: slice(c + h * HV, c + (h + 1) * HV)
-            lay.append(later(act, ps[:, 0:HV], x[:, e(xc)], rx, [tok], bank))
-            mult.append(later(tt, out[:, e(xc)], y[:, e(yc)], ps[:, 0:HV], A.mult, ry + [tok], [w] * (1 - h) + [w + str(h)], bank))
-        return lay, mult
-
     for b in range(2):
         tt(T.xr[:, ks(b)], T.t1[:].indirect(T.gu2[:, 0, b * C:(b + 1) * C]), T.tw[:, ks(b)], A.mult, T1 + ["tw%d" % b], ["xr%d" % b])
     act(T.xl[:, 0:2 * V], T.t1[:].indirect(T.gu2[:, 1, :]), T1, ["xl0", "xl1"])
     tt(T.w2[:].indirect(T.su2[:, 0, :]), T.xl[:, 0:2 * V], T.tw[:], A.mult, ["xl0", "xl1", "tw0", "tw1", "su2", "w2b"], ["zero", "w2"])
     act(T.w3[:].indirect(T.su2[:, 1, :]), T.xr[:, 0:2 * V], ["xr0", "xr1", "su2", "w3a", "w3b"], ["w3"], f=AF.Silu)
-    fold(T.w2, T.w3, "w2", "w3", V, GH, PE_G, T.pa, PA, T.pb, PB, "ga", "ga", T.sb5[:], "sb5")
-    exchange("e5", T.sb5, T.rb5, 0, ["sb5"])
+    run(su1)
+    writer["w2g"], writer["w0g"] = [], []
+    fold_ghosts(T.w2, T.w3, "w2", "w3", PE_G, None, "ident", "sb5", [(T.pb, PB), (T.p2, P2)])
+    exchange("e5", T.sb5, T.rb5, 0, two("sb5"))
+    x1 = reuse("t0c", ["t0c", "e1"], two("x1") + ["x1"])
+    sums = fold_own(T.w2, T.w3, "w2", "w3", PE_1, 0, 1.0, "ident", T.p0, P0, x1, "x1")
 
-    def inside2(b):
-        lay, mult = staged(T.bb, T.xl, b * V, T.ss, b * V, ["xl%d" % b], ["yl%d" % b], "bb%d" % b)
-
-        def begin():
-            act(T.ss[:, ks(b)], T.t1[:].indirect(T.gu2[:, 0, b * C:(b + 1) * C]), T1 + ["fw"], ["yl%d" % b, "n0"], scale=fw(2 + b))
-            run(lay)
-            run(mult, 1)
-        return [begin, later(run, mult)]
-
-    fold(T.w2, T.w3, "w2", "w3", 0, V, PE_O, T.p0, P0, T.p1, P1, "oa", "oa", T.x1[:, 0:V], "x1", inside2(0) + inside2(1))
-    pe_sum(T.p2, [(T.bb, 0), (T.bb, V)], V, ["bb00", "bb01", "bb10", "bb11"], ["yp"], P2)
-    run(right_leaves)
-    lay, mult = staged(T.xr, T.wl, V, T.o1, 0, ["wl2", "wl3"], ["o1"], "xr1")
-    run(lay)
-    run(home("e5", T.x1, "x1", T.rb5, 1, A.add))
-
-    tt(T.xr[:, ks(0)], latest(T.x1, 1), T.wl[:, ks(0)], A.mult, ["x1", "wl0", "wl1"], ["xr0"])
-    act(T.o1[:], latest(T.x1, 1), ["x1"], ["o1"])
-    act(T.w1[:].indirect(T.su1[:, 1, 0:C]), T.xr[:, ks(0)], ["xr0", "su1", "wz2", "wz3"], ["w1"], f=AF.Silu)
-    run(mult)
-    act(T.w1[:].indirect(T.su1[:, 1, C:2 * C]), T.xr[:, ks(1)], ["xr10", "xr11", "su1"], ["w1"], f=AF.Silu)
     for b in range(2):
-        tt(T.w0[:].indirect(T.su1[:, 0, b * C:(b + 1) * C]), T.wr[:, ks(b)], T.o1[:], A.mult, ["wr%d" % b, "o1", "su1", "wz1"], ["w0", "wz0"])
-    fold(T.w0, T.w1, "w0", "w1", V, GH, PE_G, T.pa, PA, T.pb, PB, "ga", "ga", T.sb6[:], "sb6")
-    exchange("e6", T.sb6, T.rb6, 0, ["sb6"])
-    fold(T.w0, T.w1, "w0", "w1", 0, V, PE_O, T.p0, P0, T.p1, P1, "oa", "oa", T.x0[:, 0:V], "x0")
-    act(T.yib[:], T.p2[:, 0:V], ["yp"], ["yib"], P2)
-    dma("s", T.yi[:], T.yib[:], ["yib", "sente6"], ["yi"])
-    run(home("e6", T.x0, "x0", T.rb6, 0, A.add))
-    ts(T.o0[:, 0:HV], latest(T.x0, 0, 0, 22), 1.0 / BIG, A.mult, ["x0"], ["o0a"])
-    act(T.o0[:, HV:V], latest(T.x0, 0, 22, C), ["x0"], ["o0b"], scale=1.0 / BIG)
-    dma("s", T.yo[:, 0:HV], T.o0[:, 0:HV], ["o0a"], ["yoa"])
-    dma("a", T.yo[:, HV:V], T.o0[:, HV:V], ["o0b"], ["yob"])
+        act(T.ss[:, ks(b)], T.t1[:].indirect(T.gu2[:, 0, b * C:(b + 1) * C]), T1 + ["fw"], ["yl%d" % b, "n0"], scale=fw(2 + b))
+    stage = ((T.pa, PA, "qa"), (T.pb, PB, "qb"))
+    lay = lambda j: act(stage[j % 2][0][:, 0:HV], T.xl[:, half(j)], ["xl%d" % (j // 2)], [stage[j % 2][2]], stage[j % 2][1])
+
+    def product(j, c0, c1):
+        ps, bank, tok = stage[j % 2]
+        tt(T.bb[:, j * HV + c0:j * HV + c1], T.ss[:, j * HV + c0:j * HV + c1], ps[:, c0:c1], A.mult, ["yl%d" % (j // 2), tok], ["y%d_%d" % (j, c0)], bank)
+        if j < 2 and c1 == HV:
+            lay(j + 2)
+
+    lay(0)
+    lay(1)
+    run(sums)
+    act(T.p0[:, 0:V], T.wl[:, ks(1)], ["wl2", "wl3"], ["q0"], P0)
+    q = HV // 2
+    pieces = [(0, 0, HV), (1, 0, q), (1, q, HV), (2, 0, HV), (3, 0, q), (3, q, HV)]
+    reuse("bb", ["bb_%d" % j for j in range(4)], ["y%d_%d" % p[:2] for p in pieces])
+    weave([later(product, *p) for p in pieces], home("e5", x1, two("x1"), "x1", T.rb5, 1, A.add))
+    pe_sum(T.p2, [(T.bb, 0), (T.bb, V)], V, ["y%d_%d" % p[:2] for p in pieces], ["yp"], P2)
+
+    tt(T.xr[:, ks(0)], latest(x1, 1), T.wl[:, ks(0)], A.mult, ["x1", "wl0", "wl1"], ["xr0"])
+    for h in range(2):
+        act(T.oc[:, half(h)], latest(x1, 1, h * 22, (h + 1) * 22), ["x1"], ["oc%d" % h])
+    act(T.w1[:].indirect(T.su1[:, 1, 0:C]), T.xr[:, ks(0)], ["xr0", "su1", "wz2", "wz3"], ["w1"], f=AF.Silu)
+    for h in range(2):
+        tt(T.xr[:, half(h, V)], T.oc[:, half(h)], T.p0[:, half(h)], A.mult, ["oc%d" % h, "q0"], ["xr1%d" % h] + ["xr1"] * (1 - h), P0)
+    act(T.w1[:].indirect(T.su1[:, 1, C:2 * C]), T.xr[:, ks(1)], two("xr1") + ["su1"], ["w1"], f=AF.Silu)
+    for b in range(2):
+        tt(T.w0[:].indirect(T.su1[:, 0, b * C:(b + 1) * C]), wr1[:, ks(b)], T.oc[:], A.mult, ["wr%d" % b, "su1", "wz1"] + two("oc"), ["w0", "wz0"])
+    fold_ghosts(T.w0, T.w1, "w0", "w1", (U - 1, U - 1), 1.0 / BIG, "idents", "sb6", [(T.pb, PB), (T.p0, P0)])
+    exchange("e6", T.sb6, T.rb6, 0, two("sb6"))
+    act(T.od[:], T.p2[:, 0:V], ["yp"], ["od"] + two("oaq"), P2)
+    dma("s", T.yi[:], T.od[:], ["od", "sente6"], ["yi"])
+    sums = fold_own(T.w0, T.w1, "w0", "w1", PE_0, 1, 1.0 / BIG, "idents", T.p2, P2, T.ob, "ob")
+    run(sums, LATE)
+    weave(home("e6", T.w0, ["w0"], "w0g", T.rb6, 0, A.add), sums)
+    for h in range(2):
+        tt(T.oc[:, half(h)], latest(T.w0, 0, h * 22, (h + 1) * 22), T.ob[:, half(h)], A.add, ["w0", "w0g", "ob%d" % h], ["oc%d" % h])
+        dma("sa"[h], T.yo[:, half(h)], T.oc[:, half(h)], ["oc%d" % h], ["yo%d" % h])
 
     for s in sorted(cnt):
         need("g", ("end", s, cnt[s], {}))

from concourse.bass import DstId, RemoteDMATransfer
from concourse.mybir import AluOpType, ActivationFunctionType

N, V, W, U, ND, G, K = 8, 704, 1024, 4, 5, 64, 3
KV, GH, C, HV = K * V, ND * G, V // 16, V // 2
BIG = float(2 ** 40)
OFF = 32
NO = 2 ** 15
DEAD = {1: 7 * NO + 16 * NO, 2: 30 * NO}
SPARE = 1536
ACT1, DVE1, ACT2 = 4, 4, 1
SPLIT_F, SPLIT_B = [4, 1], [2, 2, 1]
PE_G, PE_1, PE_0 = (3, 2), (3, 2), (3, 3)
OWN = "a0cpb1d2n3"
LATE = 4

F, I, H, B16 = "float32", "int32", "uint16", "bfloat16"


def _sb(n, dt=F):
    return ("sbuf", [128] + (n if isinstance(n, list) else [n]), dt)


SCRATCH = {
    "cl_i": _sb(V, I), "snd_i": _sb(40, I), "cu_i": _sb(528, I), "fu_i": _sb([4, 132], I), "cr_i": _sb(8, I), "th_i": _sb(4, I),
    "fw_f": _sb(4), "top_b": _sb(V, B16), "t0b": _sb(W + 16, B16), "kc": _sb(32),
    "sndu": _sb(40, H), "cuu": _sb(528, H), "zpu": _sb(264, H), "invu": _sb([8, 64], H), "lk": _sb(128, H),
    "ti": _sb(264, I), "tj": _sb(264, I), "tg": _sb(264), "base": _sb([4, 132]), "spare": _sb([2, 88]),
    "w0": _sb(U * W + SPARE), "w1": _sb(U * W + SPARE), "w2": _sb(U * W + SPARE), "w3": _sb(U * W + SPARE), "fill": _sb(256), "invf": _sb([8, 64]),
    "t0c": _sb(W), "bb": _sb(KV), "ss": _sb(KV), "t1c": _sb(W), "xl": _sb(KV + 8), "xr": _sb(KV + 8), "pp": _sb(KV),
    "zp": _sb(2 * W), "xc": _sb(W), "wl": _sb(2 * V),
    "ga": _sb(GH), "gb": _sb(GH), "gc": _sb(GH), "gd": _sb(GH),
    "oa": _sb(V), "ob": _sb(V), "oc": _sb(V), "od": _sb(V), "n0": _sb(V),
    "sb1": _sb(GH), "sbf": _sb(GH, B16), "sb2": _sb(GH), "sb3": _sb(GH), "sb4": _sb(GH), "sb5": _sb(GH), "sb6": _sb(GH),
    "rb3": _sb(GH), "rb5": _sb(GH), "rb6": _sb(GH),
    "vt1": _sb(KV, B16), "vt2": _sb(KV, B16), "sel": _sb(144, B16), "self": _sb(144), "ones": _sb(128), "ident": _sb(128),
    "idents": _sb(128), "s8a": _sb(8), "s8b": _sb(8),
    "key": _sb([2, 132]), "kq1": _sb([2, 88], I), "kq2": _sb([2, 88], I), "kt": _sb([2, C]), "kg": _sb([2, 88], I),
    "ksel1": _sb([2, 88], I), "ksel2": _sb([2, 88], I), "ks1": _sb([2, 88], I), "ks2": _sb([2, 88], I),
    "su1": _sb([2, 88], H), "gu1": _sb([2, 88], H), "su2": _sb([2, 88], H), "gu2": _sb([2, 88], H),
    "t1": _sb(W + 8), "tw": _sb(2 * V),
    "p0": ("psum", [128, 1024], F), "p1": ("psum", [128, 1024], F), "p2": ("psum", [128, 1024], F), "pa": ("psum", [128, 512], F), "pb": ("psum", [128, 512], F),
}
FWD, BACK = ["e1", "ef", "e2", "e4"], ["e3", "e5", "e6"]
SEMAPHORES = (["cv", "ca", "cp", "cg"] + ["d%d" % i for i in range(32)] + ["s" + e for e in FWD + BACK] + FWD
              + ["%s_%d" % (e, d) for e in BACK for d in range(1, ND + 1)])


def calls_of(topo, cores, r, sign):
    src = cores[r]; here = topo.cores_of(src)
    off = [d for d in range(1, ND + 1) if cores[(r + sign * d) % N] not in here]
    on = [d for d in range(1, ND + 1) if d not in off]
    out = topo.engines(src, cores[(r + sign * off[0]) % N])
    calls = []
    for m in (SPLIT_F if sign < 0 else SPLIT_B):
        part, off = off[:m], off[m:]
        if part:
            n = len(out) // len(part)
            calls.append([(d, out[i * n:(i + 1) * n]) for i, d in enumerate(part)])
    for d in on:
        calls[0].append((d, [e for e in topo.engines(src, cores[(r + sign * d) % N]) if e not in out]))
    return calls


def arrivals(topo, cores, r, sign):
    late = []
    for d in range(1, ND + 1):
        q = (r - sign * d) % N
        for j, call in enumerate(calls_of(topo, cores, q, sign)):
            late += [(j, cores[q] not in topo.cores_of(cores[r]), d, len(eng)) for d2, eng in call if d2 == d]
    return [(d, n) for j, far, d, n in sorted(late)]


def rank_program(g, core, T, topo):
    rank = T.rank_of(core)
    if rank is None:
        return
    A, AF = AluOpType, ActivationFunctionType
    cores = list(T.cores)
    Q = {"v": g.vector, "a": g.scalar, "p": g.tensor, "g": g, "s": g.sync}
    cnt, clock = {}, {q: {} for q in Q}
    writer, readers, holder, nd = {}, {}, {}, [0]

    def need(q, ev):
        s, n, ck = ev[1], ev[2], ev[3]
        if clock[q].get(s, 0) >= n:
            return
        Q[q].wait_ge(T.sem[s], n)
        clock[q][s] = n
        for k2, v2 in ck.items():
            if clock[q].get(k2, 0) < v2:
                clock[q][k2] = v2

    def order(q, r, w, x):
        evs = []
        for t in r:
            evs += writer[t]
        for t in w:
            evs += writer.get(t, []) + readers.get(t, [])
        evs += [holder[t] for t in x if t in holder and holder[t][0] != q]
        for ev in sorted(evs, key=lambda ev: -ev[2]):
            need(q, ev)

    def note(ev, r, w, x):
        for t in r:
            readers.setdefault(t, []).append(ev)
        for t in w:
            writer[t] = [ev]; readers[t] = []
        for t in x:
            holder[t] = ev

    def op(q, fn, r=(), w=(), x=()):
        order(q, r, w, x)
        s = "c" + q
        cnt[s] = cnt.get(s, 0) + 1
        fn().then_inc(T.sem[s], 1)
        note((q, s, cnt[s], dict(clock[q])), r, w, x)

    def dma(q, out, in_, r=(), w=()):
        order(q, r, w, ())
        s = "d%d" % nd[0]; nd[0] += 1
        cnt[s] = 16
        Q[q].dma_start(out, in_).then_inc(T.sem[s], 16)
        note(("dma", s, 16, dict(clock[q])), r, w, ())

    def reuse(name, old, new):
        for t in new:
            readers[t] = [ev for t0 in old for ev in writer[t0] + readers.get(t0, [])]
        return T[name]

    seq = [d for d, n in arrivals(topo, cores, rank, 1)]
    cut = max(d for d, eng in calls_of(topo, cores, rank, 1)[0])
    parts = [(0, cut), (cut, ND)]
    two = lambda name: [name + "0", name + "1"]

    def exchange(e, src, dst, at, r, after=()):
        sign = -1 if e in FWD else 1
        order("g", after, (), ())
        total = 0
        for j, call in enumerate(calls_of(topo, cores, rank, sign)):
            order("g", r if e in FWD else [r[min(j, 1)]], (), ())
            trs = []
            for d, eng in call:
                rid, pid = topo.addr(cores[(rank + sign * d) % N], core)
                trs.append(RemoteDMATransfer(dst_ids=[DstId(rid=rid, pnc=pid)], dma_engine_mask=sum(1 << k for k in eng),
                                             remote_sem=T.sem[e if e in FWD else "%s_%d" % (e, d)],
                                             src=src[:, (d - 1) * G:d * G], dst=dst[:, at + (d - 1) * G:at + d * G]))
                total += len(eng)
            g.remote_dma_fused(trs, local_sem=T.sem["s" + e])
        cnt["s" + e] = total
        note(("dma", "s" + e, total, dict(clock["g"])), r, ["sent" + e], ())
        for d, n in arrivals(topo, cores, rank, sign):
            s = e if e in FWD else "%s_%d" % (e, d)
            cnt[s] = cnt.get(s, 0) + n
            writer[s] = [("dma", s, cnt[s], {})]

    v, a, pe = g.vector, g.scalar, g.tensor
    tt = lambda o, i0, i1, f, r, w, x=(): op("v", lambda: v.tensor_tensor(o, i0, i1, f), r, w, x)
    ts = lambda o, i0, s1, f, r, w, x=(): op("v", lambda: v.tensor_scalar(o, i0, s1, None, f), r, w, x)
    ts2 = lambda o, i0, s1, f, s2, f2, r, w, x=(): op("v", lambda: v.tensor_scalar(o, i0, s1, s2, f, f2), r, w, x)
    cp = lambda o, i0, r, w, x=(): op("v", lambda: v.tensor_copy(o, i0), r, w, x)
    ms = lambda o, c, w: op("v", lambda: v.memset(o, c), (), w)
    later = lambda f, *args: lambda: f(*args)

    def run(calls, n=None):
        for j in range(len(calls) if n is None else min(n, len(calls))):
            calls.pop(0)()

    def weave(*chains):
        while any(chains):
            for c in chains:
                run(c, 1)

    def act(o, i0, r, w, x=(), f=None, **kw):
        op("a", lambda: a.activation(o, i0, AF.Identity if f is None else f, **kw), r, w, x)

    def mm(groups, r, w, x):
        def fn():
            for items in groups:
                for j, (o, l, rr) in enumerate(items):
                    ins = pe.matmul(o, l, rr, j == 0, j == len(items) - 1)
            return ins
        op("p", fn, r, w, x)

    def pe_sum(ps, srcs, n, r, w, x, by="ident"):
        mm([[(ps[:, b0:min(n, b0 + 512)], T[by][:], t[:, c + b0:c + min(n, b0 + 512)]) for t, c in srcs] for b0 in range(0, n, 512)],
           [by] + r, w, x)

    def iota(o, pattern, base, w, r=()):
        op("g", lambda: g.iota(o, pattern, base, 0, allow_small_or_imprecise_dtypes=True), r, w)

    def tolist(out, sel, x, c0, c1, r, w, bank):
        mm([[(out, T[sel][:, 15 - i:143 - i], x[:, c0 + i:c1:16]) for i in range(16)]], [sel] + r, w, bank)

    kc = lambda j: T.kc[:, j:j + 1]
    fw = lambda j: T.fw_f[:, j:j + 1]
    ks = lambda k: slice(k * V, (k + 1) * V)
    half = lambda h, at=0: slice(at + h * HV, at + (h + 1) * HV)
    wins = [T.w0, T.w1, T.w2, T.w3]
    rows8 = slice(0, 128, 18)
    P0, P1, P2, PA, PB = ["p0a", "p0b"], ["p1"], ["p2"], ["pa"], ["pb"]
    snd = lambda n, d: T.sndu[:, n * 20 + (d - 1) * 4:n * 20 + d * 4]

    dma("s", T.cl_i[:], T.cl[:], w=["cl"])
    dma("a", T.snd_i[:], T.snd[:], w=["snd_i"])
    dma("a", T.cu_i[:, 264:528], T.cu[:, 264:528], w=["cu2"])
    iota(T.pp[:, 0:V], [[1, V]], OFF, ["pp0"])
    ms(T.fill[:], float(KV + OFF), ["fill"])
    dma("s", T.w0[rows8, 0:U * W], T.fill[:], r=["fill"], w=["w0"])
    dma("s", T.w1[rows8, 0:U * W], T.fill[:], r=["fill"], w=["w1"])
    dma("s", T.cu_i[:, 0:264], T.cu[:, 0:264], w=["cu1"])
    dma("s", T.cr_i[:, 0:6], T.cr[:], w=["cr"])
    dma("s", T.t0b[:, 0:V], T.fl[:], w=["t0b"])
    dma("s", T.th_i[:, 0:2], T.th[:], w=["th"])
    dma("s", T.fw_f[:], T.fw[:], w=["fw"])
    dma("s", T.fu_i[:], T.fu[:], w=["fu"])
    dma("s", T.top_b[:], T.top[:], w=["top"])
    for name in ("xl", "xr"):
        ms(T[name][:, KV:KV + 8], 0.0, [name + "z"])
    ms(T.t1[:, W:W + 8], 0.0, ["t1z"])
    ms(T.t0b[:, W:W + 16], 0.0, ["t0z"])
    ms(T.self[:], 0.0, ["sel0"])
    ms(T.w2[:, 0:1024], 0.0, ["zero0"])
    act(T.pp[:, ks(1)], T.pp[:, ks(0)], ["pp0"], ["pp1"], f=AF.Silu, bias=float(V))
    ts(T.pp[:, ks(2)], T.pp[:, ks(0)], float(2 * V), A.add, ["pp0"], ["pp2"])

    cp(T.sndu[:], T.snd_i[:], ["snd_i"], ["sndu"])
    cp(T.sb1[:], T.cl_i[:, 0:V].indirect(T.sndu[:, 0:20]), ["cl", "sndu"], ["sb1"])
    exchange("e1", T.sb1, T.t0c, V, ["sb1"])

    def window_columns(s):
        c = slice(s * 132, (s + 1) * 132); z = T.cu_i[:, 264 + s * 132:396 + s * 132]
        return [later(ts, T.ti[:, c], z, 4, A.arith_shift_right, ["cu2"], ["ti%d" % s]),
                later(ts, T.pa[:, c], T.ti[:, c], -4095.0 / 256.0, A.mult, ["ti%d" % s], ["tf%d" % s], PA),
                later(tt, T.tg[:, c], z, T.pa[:, c], A.add, ["cu2", "tf%d" % s], ["tg%d" % s], PA),
                later(ts, T.zpu[:, c], T.tg[:, c], 256.0, A.mult, ["tg%d" % s], ["zpu%d" % s])]

    weave(window_columns(0), window_columns(1))
    iota(T.ones[:], [[0, 128]], 1, ["ones"])
    iota(T.w2[:, 1024:2048], [[0, 1024]], 0, ["zero"], ["zero0"])
    op("g", lambda: g.affine_select(T.s8a[:], T.ones[:, 0:8], [[-16, 8]], A.is_ge, 0.0, 0, 1), ["ones"], ["s8a"])
    op("g", lambda: g.affine_select(T.ident[:], T.ones[:], [[-1, 128]], A.is_equal, 0.0, 0, 1), ["ones"], ["ident"])
    op("g", lambda: g.affine_select(T.s8b[:], T.s8a[:], [[16, 8]], A.is_ge, 0.0, 15, -1), ["s8a"], ["s8b"])

    todo = {0: list(range(6)), 1: list(range(6))}

    def invert(q, s, n):
        m = min(n, len(todo[s]))
        if m:
            j = todo[s][0]
            del todo[s][:m]
            out = wins[s][:, 0:U * W].indirect(T.zpu[:, s * 132 + j * 22:s * 132 + (j + m) * 22])
            src = T.pp[:, j * 352:(j + m) * 352]
            r, w = ["zpu%d" % s] + ["pp%d" % k for k in range(j // 2, (j + m + 1) // 2)], ["w%d" % s]
            if q == "a":
                act(out, src, r, w, f=AF.Silu)
            else:
                cp(out, src, r, w)

    def links(n):
        name, calls = "zp%d" % n, []
        for p, d in enumerate(seq):
            c, nodes = V + p * G, T.zp[:, n * W:n * W + V].indirect(snd(n, d))
            if p:
                calls.append(later(act, T.zp[:, n * W + c:n * W + c + G], nodes, [name, "sndu"], [name + str(p)]))
            calls.append(later(act, nodes, T.pp[:, c:c + G], ["sndu", "pp1"], [name], (), AF.Silu))
        return calls

    invert("a", 0, ACT1)
    act(T.sbf[:], T.t0b[:, 0:V].indirect(T.sndu[:, 0:20]), ["t0b", "sndu"], ["sbf"])
    exchange("ef", T.sbf, T.t0b, V, ["sbf"], ["sente1"])
    for n in range(2):
        iota(T.zp[:, n * W:n * W + V + G], [[1, V + G]], OFF, ["zp%d" % n])
    op("g", lambda: g.iota(T.spare[:], [[0, 2], [16, 88]], U * W, 1, allow_small_or_imprecise_dtypes=True), w=["spare"])
    ts(T.tj[:], T.cu_i[:, 0:264], W - 1, A.bitwise_and, ["cu1"], ["tj"])
    cp(T.t0c[:, 0:V], T.cl_i[:], ["cl"], ["t0c"])
    cp(T.cuu[:, 0:264], T.tj[:], ["tj"], ["cuu1"])
    cp(T.kc[:, 0:6], T.cr_i[:, 0:6], ["cr"], ["kcr"])
    invert("v", 1, DVE1)

    odd = [later(cp, T.kc[:, 6:8], T.th_i[:, 0:2], ["th"], ["kth"]),
           later(cp, T.self[:, 15:143:16], T.s8b[:], ["s8b", "sel0"], ["self"]),
           later(ts2, T.kc[:, 20:23], T.kc[:, 3:6], kc(7), A.add, -1.0, A.mult, ["kcr", "kth"], ["kb2a"]),
           later(ts, T.kc[:, 16:18], T.fw_f[:, 0:2], 1.0 / BIG, A.mult, ["fw"], ["kw1"]),
           later(ts2, T.kc[:, 11:14], T.kc[:, 20:23], -1.0, A.mult, -0.5, A.add, ["kb2a"], ["kb2"]),
           later(ts, T.kc[:, 18:20], T.fw_f[:, 2:4], BIG, A.mult, ["fw"], ["kw"])]
    bases = [later(ts, T.base[:, 2 * m:2 * m + 2, k * C:(k + 1) * C], T.fu_i[:, 2 * m:2 * m + 2, k * C:(k + 1) * C], float(k * 8192 + (1 - m) * 8 * NO), A.add,
                   ["fu"], ["base%d%d" % (m, k)]) for m in range(2) for k in range(K)]

    cu = lambda blk, c0, c1: T.cuu[:, blk * 132 + c0:blk * 132 + c1]
    T0C = ["t0c", "e1", "cuu1"]
    for j in range(2 * K):
        k, c0, c1 = j // 2, j * 22, (j + 1) * 22
        if j == 0:
            ts(T.bb[:, half(j)], T.t0c[:].indirect(cu(0, c0, c1)), kc(k), A.add, T0C + ["kcr"], ["bb_%d" % j])
            run(odd, 2)
        else:
            act(T.bb[:, half(j)], T.t0c[:].indirect(cu(0, c0, c1)), T0C + ["kcr"], ["bb_%d" % j], bias=kc(k))
        tt(T.ss[:, half(j)], T.t0c[:].indirect(cu(1, c0, c1)), T.bb[:, half(j)], A.add, T0C + ["bb_%d" % j], ["ss%d%d" % (k, j % 2)])
    sent = lambda k: T.ss[:, ks(k)].indirect(T.sndu[:, 20:40])
    act(T.ga[:], sent(0), two("ss0") + ["sndu"], two("ga"))
    act(T.p1[:, 0:V], T.ss[:, ks(1)], two("ss1"), ["ps1"], P1)
    invert("a", 1, ACT2)
    tt(T.gb[:], sent(1), T.ga[:], A.max, two("ss1") + two("ga"), two("gb"))
    run(odd, 2)
    tt(T.sb2[:], sent(2), T.gb[:], A.max, two("ss2") + two("gb"), ["sb2"])
    exchange("e2", T.sb2, T.t1c, V, ["sb2"])
    for h in range(2):
        tt(T.p0[:, half(h)], T.ss[:, half(h)], T.p1[:, half(h)], A.max, ["ss0%d" % h, "ps1"], ["m01%d" % h], P0 + P1)
    for h in range(2):
        tt(T.t1c[:, half(h)], T.ss[:, half(h, 2 * V)], T.p0[:, half(h)], A.max, ["ss2%d" % h, "m01%d" % h], ["t1c%d" % h], P0)
    pe_sum(T.p2, [(T.ss, 2 * V)], V, two("ss2"), ["ps2"], P2)

    ts(T.tj[:], T.cu_i[:, 264:528], W - 1, A.bitwise_and, ["cu2"], ["tj"])
    run(odd)
    cp(T.cuu[:, 264:528], T.tj[:], ["tj"], ["cuu2"])
    invert("v", 1, 6)
    invert("v", 0, 6)
    for s in (1, 0):
        dma("s", T.invf[:, 4 * s:4 * s + 4, :], wins[s][rows8, 0:U * W], ["w%d" % s, "sente2"], ["invf%d" % s])
    dma("s", T.w2[:, 2048:4096], T.w2[:, 0:2048], ["zero"], ["w2b"])
    dma("s", T.w3[:, 0:2048], T.w2[:, 0:2048], ["zero"], ["w3a"])
    dma("s", T.w3[:, 2048:4096], T.w2[:, 0:2048], ["zero"], ["w3b"])
    weave(links(1), links(0))
    tolist(T.pa[:, 0:128], "self", T.zp, 0, 2 * W, ["zp%d%s" % (n, p or "") for n in range(2) for p in range(ND)], ["lkp"], PA)

    T1C = two("t1c") + ["e2", "cuu2", "kcr"]
    for k in range(K):
        ts(T.xl[:, ks(k)], T.t1c[:].indirect(cu(3, k * C, (k + 1) * C)), kc(3 + k), A.add, T1C, ["xl%d" % k])
        act(T.xr[:, ks(k)], T.t1c[:].indirect(cu(2, k * C, (k + 1) * C)), T1C, ["xr%d" % k], bias=kc(3 + k))
        if k == 1:
            ts(T.invu[:, :, C:64], T.invf[:, :, C:64], 0.25 - OFF, A.add, two("invf"), ["invg"])
    act(T.idents[:], T.ident[:], ["ident"], ["idents"], scale=1.0 / BIG)
    XL, XR = ["xl0", "xl1", "xl2", "xlz", "invg"], ["xr0", "xr1", "xr2", "xrz", "invg"]
    lists = [later(ts, T.invu[:, 4 * s:4 * s + 4, 0:C], T.invf[:, 4 * s:4 * s + 4, 0:C], 0.25 - OFF, A.add, two("invf"), ["invu%d" % s]) for s in range(2)]
    run(lists, 1)

    def offer(s, u, c0=0, c1=C):
        return (T.xr if s else T.xl)[:].indirect(T.invu[:, 4 * s + u, c0:c1])

    vb = [(PB, T.pb, "qb"), (PA, T.pa, "qa")]

    def sum2(j):
        bank, ps, tok = vb[j % 2]
        pe_sum(ps, [(T.xl, j * HV), (T.xr, j * HV)], HV, ["xl%d" % (j // 2), "xr%d" % (j // 2)], [tok], bank)

    def sign2(j):
        bank, ps, tok = vb[j % 2]
        act(T.vt2[:, half(j)], ps[:, 0:HV], [tok, "kb2"], ["vt2_%d" % j], bank, f=AF.Sign, scale=-1.0, bias=kc(11 + j // 2))
        if j < 4:
            sum2(j + 2)

    sum2(0)
    tail = []
    for j, (d0, d1) in enumerate(parts):
        e, n, bank = slice(d0 * G, d1 * G), str(j), [P0[j]]
        of = lambda s, u: offer(s, u, C + 4 * d0, C + 4 * d1)
        ps, q = T.p0[:, j * 512:j * 512 + (d1 - d0) * G], "qg" + n
        for u, name in enumerate(("ga", "gb", "gc", "gd")):
            act(T[name][:, e], of(1, u), XR, [name + n])
        act(ps, T["gc"][:, e], ["gc" + n], [q], bank)
        for u in range(U):
            name = ("ga", "gb")[u % 2]
            tt(T[name][:, e], of(0, u), T[name][:, e], A.max, XL + [name + n], [name + n])
            run(tail)
            if u == 2:
                run(lists)
                tt(ps, T.gd[:, e], ps, A.max, ["gd" + n, q], [q], bank)
        tt(ps, T.ga[:, e], ps, A.max, ["ga" + n, q], [q], bank)
        tail = [later(tt, T.sb3[:, e], T.gb[:, e], ps, A.max, ["gb" + n, q], ["sb3" + n], bank)]
    ts2(T.lk[:], T.pa[:, 0:128], 1.0 / 16, A.mult, 0.25 - OFF, A.add, ["lkp"], ["lk"], PA)
    run(tail)
    sum2(1)
    exchange("e3", T.sb3, T.rb3, 0, two("sb3"))
    for j in range(2):
        dma("s", T.w0[:, j * 2048:(j + 1) * 2048], T.w2[:, 0:2048], ["zero", "sente3"], ["w0"] * (1 - j) + ["wz%d" % j])

    XL, XR = XL + ["invu0"], XR + ["invu1"]
    own = {"a": later(act, T.oa[:], offer(0, 3), XL, two("oa")), "c": later(act, T.oc[:], offer(1, 0), XR, ["oc"]),
           "p": later(act, T.p0[:, 0:V], T.oc[:], ["oc"], two("q0"), P0), "b": later(act, T.ob[:], offer(1, 1), XR, ["ob"]),
           "d": later(act, T.od[:], offer(1, 2), XR, ["od"]),
           "n": lambda: act(T.n0[:], T.ss[:, ks(0)], two("ss0") + ["kth"], ["n0"], scale=-1.0, bias=kc(6))}
    for ch in OWN:
        (own[ch] if ch in own else later(sign2, int(ch)))()
    for s, u in ((0, 0), (0, 1), (0, 2), (1, 3)):
        for h in range(2):
            tt(T.oa[:, half(h)], offer(s, u, h * 22, (h + 1) * 22), T.oa[:, half(h)], A.max, XL + XR + ["oa%d" % h], ["oa%d" % h])
    for name in ("ob", "od"):
        for h in range(2):
            tt(T.p0[:, half(h)], T[name][:, half(h)], T.p0[:, half(h)], A.max, [name, "q0%d" % h], ["q0%d" % h], P0)
    for h in range(2):
        tt(T.xc[:, half(h)], T.oa[:, half(h)], T.p0[:, half(h)], A.max, ["oa%d" % h, "q0%d" % h], ["xc%d" % h], P0)

    def home(e, x, own, name, rb, n, f):
        calls = []
        for p, d in enumerate(seq):
            at = V + p * G
            off = snd(n, d) if p == 0 else T.lk[:, n * 64 + C + 4 * p:n * 64 + C + 4 * p + 4]
            calls.append(later(tt, x[:, at:at + G], x[:, 0:at].indirect(off), rb[:, (d - 1) * G:d * G], f,
                               own + [name] * (p > 0) + ["sndu", "lk", "%s_%d" % (e, d)], [name]))
        return calls

    latest = lambda x, n, c0=0, c1=C: x[:, 0:W].indirect(T.lk[:, n * 64 + c0:n * 64 + c1])
    weave(bases[:5] + [later(ts, T.sel[:], T.self[:], float(NO), A.mult, ["self"], ["sel"])], home("e3", T.xc, two("xc"), "xc", T.rb3, 1, A.max))

    tt(T.vt1[:, ks(0)], latest(T.xc, 1), T.n0[:], A.is_lt, ["xc", "n0"], ["vt1_0"])
    for h in range(2):
        act(T.oc[:, half(h)], latest(T.xc, 1, h * 22, (h + 1) * 22), ["xc", "kth"], ["oc%d" % h] + ["oc"] * (1 - h), scale=-1.0, bias=kc(6))
        tt(T.vt1[:, half(h, V)], T.oc[:, half(h)], T.p1[:, half(h)], A.is_gt, ["oc%d" % h, "ps1"], ["vt1_1%d" % h], P1)
    tolist(T.p0[:, 0:88], "sel", T.vt1, 0, 2 * V, ["vt1_0"] + two("vt1_1"), ["q0"], P0)
    tt(T.vt1[:, ks(2)], T.oc[:], T.p2[:, 0:V], A.is_gt, two("oc") + ["ps2"], ["vt1_2"], P2)
    tolist(T.p1[:, 0:C], "sel", T.vt1, 2 * V, KV, ["vt1_2"], ["ps1"], P1)
    for j in range(6):
        if str(j) not in OWN:
            sign2(j)
    tolist(T.pa[:, 0:132], "sel", T.vt2, 0, KV, ["vt2_%d" % j for j in range(6)], ["qa"], PA)
    for b in range(2):
        act(T.tw[:, ks(b)], T.top_b[:], ["top", "kw"], ["tw%d" % b], scale=kc(18 + b))

    k0, k1, k2 = [T.key[:, :, k * C:(k + 1) * C] for k in range(K)]
    KA, KB = two("ka"), two("kb")
    kmn, kmx = T.p0[:, 512:600], T.p0[:, 600:688]

    def keys(m, c0, c1, ps, tok, bank, w, sides=(0, 1)):
        for s in sides:
            tt(T.key[:, s, c0:c1], T.base[:, 2 * m + s, c0:c1], ps, A.max, ["base%d%d" % (m, k) for k in range(K)] + [tok], [t + str(s) for t in w], bank)

    least = lambda: tt(kmn, k0, k1, A.min, KA, ["kmn"], P0)
    most = lambda: tt(kmx, k0, k1, A.max, KA, ["kmx"], P0)
    first = lambda m: tt(T["ksel%d" % m][:, :, 0:C], k2, kmn, A.min, KB + ["kmn"], ["ksel%d0" % m], P0)
    third = lambda: tt(T.kt[:], k2, kmx, A.min, KB + ["kmx"], ["kt"], P0)
    second = lambda m: tt(T["ksel%d" % m][:, :, C:2 * C], T.kt[:], kmn, A.max, ["kmn", "kt"], ["ksel%d1" % m], P0)

    def children(m, b0, b1):
        c, tok = slice(b0 * C, b1 * C), lambda s: [s + str(b) for b in range(b0, b1)]
        return [later(ts, T.kg[:, :, c], T["ksel%d" % m][:, :, c], DEAD[m] + W - 1, A.bitwise_and, tok("ksel%d" % m), tok("kg")),
                later(ts, T["gu%d" % m][:, :, c], T.kg[:, :, c], float(W), A.min, tok("kg"), tok("gu%d" % m))]

    def places(m):
        return [later(ts, T["ks%d" % m][:], T["ksel%d" % m][:], DEAD[m] + U * W - 1, A.bitwise_and, two("ksel%d" % m), ["ks%d" % m]),
                later(tt, T["kq%d" % m][:], T["ks%d" % m][:], T.spare[:], A.min, ["ks%d" % m, "spare"], ["kq%d" % m]),
                later(cp, T["su%d" % m][:], T["kq%d" % m][:], ["kq%d" % m], ["su%d" % m])]

    keys(0, 0, 88, T.p0[:, 0:88], "q0", P0, ["ka"])
    bases[5]()
    least()
    keys(0, 88, 132, T.p1[:, 0:C], "ps1", P1, ["kb"])
    most()
    first(1)
    third()
    weave(children(1, 0, 1), [later(second, 1)])

    T0 = ["t0b", "t0z", "ef", "fw"]
    leaf = lambda s, c0, c1: T.t0b[:].indirect(T.gu1[:, s, c0:c1])
    for h in range(4):
        b = h // 2
        if h == 0:
            late = children(1, 1, 2)
            run(late, 1)
            ts(T.wl[:, half(h)], leaf(0, 0, 22), fw(0), A.mult, T0 + ["gu10"], ["wl0"])
            run(late)
        else:
            act(T.wl[:, half(h)], leaf(0, h * 22, (h + 1) * 22), T0 + ["gu1%d" % b], ["wl%d" % h], scale=fw(b))
        tt(T.bb[:, half(h)], leaf(1, h * 22, (h + 1) * 22), T.wl[:, half(h)], A.mult, T0 + ["gu1%d" % b, "wl%d" % h], ["bb_%d" % h])
    act(T.ga[:], T.bb[:, ks(0)].indirect(T.sndu[:, 20:40]), ["bb_0", "bb_1", "sndu"], two("ga"))
    pe_sum(T.p1, [(T.bb, 0)], V, ["bb_0", "bb_1"], ["ps1"], P1)
    keys(1, 0, 132, T.pa[:, 0:132], "qa", PA, ["ka", "kb"], [0])
    tt(T.sb4[:], T.bb[:, ks(1)].indirect(T.sndu[:, 20:40]), T.ga[:], A.add, ["bb_2", "bb_3"] + two("ga"), ["sb4"])
    exchange("e4", T.sb4, T.t1, V, ["sb4"])
    for j in range(2):
        dma("s", T.w1[:, j * 2048:(j + 1) * 2048], T.w0[:, 0:2048], ["wz0", "sente4"], ["w1"] * (1 - j) + ["wz%d" % (2 + j)])
    wr1 = reuse("pp", two("pp"), two("wr"))
    for b in range(2):
        act(wr1[:, ks(b)], leaf(1, b * C, (b + 1) * C), T0 + ["gu1%d" % b, "kw1"], ["wr%d" % b], scale=kc(16 + b))
    keys(1, 0, 132, T.pa[:, 0:132], "qa", PA, ["ka", "kb"], [1])
    tt(T.t1[:, 0:V], T.bb[:, ks(1)], T.p1[:, 0:V], A.add, ["bb_2", "bb_3", "ps1"], ["t1"], P1)
    least()
    most()
    first(2)
    third()
    su1 = places(1)
    run(su1, 1)
    second(2)
    run(su1, 1)
    weave(places(2), children(2, 0, 2))

    def fold(wl, wr, tl, tr, c0, cuts, npe, skip, start, pv, bv, tmp, tn, also=()):
        slots = [(wl, u, [tl] + list(also) * (u == 0)) for u in range(skip, U)] + [(wr, U - 1, [tr])]
        if start:
            w, u, t = slots.pop()
            act(pv[:, 0:cuts[-1]], w[:, u * W + c0:u * W + c0 + cuts[-1]], t, two(tn + "q"), bv, scale=start)
        chains = []
        for h, (e0, e1) in enumerate(zip(cuts, cuts[1:])):
            sl = lambda w, u: w[:, u * W + c0 + e0:u * W + c0 + e1]
            acc, q, rest, chain = pv[:, e0:e1], tn + "q%d" % h, slots + [(wr, u, [tr]) for u in range(npe[h], U - 1)], []
            if not start:
                chain.append(later(tt, acc, sl(wl, 0), sl(wl, 1), A.add, slots[0][2], [q], bv))
                rest = rest[2:]
            for w, u, t in rest[:-1]:
                chain.append(later(tt, acc, sl(w, u), acc, A.add, t + [q], [q], bv))
            w, u, t = rest[-1]
            chain.append(later(tt, tmp[:, e0:e1], sl(w, u), acc, A.add, t + [q], [tn + str(h)], bv))
            chains.append(chain)
        return chains

    def fold_ghosts(wl, wr, tl, tr, npe, start, by, on, banks):
        chains = fold(wl, wr, tl, tr, V, [0, cut * G, GH], npe, 0, start, T.pa, PA, T.ga, "ga", [tl + "g"])
        for j, (d0, d1) in enumerate(parts):
            n, e, (pt, bt) = (d1 - d0) * G, slice(d0 * G, d1 * G), banks[j]
            pe_sum(pt, [(wr, u * W + V + d0 * G) for u in range(npe[j])], n, [tr], ["qt%d" % j], bt, by)
            chains[j].append(later(tt, T[on][:, e], T.ga[:, e], pt[:, 0:n], A.add, ["ga%d" % j, "qt%d" % j], [on + str(j)], bt))
        weave(*chains)

    def fold_own(wl, wr, tl, tr, npe, skip, start, by, pv, bv, out, on):
        mm([[(T.p1[:, h * 512:h * 512 + HV], T[by][:], wr[:, half(h, u * W)]) for u in range(npe[h])] for h in range(2)], [by, tr], ["ps1"], P1)
        c0, c1 = fold(wl, wr, tl, tr, 0, [0, HV, V], npe, skip, start, pv, bv, T.oa, "oa")
        calls = []
        while c0 or c1:
            calls += c1[:1] + c0[:1]
            del c0[:1], c1[:1]
        return calls + [later(tt, out[:, half(h)], T.oa[:, half(h)], T.p1[:, h * 512:h * 512 + HV], A.add, ["oa%d" % h, "ps1"],
                              [on + str(h)] + [on] * (1 - h), P1) for h in range(2)]

    T1 = ["t1", "t1z", "e4", "gu20", "gu21"]
    for b in range(2):
        tt(T.xr[:, ks(b)], T.t1[:].indirect(T.gu2[:, 0, b * C:(b + 1) * C]), T.tw[:, ks(b)], A.mult, T1 + ["tw%d" % b], ["xr%d" % b])
    act(T.xl[:, 0:2 * V], T.t1[:].indirect(T.gu2[:, 1, :]), T1, ["xl0", "xl1"])
    tt(T.w2[:].indirect(T.su2[:, 0, :]), T.xl[:, 0:2 * V], T.tw[:], A.mult, ["xl0", "xl1", "tw0", "tw1", "su2", "w2b"], ["zero", "w2"])
    act(T.w3[:].indirect(T.su2[:, 1, :]), T.xr[:, 0:2 * V], ["xr0", "xr1", "su2", "w3a", "w3b"], ["w3"], f=AF.Silu)
    run(su1)
    writer["w2g"], writer["w0g"] = [], []
    fold_ghosts(T.w2, T.w3, "w2", "w3", PE_G, None, "ident", "sb5", [(T.pb, PB), (T.p2, P2)])
    exchange("e5", T.sb5, T.rb5, 0, two("sb5"))
    x1 = reuse("t0c", ["t0c", "e1"], two("x1") + ["x1"])
    sums = fold_own(T.w2, T.w3, "w2", "w3", PE_1, 0, 1.0, "ident", T.p0, P0, x1, "x1")

    for b in range(2):
        act(T.ss[:, ks(b)], T.t1[:].indirect(T.gu2[:, 0, b * C:(b + 1) * C]), T1 + ["fw"], ["yl%d" % b, "n0"], scale=fw(2 + b))
    stage = ((T.pa, PA, "qa"), (T.pb, PB, "qb"))
    lay = lambda j: act(stage[j % 2][0][:, 0:HV], T.xl[:, half(j)], ["xl%d" % (j // 2)], [stage[j % 2][2]], stage[j % 2][1])

    def product(j, c0, c1):
        ps, bank, tok = stage[j % 2]
        tt(T.bb[:, j * HV + c0:j * HV + c1], T.ss[:, j * HV + c0:j * HV + c1], ps[:, c0:c1], A.mult, ["yl%d" % (j // 2), tok], ["y%d_%d" % (j, c0)], bank)
        if j < 2 and c1 == HV:
            lay(j + 2)

    lay(0)
    lay(1)
    run(sums)
    act(T.p0[:, 0:V], T.wl[:, ks(1)], ["wl2", "wl3"], ["q0"], P0)
    q = HV // 2
    pieces = [(0, 0, HV), (1, 0, q), (1, q, HV), (2, 0, HV), (3, 0, q), (3, q, HV)]
    reuse("bb", ["bb_%d" % j for j in range(4)], ["y%d_%d" % p[:2] for p in pieces])
    weave([later(product, *p) for p in pieces], home("e5", x1, two("x1"), "x1", T.rb5, 1, A.add))
    pe_sum(T.p2, [(T.bb, 0), (T.bb, V)], V, ["y%d_%d" % p[:2] for p in pieces], ["yp"], P2)

    tt(T.xr[:, ks(0)], latest(x1, 1), T.wl[:, ks(0)], A.mult, ["x1", "wl0", "wl1"], ["xr0"])
    for h in range(2):
        act(T.oc[:, half(h)], latest(x1, 1, h * 22, (h + 1) * 22), ["x1"], ["oc%d" % h])
    act(T.w1[:].indirect(T.su1[:, 1, 0:C]), T.xr[:, ks(0)], ["xr0", "su1", "wz2", "wz3"], ["w1"], f=AF.Silu)
    for h in range(2):
        tt(T.xr[:, half(h, V)], T.oc[:, half(h)], T.p0[:, half(h)], A.mult, ["oc%d" % h, "q0"], ["xr1%d" % h] + ["xr1"] * (1 - h), P0)
    act(T.w1[:].indirect(T.su1[:, 1, C:2 * C]), T.xr[:, ks(1)], two("xr1") + ["su1"], ["w1"], f=AF.Silu)
    for b in range(2):
        tt(T.w0[:].indirect(T.su1[:, 0, b * C:(b + 1) * C]), wr1[:, ks(b)], T.oc[:], A.mult, ["wr%d" % b, "su1", "wz1"] + two("oc"), ["w0", "wz0"])
    fold_ghosts(T.w0, T.w1, "w0", "w1", (U - 1, U - 1), 1.0 / BIG, "idents", "sb6", [(T.pb, PB), (T.p0, P0)])
    exchange("e6", T.sb6, T.rb6, 0, two("sb6"))
    act(T.od[:], T.p2[:, 0:V], ["yp"], ["od"] + two("oaq"), P2)
    dma("s", T.yi[:], T.od[:], ["od", "sente6"], ["yi"])
    sums = fold_own(T.w0, T.w1, "w0", "w1", PE_0, 1, 1.0 / BIG, "idents", T.p2, P2, T.ob, "ob")
    run(sums, LATE)
    weave(home("e6", T.w0, ["w0"], "w0g", T.rb6, 0, A.add), sums)
    for h in range(2):
        tt(T.oc[:, half(h)], latest(T.w0, 0, h * 22, (h + 1) * 22), T.ob[:, half(h)], A.add, ["w0", "w0g", "ob%d" % h], ["oc%d" % h])
        dma("sa"[h], T.yo[:, half(h)], T.oc[:, half(h)], ["oc%d" % h], ["yo%d" % h])

    for s in sorted(cnt):
        need("g", ("end", s, cnt[s], {}))
